import numpy as np, ml_dtypes
CORES = [6,15,38,47]
N = 4
BF = ml_dtypes.bfloat16
def gentries(a):
    return np.ascontiguousarray(a.reshape(8, 16, -1).transpose(0, 2, 1)).reshape(8, -1)
def gtable(e):
    e = np.asarray(e); return np.ascontiguousarray(e.reshape(8, -1, 16).transpose(0, 2, 1)).reshape(128, -1).astype(np.int32)
V, NL, NB, L, CAP, T = 2048, 4096, 2048, 512, 192, 4
CN, Q = 128, NL // 64
D = np.arange(16)
def nearby(rng, J, K, P):
    a = 2 * int(rng.integers(0, 8)); x = int(rng.integers(0, 16))
    P[2, a] = rng.integers(1, 8); P[2, a + 1] = rng.integers(-7, 7); P[3] = P[2]; P[3, a] -= 8; P[3, a + 1] += 1
    P[6, x] = rng.integers(-5, 8); P[7] = P[6]; P[7, x] -= 2
    P[10, x] = rng.integers(-7, 7); P[11] = P[10]; P[11, x] += 1
    for r in range(8):
        c = 64 + r; o = rng.permutation(16); d = 2 * int(rng.integers(0, 8))
        J[c, o[:8]] = 7; J[c, o[8:15]] = 6; J[c, o[15]] = 0
        K[c] = rng.integers(0, Q, 16); K[c, d] = 6; K[c, d + 1] = 10; K[c, d ^ 2] = 2
        for k in range(1, 5): J[c + 8 * k] = J[c]; K[c + 8 * k] = K[c]
        J[c + 8, o[15]] = 1
        J[c + 16, o[0]] = 6; J[c + 16, o[8]] = 7
        K[c + 24, d ^ 2] = 3
        K[c + 32, d] = 7; K[c + 32, d + 1] = 11
def classes(rng, how):
    c = np.arange(CN); fam = (c // 8 % 4)[:, None]; q = np.arange(Q)[:, None]; bits = 1 << rng.integers(0, 4, 3)
    if how == "ends":
        k = rng.integers(0, 17, CN); k[[0, 8, 16, 24]] = (16, 0, 1, 15)
        J = 7 * (np.argsort(rng.random((CN, 16)), axis=1) < k[:, None]); K = rng.integers(0, 2, (CN, 16)); K[0] = 0; K[8] = 1
        P = 7 - 14 * rng.integers(0, 2, (Q, 16)); P[1] = 7
        return J, K, P
    J = rng.integers(0, 8, (CN, 16)); K = rng.integers(0, Q, (CN, 16)); P = rng.integers(-7, 8, (Q, 16))
    mk = np.where(c // 32 == 0, 15 - bits[0], 15)
    if how == "spread":
        J = (8 * rng.random((CN, 16)) ** 3).astype(np.int64); P = np.rint(rng.integers(1, 8, (Q, 1)) * (2 * rng.random((Q, 16)) - 1)).astype(np.int64)
    if how == "alike": mk = rng.choice(np.array([0, 1, 6, 8, 9, 15]), CN)
    K = np.where(fam == 0, K // 4 * 4, np.where(fam == 1, K // 4 * 4 + 1, K))
    if how == "alike": K[c // 32 == 1] = 0
    km = np.where(rng.random(CN) < 0.5, mk, 15)
    J = np.take_along_axis(J, D[None, :] & mk[:, None], 1); K = np.take_along_axis(K, D[None, :] & km[:, None], 1)
    P = np.where(q % 4 == 0, P[:, D & (15 - bits[1])], P)
    P = np.where(q % 4 == 1, P[:, D & (15 - bits[2])] * (1 - 2 * ((D & bits[2]) > 0)), P)
    if how == "alike":
        P[0] = 0; nearby(rng, J, K, P)
    else:
        pa = np.where(mk == 15, 1, 15 - mk); J[c, 0] = 0; J[c, pa] = 0
        x = (c - np.add.reduce(J, axis=1) // 2) % 8; J[c, 0] = x; J[c, pa] = x
    return J, K, P
def swap(p, i, x):
    j = int(np.flatnonzero(p == x)[0]); p[j] = p[i]; p[i] = x
def places(rng, J, K, P, faults, ends=False):
    idx = np.argsort(rng.random((N, 8, V)), axis=-1); cp = np.argsort(rng.random((N, 8, NL)), axis=-1)
    sh = rng.integers(0, 16, (N, 8, V)); lm = rng.integers(0, 16, (N, 8, V)); ls = rng.integers(0, 2, (N, 8, V))
    if ends:
        own = rng.random((N, 8, V)) < 0.75; own[..., 0] = True; own[..., V - 1] = True
        pm = 15 * rng.integers(0, 2, (N, 8, 1)); ps = rng.integers(0, 2, (N, 8, 1)); lm = np.where(own, pm, lm); ls = np.where(own, ps, ls)
        sh[..., 0] = 15 * rng.integers(0, 2, (N, 8)); sh[..., V - 1] = 15 * rng.integers(0, 2, (N, 8))
        for q in range(N):
            for h in range(8):
                z = rng.permutation(np.array([0, 8, 16, 24]))[:2] + CN * rng.integers(0, 2, 2)
                if q == N - 1 and h == 7: z = np.array([8, 0])
                swap(idx[q, h], 0, int(z[0])); swap(idx[q, h], V - 1, int(z[1]))
                tr = int(2 * pm[q, h, 0] + ps[q, h, 0]); swap(cp[q, h], tr, 0); swap(cp[q, h], 32 + tr, NL - 1)
    cls = (idx % CN)[:, :, None, :]; fault = np.where(idx // CN % 2 == 0, 0, rng.choice(np.array(faults), (N, 8, V)))[:, :, None, :]
    e = D[:, None] ^ sh[:, :, None, :]; iv = J[cls, e]; lc = K[cls, e]
    at = rng.integers(0, 16, (N, 8, 1, V)) == D[:, None]
    lc = np.where(at & (fault == 4), (lc + rng.integers(1, Q, (N, 8, 1, V))) % Q, lc)
    m = np.where(at & (fault == 2), (lm ^ rng.integers(1, 16, (N, 8, V)))[:, :, None, :], lm[:, :, None, :])
    s = np.where(at & (fault == 3), 1 - ls[:, :, None, :], ls[:, :, None, :])
    made = lc * 32 + m * 2 + s + (at & (fault == 1)) * (NL // 2)
    kids = np.take_along_axis(cp, made.reshape(N, 8, 16 * V), 2).reshape(N, 8, 16, V)
    i = np.arange(NL // 2); z = (P[i // 32, D[:, None] ^ (i % 32 // 2)] * (1 - 2 * (i % 2))).astype(np.int8)
    near = np.where(rng.integers(0, 16, (N, 8, 1, NL // 2)) == D[:, None], np.where(z > 0, z - 1, z + 1), z).astype(np.int8)
    x = np.concatenate([np.broadcast_to(z, near.shape), near], axis=3)
    lf = np.take_along_axis(x, np.argsort(cp, axis=-1)[:, :, None, :], 3)
    return lf, iv, kids, idx, np.argsort(idx, axis=-1)
def nodes(rng, inv, odd):
    c = np.arange(N)[:, None, None] + 8 * rng.integers(0, CN // 8, (N, 8, L))
    return np.take_along_axis(inv, (2 * rng.integers(0, V // CN // 2, (N, 8, L)) + (rng.random((N, 8, L)) < odd)) * CN + c, 2)
def cold(rng, inv):
    col = np.array([7 if N < 8 else (q + 1) % 8 for q in range(N)])[:, None, None]
    code = col + 8 * rng.integers(0, CN // 8, (N, 8, 16 * NB)) + CN * rng.integers(0, V // CN, (N, 8, 16 * NB))
    return np.take_along_axis(inv, code, 2).reshape(N, 8, 16, NB)
def buckets(rng, inv, idx, v, b, want, base, reps):
    bk = base.copy()
    for t in range(T):
        for q in range(N):
            for h in range(8):
                r, g = (q - t) % N, (h - t * (t + 1) // 2) % 8
                c = idx[r, g][v[r, g]] % CN; w = want[r, g, t]
                for j in range(reps):
                    odd = np.where(w == 3, rng.integers(0, 2, L), (w == 1).astype(np.int64))
                    n = inv[q, h][(2 * rng.integers(0, V // CN // 2, L) + odd) * CN + c]
                    on = (w > 0) & ((j == 0) | (rng.random(L) < 0.4))
                    bk[q, h, 3 * t + j, b[r, g][on]] = n[on]
    return np.take_along_axis(bk, np.argsort(rng.random(bk.shape), axis=2), 2)
def wish(rng, rates, values):
    rate = rng.choice(np.array(rates), (N, 8, T, 1))
    return np.where(rng.random((N, 8, T, L)) < rate, rng.choice(np.array(values), (N, 8, T, L)), 0)
def pack(lf, iv, kids, bk, v, b):
    return {"lf": lf.reshape(N, 128, NL).astype(np.float32).astype(BF), "iv": iv.reshape(N, 128, V).astype(np.float32).astype(BF), "kd": kids.reshape(N, 128, V).astype(np.int32),
            "bk": bk.reshape(N, 128, NB).astype(np.int32), "lv": np.stack([gtable(x) for x in v]), "lb": np.stack([gtable(x) for x in b])}
def setup_inputs(rng):
    lf, iv, kids, idx, inv = places(rng, *classes(rng, "plain"), (1, 2, 3, 4))
    v = nodes(rng, inv, 0.2); b = rng.integers(0, NB, (N, 8, L))
    bk = buckets(rng, inv, idx, v, b, wish(rng, [0.25, 0.5, 0.75, 0.97], [1, 2, 2, 3]), rng.integers(0, V, (N, 8, 16, NB)), 3)
    return pack(lf, iv, kids, bk, v, b)
def setup_inputs_spread(rng):
    lf, iv, kids, idx, inv = places(rng, *classes(rng, "spread"), (1, 2, 3, 4))
    v = nodes(rng, inv, 0.2); b = (NB * rng.random((N, 8, L)) ** 2).astype(np.int64)
    bk = buckets(rng, inv, idx, v, b, wish(rng, [0.1, 0.6, 0.9, 1.0], [1, 2, 2, 3]), (V * rng.random((N, 8, 16, NB)) ** 3).astype(np.int64), 3)
    return pack(lf, iv, kids, bk, v, b)
def setup_inputs_alike(rng):
    lf, iv, kids, idx, inv = places(rng, *classes(rng, "alike"), (1, 2, 3, 4))
    v = nodes(rng, inv, 0.2); b = rng.integers(0, NB, (N, 8, L)); want = wish(rng, [0.3, 0.6, 0.9], [1, 2, 2, 3]); n4 = L // 4
    v[..., 1::4] = np.take_along_axis(inv, 64 + np.arange(N)[:, None, None] + 2 * CN * rng.integers(0, V // CN // 2, (N, 8, n4)), 2); want[..., 1::4] = 0
    bk = buckets(rng, inv, idx, v, b, want, rng.integers(0, V, (N, 8, 16, NB)), 3)
    for r in range(N):
        for g in range(8):
            when = rng.integers(0, T, n4); how = rng.integers(1, 5, n4)
            for t in range(T):
                q, h = (r + t) % N, (g + t * (t + 1) // 2) % 8; on = np.flatnonzero(when == t)
                code = 64 + r + 2 * CN * rng.integers(0, V // CN // 2, (16, len(on))); code[:15] += 8 * how[on]
                bk[q, h][:, b[r, g, 1::4][on]] = inv[q, h][code]
    return pack(lf, iv, kids, bk, v, b)
def setup_inputs_corners(rng):
    lf, iv, kids, idx, inv = places(rng, *classes(rng, "plain"), (1,))
    v = nodes(rng, inv, 0.0); b = np.argsort(rng.random((N, 8, NB)), axis=-1)[..., :L]; want = np.zeros((N, 8, T, L), np.int64)
    counts = (0, 1, CAP - 1, CAP, CAP + 1, L)
    for r in range(N):
        full = (5 * r + 2) % 8
        for g in range(8):
            e = 7 * r + g - int(g > full)
            ts = e % T
            for t in range(T):
                n = counts[int(rng.integers(0, 6))]
                if t == ts: n = counts[(e // T + 2 * ts) % 6]
                want[r, g, t, rng.permutation(L)[:n]] = 1 if t < ts else 2
            if g == full:
                c = r + 8 * rng.integers(4, CN // 8, L); v[r, g] = inv[r, g][2 * CN * rng.integers(0, V // CN // 2, L) + c]
                want[r, g] = 2; want[r, g][:T - 1, rng.permutation(L)[:r % 4]] = 0
    return pack(lf, iv, kids, buckets(rng, inv, idx, v, b, want, cold(rng, inv), 3), v, b)
def setup_inputs_crowd(rng):
    lf, iv, kids, idx, inv = places(rng, *classes(rng, "plain"), (1,))
    v = nodes(rng, inv, 0.0); b = np.argsort(rng.random((N, 8, NB)), axis=-1)[..., :L].copy(); want = np.zeros((N, 8, T, L), np.int64)
    for r in range(N):
        for g in range(8):
            if g % 4 == 3:
                i = rng.integers(0, 3, L); v[r, g] = v[r, g, :3][i]; b[r, g] = b[r, g, :3][i]; want[r, g] = rng.integers(0, 3, (T, 3))[:, i]
                continue
            x = (r + g // 2) % T; v0, v1, b0 = int(v[r, g, 0]), int(v[r, g, 1]), int(b[r, g, 0]); e = int(rng.integers(0, L))
            v[r, g] = v0; b[r, g] = b0; want[r, g, :x] = 1; want[r, g, x:] = 2
            if g % 2 == 1: v[r, g, e] = v1; b[r, g, e] = (b0 + 1) % NB; want[r, g, :, e] = 0
    return pack(lf, iv, kids, buckets(rng, inv, idx, v, b, want, cold(rng, inv), 3), v, b)
def setup_inputs_ends(rng):
    lf, iv, kids, idx, inv = places(rng, *classes(rng, "ends"), (1, 2, 3), True)
    u = rng.random((N, 8, L)); v = np.where(u < 0.35, 0, np.where(u < 0.7, V - 1, nodes(rng, inv, 0.2)))
    u = rng.random((N, 8, L)); b = np.where(u < 0.35, 0, np.where(u < 0.7, NB - 1, rng.integers(0, NB, (N, 8, L))))
    v[..., 0] = 0; b[..., 0] = 0; v[..., L - 1] = V - 1; b[..., L - 1] = NB - 1
    base = (V - 1) * np.where(rng.random((N, 8, 1, NB)) < 0.25, rng.integers(0, 2, (N, 8, 16, NB)), rng.integers(0, 2, (N, 8, 1, NB)))
    bk = buckets(rng, inv, idx, v, b, wish(rng, [0.4, 0.7], [1, 2, 2]), base, 1)
    bk[:, :, :15, 0] = V - 1; bk[:, :, 15, 0] = 0; bk[:, :, :15, NB - 1] = 0; bk[:, :, 15, NB - 1] = V - 1
    return pack(lf, iv, kids, bk, v, b)
def check_inputs(d):
    bad = []
    for k, lo, hi in (("lf", -7, 7), ("iv", 0, 7), ("kd", 0, NL - 1), ("bk", 0, V - 1), ("lv", 0, V - 1), ("lb", 0, NB - 1)):
        x = np.asarray(d[k]).astype(np.float64)
        if not (np.min(x) >= lo and np.max(x) <= hi): bad.append("range of " + k)
        if np.any(x != np.floor(x)): bad.append("whole numbers of " + k)
    return bad
def codes(x, base):
    return np.matmul(np.swapaxes(x, -1, -2), base ** (D[:, None] ^ D[None, :]))
def reference(lf, iv, kd, bk, lv, lb):
    x = lf.astype(np.float32).astype(np.int64).reshape(N, 8, 16, NL); inv = iv.astype(np.float32).astype(np.int64).reshape(N, 8, 16, V)
    kids = kd.astype(np.int64).reshape(N, 8, 16, V); slots = bk.astype(np.int64).reshape(N, 8, 16, NB)
    v = np.stack([gentries(e) for e in lv]).astype(np.int64); b = np.stack([gentries(e) for e in lb]).astype(np.int64)
    node = codes(inv, 8)
    leaf = np.stack([codes(7 + x, 15), codes(7 - x, 15)], axis=-1)
    live = np.ones((N, 8, L), bool); out = np.zeros((N, 8, 5, L), np.int64); out[:, :, 0] = -1
    for t in range(T):
        for r in range(N):
            for g in range(8):
                q, h = (r + t) % N, (g + t * (t + 1) // 2) % 8; vv = v[r, g]
                w = slots[q, h][:, b[r, g]].T
                hit = (node[q, h][w] == node[r, g][vv, 0][:, None, None]).reshape(L, 256) & live[r, g][:, None]
                lanes = np.flatnonzero(np.any(hit, axis=1))[:CAP]
                first = np.argmax(hit[lanes], axis=1); w = w[lanes, first >> 4]; M = first & 15
                A = leaf[r, g][kids[r, g][:, vv[lanes]], 0, 0]
                B = leaf[q, h][kids[q, h][D[:, None] ^ M[None, :], w[None, :]]]
                same = np.all(B == A[:, :, None, None], axis=0).reshape(len(lanes), 32)
                won = np.any(same, axis=1); s = np.argmax(same, axis=1)[won]; j = lanes[won]
                out[r, g][:, j] = np.stack([np.full(len(j), q), w[won], M[won], s >> 1, 1 - 2 * (s & 1)])
                live[r, g, j] = False
    return {"y": out.reshape(N, 40, L).astype(np.float32)}

@@ -1,0 +1,690 @@
+import numpy as np
+from concourse.mybir import AluOpType, ActivationFunctionType
+
+ALU = AluOpType
+AF = ActivationFunctionType
+NV, NL, L, CAP, NT = 2048, 4096, 512, 192, 4
+SH = [t * (t + 1) // 2 % 8 for t in range(NT)]
+RW = CAP + 8
+BF, F32, I32, U16 = "bfloat16", "float32", "int32", "uint16"
+HALF = "float16"
+BIG = float(2 ** 25)
+WOFF = 7.0 * 4369
+
+SCRATCH = {}
+for _t, _l in [
+    (BF, "lfs 4096 ivs 2048 wc 128 wf 64 wb 128 iw 256 isc 384 hs 512 ex 144 et 128 ts 128 tb 128 cw 136 tr 128 tp 128 on 128 dl 144 dm 256 "
+         "mm 128 ge 128 pl 128 mi 128 gp 128 gm 128 oy 80 oc 40 ones 512 rm 112 jt 512 jrow 512 m8 512 xt 2048 ct 2048 tg 2048 ga 8192 "
+         "gc0 8192 gc1 8192 nz 1024 mt 512 cl 128 gi 512 fit 512 chi 512 lin 128 lout 128 ff 32 ss 32 ln 1536 gb 3072 uu 768 vv 768 "
+         "fl 384 wt 192 rv 832 rh 832 ev 512 eh 2048"),
+    (F32, "pf 32 bit 512 fac 512 hfa 512 cg 128 c2 256 bm 128 ee 256 hh 256 k16 112 row 112 oh 112 vec 112 bms 16 kv 16 "
+          "sg 128 hn 128 jc 32 jn 32 sb 1024 sc 1024 eq 1024 awf 4096 kp 512 kb 2048 wm 2048 ac 768 a2 768 w32 192 wd 192 ys 512"),
+    (I32, "kds 2048 bks 2048 lvi 32 lbi 128 pin 16"),
+    (U16, "lvu 32 lbu 128 kau 512 awu 8192 wu 2048 wl 128 ofu 32 o2 128 o2h 128 lnu 16 kbu 192"),
+    (HALF, "h16 128 i16 128 dg 144 wr 128 jh 32 wh 1024 cc 512 gk 512 gd 32"),
+]:
+    _w = _l.split()
+    for _i in range(0, len(_w), 2):
+        SCRATCH[_w[_i]] = ("sbuf", [128, int(_w[_i + 1])], _t)
+for _n in ("p0", "p1", "p2", "p3"):
+    SCRATCH[_n] = ("psum", [128, 1024], F32)
+SCRATCH["lbd"] = ("dram", [256, 32], I32)
+SCRATCH["awd"] = ("dram", [256, 2048], U16)
+SCRATCH["tgd"] = ("dram", [3, 128, 128], BF)
+SCRATCH["tgl"] = ("dram", [9, 128, 128], BF)
+
+SEMAPHORES = ["ev_v", "ev_a", "ev_p", "ev_g", "sent"] + ["d%d" % i for i in range(40)] + ["r%d" % i for i in range(24)]
+
+CYC, PEC, FIX, HOP, LAT = 1.04, 0.55, 70.0, 2600.0, 120.0
+RATE = {"c": 1.0, "g": 1.6, "s": 3.8}
+LOCAL_RATE, LINK_RATE = 250.0, 40.0
+CASES = [{}, {"g": 0.7, "s": 0.6}, {"g": 1.25, "s": 1.4, "l": 1.5}, {"p": 1.6, "d": 0.7}, {"c": 0.85, "g": 0.8, "p": 0.8, "d": 1.4, "l": 0.7}]
+TRIES, SEED = 2000, 2
+BIAS = {"kids": 40000.0, "const": 5000.0}
+PLAN = {}
+
+
+def GA(n):
+    return ("g", n)
+
+
+def replay(ops, order, eng, case):
+    free, end = {}, [0.0] * len(ops)
+    for i in order:
+        o, e = ops[i], eng[i]
+        c = o["cost"][e] * case.get(o["cls"], 1.0)
+        t = max([end[d] + lat for d, lat in o["in"]] + [0.0])
+        if e != "x":
+            t = max(t, free.get(e, 0.0))
+            free[e] = t + c
+        end[i] = t + c
+    return max(end)
+
+
+def lay(ops, succ, pr, wait, spare):
+    n = len(ops)
+    left = [len(o["deps"]) for o in ops]
+    rdy, start, end, eng = [0.0] * n, [0.0] * n, [0.0] * n, [None] * n
+    pool = {e: set() for e in "vapgs"}
+    free = {e: 0.0 for e in "vapgs"}
+    todo = [i for i in range(n) if left[i] == 0]
+
+    def place(i, e, t):
+        start[i], eng[i], end[i] = t, e, t + ops[i]["cost"][e]
+        for x, lat in succ[i]:
+            rdy[x] = max(rdy[x], end[i] + lat)
+            left[x] -= 1
+            if left[x] == 0:
+                todo.append(x)
+    while True:
+        while todo:
+            i = todo.pop()
+            if "x" in ops[i]["cost"]:
+                place(i, "x", rdy[i])
+            else:
+                for e in ops[i]["cost"]:
+                    pool[e].add(i)
+        nxt = [(max(free[q], min(rdy[i] for i in pool[q])), q) for q in "apgsv" if pool[q]]
+        if not nxt:
+            break
+        now, e = min(nxt)
+        i = max((x for x in pool[e] if rdy[x] <= now + wait),
+                key=lambda x: (pr[x] - (spare if e == "v" and len(ops[x]["cost"]) > 1 else 0.0), -x))
+        for q in ops[i]["cost"]:
+            pool[q].discard(i)
+        place(i, e, max(now, rdy[i]))
+        free[e] = end[i]
+    return sorted(range(n), key=lambda x: (start[x], x)), eng, start, end
+
+
+def plan(ops):
+    n = len(ops)
+    succ = [[] for _ in range(n)]
+    for i, o in enumerate(ops):
+        for d, lat in o["in"]:
+            succ[d].append((i, lat))
+    pr = [0.0] * n
+    for i in range(n - 1, -1, -1):
+        pr[i] = min(ops[i]["cost"].values()) + max([pr[x] + lat for x, lat in succ[i]] + [0.0])
+    pr = np.array(pr)
+    tags = sorted(set(o["tag"] for o in ops))
+    tg = np.array([tags.index(o["tag"]) for o in ops])
+    rng = np.random.default_rng(SEED)
+    cur = (np.array([BIAS.get(x, 0.0) for x in tags]), np.zeros(n), 300.0, 3000.0)
+    top = None
+    for trial in range(TRIES):
+        bias, noise, wait, spare = cur[0].copy(), cur[1].copy(), cur[2], cur[3]
+        if trial:
+            k = rng.integers(0, 8)
+            if k < 2:
+                bias[rng.integers(0, len(tags))] += rng.normal() * 5000.0
+            elif k == 2:
+                wait = float(rng.choice([100.0, 200.0, 300.0, 450.0, 600.0, 900.0]))
+                spare = float(rng.choice([0.0, 1000.0, 3000.0, 8000.0, 20000.0]))
+            else:
+                noise[rng.integers(0, n, 10)] += rng.normal(size=10) * 3000.0
+        order, eng, start, end = lay(ops, succ, (pr + bias[tg] + noise).tolist(), wait, spare)
+        score = sum(replay(ops, order, eng, c) for c in CASES)
+        if top is None or score <= top[0]:
+            top = (score, order, eng, start, end, dict(zip(tags, bias.tolist())), wait, spare)
+            cur = (bias, noise, wait, spare)
+    return top
+
+
+def rank_program(g, core, T, topo):
+    rank = T.rank_of(core)
+    if rank is None:
+        return None
+    N = len(T.cores)
+    ops = []
+    hist = {}
+    bulks = []
+    cnt = {"d": 0, "r": 0, "sent": 0, "tag": "load"}
+    Q = {"v": g.vector, "a": g.scalar, "p": g.tensor, "g": g, "s": g.sync, "x": None}
+
+    def add(engs, fn, rd, wr, cost, lat=LAT, kind="c", extra=(), acc=False, cls="c", soft=()):
+        i = len(ops)
+        deps = set(extra) | set(soft)
+        for isw, lst in ((False, rd), (True, wr)):
+            for x in lst:
+                nm, lo, hi = x if isinstance(x, tuple) else (x, 0, 1 << 30)
+                w = isw or nm[0] == "@"
+                h = hist.setdefault(nm, [])
+                for (j, jw, a, b) in h:
+                    if j != i and a < hi and lo < b and (w or jw):
+                        deps.add(j)
+                if w:
+                    h[:] = [e for e in h if not (lo <= e[2] and e[3] <= hi)]
+                h.append((i, w, lo, hi))
+        ops.append({"fn": fn, "deps": sorted(deps), "lat": lat, "kind": kind, "acc": acc, "cls": cls, "wr": wr, "soft": tuple(soft),
+                    "tag": cnt["tag"], "in": [(d, 0.0 if d in soft else ops[d]["lat"]) for d in sorted(deps)],
+                    "cost": cost if isinstance(cost, dict) else {e: cost for e in engs}})
+        return i
+
+    def bank(b, lo=0, hi=512, st=1):
+        return T["p%d" % (b // 2)][:, (b % 2) * 512 + lo:(b % 2) * 512 + hi:st]
+
+    def bk_(b):
+        return "@%d" % b
+
+    def comp(engs, fn, rd, wr, cyc):
+        cls, n = cyc if isinstance(cyc, tuple) else ("c", cyc)
+        return add(engs, fn, rd, wr, FIX + max(64, n * RATE[cls]) * CYC, cls=cls)
+
+    def V(fn, rd, wr, cyc):
+        return comp("v", lambda e: fn(g.vector), rd, wr, cyc)
+
+    def ts(out, in0, s1, s2, o0, o1, rd, wr, cyc=64):
+        if s2 is None:
+            return V(lambda q: q.tensor_scalar(out, in0, s1, None, o0), rd, wr, cyc)
+        return V(lambda q: q.tensor_scalar(out, in0, s1, s2, o0, o1), rd, wr, cyc)
+
+    def tt(out, a, b, op, rd, wr, cyc=64):
+        return V(lambda q: q.tensor_tensor(out, a, b, op), rd, wr, cyc)
+
+    def cp(out, a, rd, wr, cyc=64):
+        return V(lambda q: q.tensor_copy(out, a), rd, wr, cyc)
+
+    def scan(out, d0, d1, init, o0, o1, rd, wr, cyc=64):
+        return V(lambda q: q.tensor_tensor_scan(out, d0, d1, init, o0, o1), rd, wr, cyc)
+
+    def ms(out, c, wr, n, half=True):
+        def fn(e):
+            if e == "v":
+                return g.vector.memset(out, float(c))
+            return g.iota(out, [[0, n]], int(c), 0, allow_small_or_imprecise_dtypes=True)
+        return add("vg", fn, [], wr, {"g": 130 + 2 * n * CYC, "v": FIX + max(64, n / 2 if half else n) * CYC})
+
+    def lin(out, a, sc, bi, rd, wr, cyc=64, engs="va"):
+        def fn(e):
+            plain = isinstance(bi, float) and bi == 0.0
+            if e == "a":
+                if plain:
+                    return g.scalar.activation(out, a, AF.Copy, scale=sc)
+                return g.scalar.activation(out, a, AF.Identity, bias=bi, scale=sc)
+            if plain and isinstance(sc, float) and sc == 1.0:
+                return g.vector.tensor_copy(out, a)
+            if plain:
+                return g.vector.tensor_scalar(out, a, sc, None, ALU.mult)
+            return g.vector.tensor_scalar(out, a, sc, bi, ALU.mult, ALU.add)
+        return comp(engs, fn, rd, wr, cyc)
+
+    def either(fv, fa, rd, wr, cyc, engs="va"):
+        return comp(engs, lambda e: fa() if e == "a" else fv(), rd, wr, cyc)
+
+    def nonzero(out, a, rd, wr, cyc, engs="va"):
+        return either(lambda: g.vector.tensor_scalar(out, a, 0.0, None, ALU.not_equal),
+                      lambda: g.scalar.activation(out, a, AF.Abs), rd, wr, cyc, engs)
+
+    def iszero(out, a, rd, wr, cyc):
+        return either(lambda: g.vector.tensor_scalar(out, a, 0.0, None, ALU.is_equal),
+                      lambda: g.scalar.activation(out, a, AF.Relu, bias=1.0, scale=-1.0), rd, wr, cyc)
+
+    def relu(out, a, rd, wr, cyc):
+        return either(lambda: g.vector.tensor_scalar(out, a, 0.0, None, ALU.max),
+                      lambda: g.scalar.activation(out, a, AF.Relu), rd, wr, cyc)
+
+    def pe(mms, rd, wr, acc=False):
+        def fn(e):
+            r = None
+            for m in mms:
+                r = g.tensor.matmul(m[0], m[1], m[2], m[3], m[4])
+            return r
+        return add("p", fn, rd, wr, FIX + sum(max(64, m[5]) for m in mms) * PEC, acc=acc, cls="p")
+
+    def iota(out, pat, base, cm, wr, n, flt=True):
+        if flt:
+            return add("g", lambda e: g.iota(out, pat, base, cm, allow_small_or_imprecise_dtypes=True), [], wr, 130 + 2 * n * CYC)
+        return add("g", lambda e: g.iota(out, pat, base, cm), [], wr, 130 + 2 * n * CYC)
+
+    def sel(out, a, pat, op, fill, base, cm, rd, wr, n):
+        return add("g", lambda e: g.affine_select(out, a, pat, op, fill, base, cm), rd, wr, 170 + 2 * n * CYC)
+
+    def dma(out, src, rd, wr, nbytes, soft=()):
+        sem = T.sem["d%d" % cnt["d"]]
+        cnt["d"] += 1
+        i = add("s", lambda e: g.sync.dma_start(out, src).then_inc(sem, 16), rd, wr, nbytes / LOCAL_RATE + 100.0, lat=2000.0, kind="d",
+                cls="d", soft=soft)
+        ops[i]["sem"], ops[i]["val"] = sem, 16
+        return i
+
+    def send(dr, pairs, rd, land, nbytes, bulk, after=()):
+        sem = T.sem["r%d" % cnt["r"]]
+        cnt["r"] += 1
+        dst = T.cores[(rank + dr) % N]
+        rid, pid = topo.addr(dst)[:2]
+        mask = topo.mask(core, dst)
+        cnt["sent"] += len(topo.engines(core, dst)) * len(pairs)
+
+        def fn(e):
+            for (o, s) in pairs:
+                g.remote_dma(o, s, sem, T.sem.sent, pid, rid, mask)
+        i = add("g", fn, rd, [], 300.0 * len(pairs), lat=0.0, kind="r", extra=after)
+        before = [i] + (bulks[-1:] if bulk else [])
+        j = add("x", None, [], list(land), nbytes / LINK_RATE, lat=HOP, kind="l", extra=before, cls="l")
+        if bulk:
+            bulks.append(add("x", None, [], [], nbytes / LINK_RATE, lat=0.0, kind="r", extra=before, cls="l"))
+        ops[j]["sem"], ops[j]["val"] = sem, len(topo.engines(T.cores[(rank - dr) % N], core)) * len(pairs)
+        return i
+
+    def ind(win, off):
+        return win.indirect(off)
+
+    k = ()
+    for (o, x, wr, nb) in [(T.ivs[:], T.iv[:], "ivs", 19), (T.lvi[:], T.lv[:], "lvi", 14), (T.kds[:], T.kd[:], "kds", 20),
+                           (T.lfs[:], T.lf[:], "lfs", 20), (T.lbi[:, 0:32], T.lb[:], ("lbi", 0, 32), 14), (T.bks[:], T.bk[:], "bks", 20),
+                           (T.lbd[0:128, :], T.lb[:], ("lbd", 0, 1), 14), (T.lbd[128:240, :], T.lb[0:112, :], ("lbd", 1, 2), 14)]:
+        k = (dma(o, x, [], [wr], 1 << nb, k),)
+    for t in range(1, NT):
+        s0 = 16 * ((-SH[t]) % 8)
+        send(t, [(T.lbi[:, 32 * t:32 * t + 32], T.lbd[s0:s0 + 128, :])], ["lbd"], [("lbi", 32 * t, 32 * t + 32)], 1 << 14, False)
+
+    cnt["tag"] = "const"
+    pin, pf = T.pin, T.pf
+    ms(T.ones[:], 1, ["ones"], 512)
+    iota(pin[:, 15:16], [[0, 1]], 0, 1, [("pin", 15, 16)], 1, False)
+    for i in (1, 2, 3, 0):
+        iota(T.bit[:, 128 * i:128 * i + 128], [[0, 64 >> i], [1, 2], [0, 1 << i]], 0, 0, [("bit", 128 * i, 128 * i + 128)], 128)
+    iota(T.cg[:], [[1, 8], [0, 16]], 0, 0, ["cg"], 128)
+    iota(T.c2[:], [[0, 2], [1, 128]], 0, 0, ["c2"], 256)
+    iota(T.k16[:], [[0, 7], [1, 16]], 0, 0, ["k16"], 112)
+    iota(T.bms[:], [[0, 2], [1, 8]], 0, 0, ["bms"], 16)
+    iota(T.jc[:], [[16, 32]], 512, 0, ["jc"], 32)
+    iota(T.jt[:], [[1, 32], [0, 16]], 0, 0, ["jt"], 512)
+    iota(T.jrow[:], [[0, 32], [1, 16]], 0, 0, ["jrow"], 512)
+    dma(T.jrow[0::16, :], T.jt[0::16, :], ["jt"], ["jrow"], 1 << 13)
+    for c, (sh, an) in enumerate([(0, 1), (1, 1), (2, 1), (3, 1), (4, 7), (0, 15), (2, 3), (1, 63), (0, 127)]):
+        ts(pin[:, c:c + 1], pin[:, 15:16], sh, an, ALU.logical_shift_right, ALU.bitwise_and, [("pin", 15, 16)], [("pin", c, c + 1)])
+    P0, P1 = ("pf", 0, 5), ("pf", 5, 9)
+    cp(pf[:, 0:5], pin[:, 0:5], [("pin", 0, 5)], [P0])
+    cp(pf[:, 5:9], pin[:, 5:9], [("pin", 5, 9)], [P1])
+    lin(pf[:, 12:16], pf[:, 0:4], -2.0, 1.0, [P0], [("pf", 12, 16)])
+    lin(pf[:, 16:20], pf[:, 0:4], -2.0, 0.0, [P0], [("pf", 16, 20)])
+    lin(pf[:, 20:24], pf[:, 0:4], 2.0, -1.0, [P0], [("pf", 20, 24)])
+    lin(pf[:, 24:25], pf[:, 4:5], 8.0, 8.0, [P0], [("pf", 24, 25)])
+    lin(pf[:, 25:26], pf[:, 24:25], 1.0, pf[:, 7:8], [P1, ("pf", 24, 25)], [("pf", 25, 26)])
+    ts(T.bm[:], T.cg[:], pf[:, 4:5], None, ALU.is_equal, None, ["cg", P0], ["bm"], 128)
+
+    def blk(nm, i):
+        return T[nm][:, 128 * i:128 * i + 128], (nm, 128 * i, 128 * i + 128)
+    for i in (1, 2, 3, 0):
+        (fa, fr), (ba, br) = blk("fac", i), blk("bit", i)
+        lin(fa, ba, pf[:, 12 + i:13 + i], pf[:, i:i + 1], [br, P0, ("pf", 12, 16)], [fr], 128)
+        if i:
+            lin(fa, fa, float(8 ** (1 << (i - 1)) - 1), 1.0, [fr], [fr], 128)
+        (ha, hr) = blk("hfa", i)
+        lin(ha, ba, pf[:, 16 + i:17 + i], 1.0, [br, ("pf", 16, 20)], [hr], 128)
+    (e0, e0r), (e1, e1r) = blk("ee", 0), blk("ee", 1)
+    tt(e0, blk("fac", 1)[0], T.bm[:], ALU.mult, [blk("fac", 1)[1], "bm"], [e0r], 256)
+    tt(e1, blk("fac", 2)[0], blk("fac", 3)[0], ALU.mult, [blk("fac", 2)[1], blk("fac", 3)[1]], [e1r], 256)
+    tt(e0, e0, e1, ALU.mult, [e0r, e1r], [e0r], 256)
+    tt(e1, e0, blk("fac", 0)[0], ALU.mult, [e0r, blk("fac", 0)[1]], [e1r], 256)
+    tt(T.wc[:], e0, e1, ALU.subtract, [e0r, e1r], ["wc"], 256)
+    lin(T.wb[:], e1, BIG, 0.0, [e1r], ["wb"], 128)
+    tt(T.wf[:], T.wc[:, 0::2], T.wc[:, 1::2], ALU.subtract, ["wc"], ["wf"], 128)
+    (h0, h0r), (h1, h1r) = blk("hh", 0), blk("hh", 1)
+    tt(h0, blk("hfa", 0)[0], blk("hfa", 1)[0], ALU.mult, [("hfa", 0, 256)], [h0r], 256)
+    tt(h1, blk("hfa", 2)[0], blk("hfa", 3)[0], ALU.mult, [("hfa", 256, 512)], [h1r], 256)
+    tt(h0, h0, h1, ALU.mult, [h0r, h1r], [h0r], 256)
+    tt(h0, h0, T.bm[:], ALU.mult, [h0r, "bm"], [h0r], 256)
+    for i in range(4):
+        lin(blk("hs", i)[0], h0, float(16 ** i), 0.0, [h0r], [blk("hs", i)[1]], 128)
+    lin(T.hn[:], h0, -1.0, 0.0, [h0r], ["hn"], 128)
+    cp(T.h16[:], h0, [h0r], ["h16"], 128)
+    relu(T.pl[:], h0, [h0r], ["pl"], 128)
+    relu(T.mi[:], T.hn[:], ["hn"], ["mi"], 128)
+    sel(T.iw[:], T.ones[:, 0:256], [[0, 2], [-1, 128]], ALU.is_equal, 0.0, 0, 1, ["ones"], ["iw"], 256)
+    ident = T.iw[:, 0:128]
+    for i in range(3):
+        lin(blk("isc", i)[0], ident, float(16 ** (i + 1)), 0.0, ["iw"], [blk("isc", i)[1]], 128)
+    cp(T.i16[:], ident, ["iw"], ["i16"], 64)
+    ts(T.cw[:], T.c2[:, 0:136], pf[:, 25:26], None, ALU.is_equal, None, ["c2", ("pf", 25, 26)], ["cw"], 136)
+    ts(T.bms[:], T.bms[:], pf[:, 4:5], None, ALU.is_equal, None, ["bms", P0], ["bms"])
+    ts(T.kv[:, 0:4], T.k16[:, 0:4], pf[:, 6:7], None, ALU.is_equal, None, ["k16", P1], [("kv", 0, 4)])
+    lin(T.kv[:, 4:7], T.kv[:, 0:3], -1.0, 0.0, [("kv", 0, 4)], [("kv", 4, 7)])
+    lin(T.kv[:, 7:8], T.kv[:, 3:4], -BIG, 0.0, [("kv", 0, 4)], [("kv", 7, 8)])
+    ts(T.oh[:], T.k16[:], pf[:, 5:6], None, ALU.is_equal, None, ["k16", P1], ["oh"], 112)
+    sel(T.rm[:], T.ones[:, 0:112], [[0, 7], [1, 16]], ALU.not_equal, 0.0, 0, 0, ["ones"], ["rm"], 112)
+    ms(T.row[:], 0, ["row"], 112, False)
+    ent = [(0, 0, 1, 16), (0, 1, 2, 1), (1, 0, 1, 15), (1, 1, 2, -1), (1, 2, 3, -2), (1, 4, 5, -4), (1, 8, 9, -8),
+           (2, 0, 1, rank + 1), (2, 4, 10, 1), (2, 2, 3, 8), (3, 1, 3, 1), (3, 9, 10, -9),
+           (4, 4, 5, 1), (4, 5, 6, 2), (4, 6, 7, 4), (4, 7, 8, 8), (5, 9, 10, 1), (5, 8, 9, -2)]
+    for (v, a, b, c) in ent:
+        ms(T.row[:, 16 * v + a:16 * v + b], c, [("row", 16 * v + a, 16 * v + b)], b - a, False)
+    V(lambda q: q.memset(T.vec[:, 0:16], 0.25), [], ["vec"], 64)
+    scan(T.row[:, 96:112], T.vec[:, 0:16], T.vec[:, 0:16], float(4 ** 16), ALU.mult, ALU.max, ["vec"], [("row", 96, 112)])
+    tt(T.row[:], T.row[:], T.oh[:], ALU.mult, ["row", "oh"], ["row"], 224)
+    scan(T.vec[:], T.rm[:], T.row[:], 0.0, ALU.mult, ALU.add, ["rm", "row"], ["vec"], 112)
+
+    def vec(v):
+        return T.vec[:, 16 * v + 15:16 * v + 16]
+
+    def z(k):
+        return T.oh[:, k:k + 1]
+    for nm in ("ex", "dg", "dl", "dm", "wr", "mm"):
+        if SCRATCH[nm][2] == HALF:
+            ts(T[nm][:], T.c2[:, 0:SCRATCH[nm][1][1]], 0.0, None, ALU.mult, None, ["c2"], [nm], 144)
+        else:
+            ms(T[nm][:], 0, [nm], SCRATCH[nm][1][1])
+    for h in range(2):
+        lin(T.ex[:, 14 + h:142:16], T.bms[:, 0:8], T.kv[:, h:h + 1], 0.0, ["bms", "kv"], ["ex"])
+        lin(T.et[:, h::2], T.bm[:, h::2], T.kv[:, 4 + h:5 + h], 0.0, ["bm", "kv"], [("et", h, h + 1)])
+        cp(T.wr[:, 1 + h::16], T.bms[:, 0:8], ["bms"], ["wr"])
+    lin(T.ts[:], T.bm[:], T.kv[:, 6:7], 0.0, ["bm", "kv"], ["ts"], 128)
+    lin(T.tb[:], T.bm[:], T.kv[:, 7:8], 0.0, ["bm", "kv"], ["tb"], 128)
+    cp(T.dg[:, 15:143:16], T.bms[:, 0:8], ["bms"], ["dg"])
+    lin(T.dl[:, 15:143:16], T.bms[:, 0:8], vec(0), 0.0, ["bms", "vec"], ["dl"])
+    ts(T.dm[:, 15::16], T.bms[:], z(9), -1.0, ALU.mult, ALU.mult, ["bms", "oh"], ["dm"])
+    lin(T.mm[:, 3::16], T.bms[:, 0:8], vec(1), 0.0, ["bms", "vec"], ["mm"])
+    lin(T.tp[:], T.bm[:], -1.0, 0.0, ["bm"], ["tp"], 128)
+    sel(T.tp[:], T.tp[:], [[-1, 128]], ALU.is_ge, 0.0, 0, 1, ["tp"], ["tp"], 128)
+    lin(T.tr[:], T.bm[:], -4096.0, 0.0, ["bm"], ["tr"], 128)
+    sel(T.tr[:], T.tr[:], [[1, 128]], ALU.is_gt, 0.0, 0, -1, ["tr"], ["tr"], 128)
+    sel(T.tr[:], T.tr[:], [[1, 128]], ALU.not_equal, 4096.0, 0, -1, ["tr"], ["tr"], 128)
+    lin(T.on[:], T.bm[:], 1.0, 0.0, ["bm"], ["on"], 128)
+    lin(T.ge[:], h0, vec(6), 0.0, [h0r, "vec"], ["ge"], 128)
+    lin(pf[:, 26:27], vec(6), vec(6), 0.0, ["vec"], [("pf", 26, 27)])
+    lin(T.sg[:], T.bm[:], pf[:, 26:27], 0.0, ["bm", ("pf", 26, 27)], ["sg"], 128)
+    for b in range(4):
+        lin(T.sg[:, 4 + b::16], T.sg[:, 4 + b::16], pf[:, 20 + b:21 + b], 0.0, ["sg", ("pf", 20, 24)], ["sg"])
+    lin(T.gm[:], T.sg[:], 4096.0, 0.0, ["sg"], ["gm"], 128)
+    lin(T.gp[:], T.sg[:], 16384.0, 0.0, ["sg"], ["gp"], 128)
+    lin(T.gp[:, 8::16], T.sg[:, 8::16], -16384.0, 0.0, ["sg"], ["gp"])
+    for f, (col, nm) in enumerate([(z(0), "oh"), (vec(3), "vec"), (z(3), "oh"), (vec(4), "vec"), (vec(5), "vec")]):
+        if f == 2:
+            ts(T.oy[:, f::5], T.bms[:], col, 0.5, ALU.mult, ALU.mult, ["bms", nm], [("oy", f, f + 1)])
+        else:
+            lin(T.oy[:, f::5], T.bms[:], col, 0.0, ["bms", nm], [("oy", f, f + 1)])
+    ms(T.oc[:], 0, ["oc"], 40)
+    ms(T.oc[:, 0::5], -1, ["oc"], 8)
+    lin(pf[:, 27:28], z(2), -8.0, 0.0, ["oh"], [("pf", 27, 28)])
+    lin(T.jc[:], T.jc[:], 1.0, pf[:, 5:6], ["jc", P1], ["jc"])
+    cp(T.jh[:], T.jc[:], ["jc"], ["jh"])
+    lin(T.jn[:], T.jc[:], -1.0, 0.0, ["jc"], ["jn"])
+    sel(T.m8[:], T.ones[:], [[0, 64], [1, 8]], ALU.not_equal, 0.0, 0, 0, ["ones"], ["m8"], 512)
+    ms(T.xt[:, 3::4], 0, ["xt3"], 512)
+    ms(T.ln[:, 0:CAP], 0, ["ln"], CAP)
+    for t in range(NT):
+        ms(T.rv[:, 208 * t + CAP:208 * t + 208], 0, [("rv", 208 * t, 208 * t + 208)], 16)
+        if t:
+            ms(T.tg[:, 512 * t:512 * t + 512], 0, [("tg", 512 * t, 512 * t + 512)], 512)
+    cnt["tag"] = "kids"
+    cp(T.lvu[:], T.lvi[:], ["lvi"], ["lvu"])
+    cp(T.kau[:], ind(T.kds[:], T.lvu[:]), ["kds", "lvu"], ["kau"], GA(512))
+    cnt["tag"] = "canon"
+
+    PA, PB, PL = T.p0, T.p1, T.p2
+    for hf in range(2):
+        mm = []
+        for c in range(8 * hf, 8 * hf + 8):
+            x = T.ivs[:, 128 * c:128 * c + 128]
+            mm.append((PB[:, 64 * c:64 * c + 64], x, T.wc[:, 1::2], True, True, 128))
+            mm.append((PA[:, 64 * c:64 * c + 64], x, T.wc[:, 0::2], True, True, 128))
+        pe(mm, ["ivs", "wc"], [bk_(hf), bk_(2 + hf)])
+        pe([(PL[:, 64 * c:64 * c + 64], T.ivs[:, 128 * c:128 * c + 128], T.wf[:], True, True, 128) for c in range(8 * hf, 8 * hf + 8)],
+           ["ivs", "wf"], [bk_(4 + hf)])
+    for hf in range(2):
+        a, b = 512 * hf, 512 * hf + 512
+        sb, scr, eqr = ("sb", a, b), ("sc", a, b), ("eq", a, b)
+        qb = 6 + hf
+        lin(T.sb[:, a:b], PB[:, a:b], 1.0, 0.0, [bk_(2 + hf)], [sb], 512)
+        tt(PB[:, a:b], PA[:, a:b], T.sb[:, a:b], ALU.max, [bk_(hf), sb], [bk_(2 + hf)], 512)
+        comp("a", lambda e, a=a, b=b: g.scalar.activation(PL[:, a:b], PL[:, a:b], AF.Abs), [], [bk_(4 + hf)], 512)
+        lin(bank(qb, 2, 256, 4), PA[:, a:b:8], 1.0, 0.0, [bk_(hf)], [bk_(qb)])
+        lin(bank(qb, 3, 256, 4), T.sb[:, a:b:8], 1.0, 0.0, [sb], [bk_(qb)])
+        scan(T.sc[:, a:b], T.m8[:], PB[:, a:b], 0.0, ALU.mult, ALU.max, ["m8", bk_(2 + hf)], [scr], 512)
+        lin(bank(qb, 0, 256, 4), T.sc[:, a + 7:b:8], 1.0, 0.0, [scr], [bk_(qb)])
+
+        def cmp8(e, a=a, b=b):
+            r = None
+            for m in range(8):
+                r = g.vector.tensor_tensor(T.eq[:, a + m:b:8], PB[:, a + m:b:8], T.sc[:, a + 7:b:8], ALU.is_equal)
+            return r
+        add("v", cmp8, [bk_(2 + hf), scr], [eqr], 8 * (FIX + 64 * CYC))
+        tt(T.eq[:, a:b], PL[:, a:b], T.eq[:, a:b], ALU.mult, [bk_(4 + hf), eqr], [eqr], 512)
+        scan(T.sb[:, a:b], T.m8[:], T.eq[:, a:b], 0.0, ALU.mult, ALU.max, ["m8", eqr], [sb], 512)
+        lin(bank(qb, 1, 256, 4), T.sb[:, a + 7:b:8], 1.0, 0.0, [sb], [bk_(qb)])
+        xa, xb = 1024 * hf, 1024 * hf + 1024
+        xr = [("xt%d" % k, hf, hf + 1) for k in range(3)]
+        qq, rr = bank(qb, 0, 256), bank(qb, 256, 512)
+        lin(T.xt[:, xa:xb:4], qq, 1.0, 0.0, [bk_(qb)], [xr[0]], 256)
+        tt(rr, qq, T.xt[:, xa:xb:4], ALU.subtract, [xr[0]], [bk_(qb)], 256)
+        lin(T.xt[:, xa + 1:xb:4], rr, 1.0, 0.0, [bk_(qb)], [xr[1]], 256)
+        tt(T.xt[:, xa + 2:xb:4], rr, T.xt[:, xa + 1:xb:4], ALU.subtract, [bk_(qb), xr[1]], [xr[2]], 256)
+        for u in range(2):
+            bn, lo = hf + 2 * u, xa + 512 * u
+            pe([(bank(bn, 128 * k, 128 * k + 128), T.xt[:, lo + 128 * k:lo + 128 * k + 128], ident, True, True, 128)
+                for k in range(4)], xr + ["xt3", "iw"], [bk_(bn)])
+            lin(T.ct[:, lo:lo + 512], bank(bn), 1.0, 0.0, [bk_(bn)], [("ct", lo, lo + 512)], 512)
+
+    lin(T.tg[:, 0:512], ind(T.ct[:], T.lvu[:]), 1.0, 0.0, ["ct", "lvu"], [("tg", 0, 512)], GA(512))
+    for k in range(3):
+        dma(T.tgd[k], T.tg[k::4, 0:512], [("tg", 0, 512)], [("tgd", k, k + 1)], 1 << 15)
+    for t in range(1, NT):
+        send(t, [(T.tgl[3 * (t - 1) + k], T.tgd[k]) for k in range(3)], ["tgd"], [("tgl", t, t + 1)], 3 << 15, True)
+        s0, c0 = 16 * SH[t], 512 * t
+        for k in range(3):
+            sl, rd = 3 * (t - 1) + k, [("tgl", t, t + 1), ("tg", c0, c0 + 512)]
+            dma(T.tg[s0 + k::4, c0:c0 + 512], T.tgl[sl, 0:128 - s0, :], rd, [("tg%d" % t, 2 * k, 2 * k + 1)], 1 << 14)
+            dma(T.tg[k:s0:4, c0:c0 + 512], T.tgl[sl, 128 - s0:128, :], rd, [("tg%d" % t, 2 * k + 1, 2 * k + 2)], 1 << 14)
+    cnt["tag"] = "words"
+    for q in range(8):
+        lin(T.ga[:, 1024 * q:1024 * q + 1024], ind(T.lfs[:], T.kau[:, 64 * q:64 * q + 64]), 1.0, 0.0, ["lfs", "kau"], [("ga", q, q + 1)], GA(1024))
+    for hf in range(2):
+        for ep in range(2):
+            mm = []
+            for e in (2 * ep, 2 * ep + 1):
+                for i in range(4):
+                    w = ident if i == 0 else blk("isc", i - 1)[0]
+                    mm.append((bank(4 + e, 256 * hf, 256 * hf + 256), w, T.ga[:, 4096 * hf + 4 * e + i:4096 * hf + 4096:16],
+                               i == 0, i == 3, 256))
+            pe(mm, ["iw", "isc", ("ga", 4 * hf, 4 * hf + 4)], [bk_(4 + 2 * ep), bk_(5 + 2 * ep)])
+    for e in range(4):
+        a = 512 * e
+        ts(T.awu[:, a:a + 512], bank(4 + e), WOFF, None, ALU.add, None, [bk_(4 + e)], [("awu", a, a + 512)], 512)
+        lin(T.awf[:, a:a + 512], bank(4 + e), 1.0, 0.0, [bk_(4 + e)], [("awf", a, a + 512)], 512)
+    dma(T.awd[0:128, :], T.awu[:, 0:2048], [("awu", 0, 2048)], [("awd", 0, 1)], 1 << 19)
+    dma(T.awd[128:240, :], T.awu[0:112, 0:2048], [("awu", 0, 2048)], [("awd", 1, 2)], 1 << 19)
+
+    def words(t, after):
+        s0 = 16 * ((-SH[t]) % 8)
+        send(t, [(T.awu[:, 2048 * t:2048 * t + 2048], T.awd[s0:s0 + 128, :])], ["awd"], [("awu", 2048 * t, 2048 * t + 2048)],
+             1 << 19, True, after)
+    words(1, ())
+
+    def claims(t):
+        l0, l1, c0, u = 32 * t, 32 * t + 32, 512 * t, t % 2
+        cnt["tag"] = "claim%d" % t
+        tg = T.tg[:, c0:c0 + 512]
+        tgr = [("tg", c0, c0 + 512), "tg%d" % t]
+        gc, gn = T["gc%d" % u], "gc%d" % u
+        wh, whr = T.wh[:, 512 * u:512 * u + 512], ("wh", u, u + 1)
+        cp(T.lbu[:, l0:l1], T.lbi[:, l0:l1], [("lbi", l0, l1)], [("lbu", l0, l1)])
+        cp(T.wu[:, c0:c0 + 512], ind(T.bks[:], T.lbu[:, l0:l1]), ["bks", ("lbu", l0, l1)], [("wu", t, t + 1)], GA(512))
+        cp(wh, T.wu[:, c0:c0 + 512], [("wu", t, t + 1)], [whr], 256)
+        for q in range(8):
+            lin(gc[:, 1024 * q:1024 * q + 1024], ind(T.ct[:], T.wu[:, c0 + 64 * q:c0 + 64 * q + 64]), 1.0, 0.0,
+                ["ct", ("wu", t, t + 1)], [(gn, q, q + 1)], GA(1024))
+        for q in range(4):
+            mm = []
+            for b in range(2):
+                o = bank(b, 128 * q, 128 * q + 128)
+                mm.append((o, T.et[:], T.tg[:, c0 + 128 * q:c0 + 128 * q + 128], True, False, 128))
+                for kk in range(8):
+                    mm.append((o, T.ex[:, 14 - 2 * kk:142 - 2 * kk], gc[:, 2048 * q + 8 * b + kk:2048 * q + 2048:16], False, kk == 7, 128))
+            pe(mm, ["et", "ex", (gn, 2 * q, 2 * q + 2)] + tgr, [bk_(0), bk_(1)])
+        for b in range(2):
+            nonzero(T.nz[:, 512 * b:512 * b + 512], bank(b), [bk_(b)], [("nz", b, b + 1)], 512)
+        pe([(bank(2), T.cw[:, 8:136], T.nz[:, 0:512], True, False, 512), (bank(2), T.cw[:, 0:128], T.nz[:, 512:1024], False, True, 512)],
+           ["cw", "nz"], [bk_(2)])
+        iszero(T.mt[:], bank(2), [bk_(2)], ["mt"], 512)
+        pe([(bank(3), T.i16[:], wh, True, False, 512), (bank(3), T.tr[:], T.mt[:], False, True, 512)], ["i16", whr, "tr", "mt"], [bk_(3)])
+        ts(T.cc[:], bank(3), -4095.0, 0.0, ALU.add, ALU.max, [bk_(3)], ["cc"], 512)
+        pe([(bank(2, 0, 32), T.dg[:, 15 - i:143 - i], T.cc[:, i::16], i == 0, i == 15, 32) for i in range(16)], ["dg", "cc"], [bk_(2)])
+        ts(T.wl[:, l0:l1], bank(2, 0, 32), -1.0, 0.0, ALU.add, ALU.max, [bk_(2)], [("wl", l0, l1)])
+        ts(T.cl[:, l0:l1], bank(2, 0, 32), 0.0, None, ALU.is_gt, None, [bk_(2)], [("cl", l0, l1)])
+        cnt["tag"] = "shift%d" % t
+        wl, wlr = T.wl[:, l0:l1], ("wl", l0, l1)
+        lin(T.gi[:], ind(T.ivs[:], wl), 1.0, 0.0, ["ivs", wlr], ["gi"], GA(512))
+        ts(T.gk[:], ind(T.kds[:], wl), -2048.0, None, ALU.add, None, ["kds", wlr], ["gk"], GA(512))
+        pe([(bank(3), T.tb[:], tg, True, False, 512), (bank(3), T.wb[:], T.gi[:], False, False, 512),
+            (bank(3), T.wc[:], T.gi[:], False, False, 512), (bank(3), T.ts[:], tg, False, True, 512)],
+           ["tb", "wb", "wc", "ts", "gi"] + tgr, [bk_(3)])
+        ts(T.fit[:], bank(3), 0.0, None, ALU.is_equal, None, [bk_(3)], ["fit"], 512)
+        pe([(bank(2), T.h16[:], T.gk[:], True, True, 512)], ["h16", "gk"], [bk_(2)])
+        pe([(bank(3), T.ge[:], T.fit[:], True, True, 512)], ["ge", "fit"], [bk_(3)])
+        comp("a", lambda e: g.scalar.activation(T.chi[:], bank(3), AF.Sign), [bk_(3)], ["chi"], 512)
+        tt(T.kp[:], bank(2), T.chi[:], ALU.mult, [bk_(2), "chi"], ["kp"], 512)
+        pe([(bank(2), T.hn[:], T.kp[:], True, True, 2048)], ["hn", "kp"], [bk_(2)])
+        lin(T.kb[:, c0:c0 + 512], bank(2), -1.0 / 16, 2048.0, [bk_(2)], [("kb", t, t + 1)], 512)
+        pe([(bank(3), T.wr[:], T.cc[:], True, False, 512), (bank(3), T.mm[:], T.chi[:], False, True, 512)], ["wr", "cc", "mm", "chi"], [bk_(3)])
+        lin(T.wm[:, c0:c0 + 512], bank(3), 1.0, vec(2), [bk_(3), "vec"], [("wm", t, t + 1)], 512)
+
+    def expand(dst, dn, d0, src, sn, off, on, t):
+        r0 = 208 * t
+        for h in range(2):
+            relu(dst[:, d0 + 256 * h:d0 + 256 * h + 256], ind(src[:, r0:r0 + RW], off[:, 32 * t + 16 * h:32 * t + 16 * h + 16]),
+                 [(sn, r0, r0 + 208), (on, 32 * t, 32 * t + 32)], [(dn, d0 + 256 * h, d0 + 256 * h + 256)], GA(256))
+
+    def tests(t):
+        l0, l1, u, c0 = 32 * t, 32 * t + 32, t % 2, 512 * t
+        cnt["tag"] = "test%d" % t
+        if t == 0:
+            F, fr = T.cl[:, 0:32], ("cl", 0, 32)
+            live, lr = T.ones[:, 0:32], "ones"
+        else:
+            for e in range(4):
+                a, o = 2048 * t + 512 * e, 2048 * u + 512 * e
+                ts(T.awf[:, o:o + 512], T.awu[:, a:a + 512], -WOFF, None, ALU.add, None, [("awu", a, a + 512)], [("awf", o, o + 512)], 512)
+            F, fr = T.ff[:], "ff"
+            live, lr = T.lin[:, l0:l1], ("lin", l0, l1)
+            tt(F, live, T.cl[:, l0:l1], ALU.mult, [lr, ("cl", l0, l1)], [fr])
+        scan(T.ss[:], T.ones[:, 0:32], F, 0.0, ALU.mult, ALU.add, ["ones", fr], ["ss"])
+        tt(T.gd[:], F, T.jn[:], ALU.mult, [fr, "jn"], ["gd"])
+        o6 = bank(6, 0, 32)
+        pe([(o6, T.i16[:], T.jh[:], True, False, 32), (o6, T.tp[:], F, False, False, 32), (o6, T.on[:], T.ss[:], False, False, 32),
+            (o6, T.i16[:], T.gd[:], False, True, 32)], ["i16", "jh", "tp", "on", "ss", "gd", fr], [bk_(6)])
+        cp(T.ofu[:], o6, [bk_(6)], ["ofu"])
+        cp(ind(T.ln[:], T.ofu[:]), T.jrow[:], ["ofu", "jrow"], ["ln"], ("s", 512))
+        ts(T.o2[:, l0:l1], T.ofu[:], float(CAP), None, ALU.min, None, ["ofu"], [("o2", l0, l1)])
+        if t:
+            send(-t, [(T.o2h[:, l0:l1], T.o2[:, l0:l1])], [("o2", l0, l1)], [("o2h", l0, l1)], 1 << 13, False)
+        pe([(bank(7, 0, 12), T.dl[:, 15 - i:143 - i], T.ln[:, i:CAP:16], i == 0, i == 15, 12) for i in range(16)], ["dl", "ln"], [bk_(7)])
+        ll = T.lnu[:, 0:12]
+        cp(ll, bank(7, 0, 12), [bk_(7)], ["lnu"])
+        cp(T.kbu[:], ind(T.kb[:, c0:c0 + 512], ll), [("kb", t, t + 1), "lnu"], ["kbu"], GA(CAP))
+        for e in range(4):
+            o = 2048 * u + 512 * e
+            lin(T.ac[:, CAP * e:CAP * e + CAP], ind(T.awf[:, o:o + 512], ll), 1.0, 0.0, [("awf", o, o + 512), "lnu"], [("ac", e, e + 1)], GA(CAP))
+        for b in range(2):
+            x, xr = T.ac[:, 384 * b:384 * b + 384], ("ac", 2 * b, 2 * b + 2)
+            pe([(bank(4 + b, 0, 384), T.hn[:], x, True, False, 1536)], ["hn", xr], [bk_(4 + b)])
+            pe([(bank(6 + b, 0, 384), T.hn[:], x, True, True, 1536)], ["hn", xr], [bk_(6 + b)])
+            lin(T.a2[:, 384 * b:384 * b + 384], bank(6 + b, 0, 384), 2.0, 0.0, [bk_(6 + b)], [("a2", b, b + 1)], 384)
+        for q in range(4):
+            lin(T.gb[:, 768 * q:768 * q + 768], ind(T.lfs[:], T.kbu[:, 48 * q:48 * q + 48]), 1.0, 0.0, ["lfs", "kbu"], [("gb", q, q + 1)], GA(768))
+        for hf in range(2):
+            for b in range(2):
+                mm = []
+                for e in (2 * b, 2 * b + 1):
+                    o = CAP * (e % 2) + 96 * hf
+                    for i in range(4):
+                        mm.append((bank(4 + b, o, o + 96), blk("hs", i)[0], T.gb[:, 1536 * hf + 4 * e + i:1536 * hf + 1536:16],
+                                   False, hf == 1 and e % 2 == 1 and i == 3, 96))
+                pe(mm, ["hs", ("gb", 2 * hf, 2 * hf + 2)], [bk_(4 + b)], acc=True)
+        for k, (bu, bv) in enumerate([(1, 0), (0, 1)]):
+            tt(T.vv[:, 384 * bv:384 * bv + 384], bank(4 + bv, 0, 384), T.a2[:, 384 * bv:384 * bv + 384], ALU.not_equal,
+               [bk_(4 + bv), ("a2", bv, bv + 1)], [("vv", bv, bv + 1)], 384)
+            nonzero(T.uu[:, 384 * bu:384 * bu + 384], bank(4 + bu, 0, 384), [bk_(4 + bu)], [("uu", bu, bu + 1)], 384, "a")
+        for k, (bu, bv) in enumerate([(1, 0), (0, 1)]):
+            mm = []
+            for sgn in range(2):
+                o = bank(6 + sgn, 0, CAP)
+                for x in range(2):
+                    eu, ev = CAP * (2 * bu + x), CAP * (2 * bv + x)
+                    mm.append((o, T.mi[:] if sgn else T.pl[:], T.uu[:, eu:eu + CAP], k == 0 and x == 0, False, CAP))
+                    mm.append((o, T.pl[:] if sgn else T.mi[:], T.vv[:, ev:ev + CAP], False, k == 1 and x == 1, CAP))
+            pe(mm, ["pl", "mi", ("uu", bu, bu + 1), ("vv", bv, bv + 1)], [bk_(6), bk_(7)], acc=(k == 1))
+        for sgn in range(2):
+            iszero(T.fl[:, CAP * sgn:CAP * sgn + CAP], bank(6 + sgn, 0, CAP), [bk_(6 + sgn)], [("fl", sgn, sgn + 1)], CAP)
+        pe([(bank(7, 0, CAP), T.gp[:], T.fl[:, 0:CAP], True, False, CAP), (bank(7, 0, CAP), T.gm[:], T.fl[:, CAP:384], False, True, CAP)],
+           ["gp", "gm", "fl"], [bk_(7)])
+        lin(T.w32[:], ind(T.wm[:, c0:c0 + 512], ll), 1.0, 0.0, [("wm", t, t + 1), "lnu"], ["w32"], GA(CAP))
+        lin(T.wt[:], T.w32[:], z(2), pf[:, 27:28], ["w32", "oh", ("pf", 27, 28)], ["wt"], CAP)
+        tt(T.wd[:], T.w32[:], T.wt[:], ALU.subtract, ["w32", "wt"], ["wd"], 2 * CAP)
+        r0 = 208 * t
+        rr = ("rv", r0, r0 + 208)
+        tt(T.rv[:, r0:r0 + CAP], bank(7, 0, CAP), T.wd[:], ALU.min, [bk_(7), "wd"], [rr], CAP)
+        if t < NT - 1:
+            E, en = (T.eh, "eh") if t == 0 else (T.ev, "ev")
+            expand(E, en, 0, T.rv, "rv", T.o2, "o2", t)
+            rho = 16 * (SH[t + 1] - SH[t])
+            mm = [(o6, T.iw[:, (-rho) % 128:(-rho) % 128 + 128], live, True, False, 32)]
+            for i in range(16):
+                s0 = (15 - i - rho) % 128
+                mm.append((o6, T.dm[:, s0:s0 + 128], E[:, i:512:16], False, i == 15, 32))
+            pe(mm, ["iw", "dm", lr, (en, 0, 512)], [bk_(6)])
+            lin(T.lout[:, l0:l1], o6, 1.0, 0.0, [bk_(6)], [("lout", l0, l1)])
+            k = send(1, [(T.lin[:, l1:l1 + 32], T.lout[:, l0:l1])], [("lout", l0, l1)], [("lin", l1, l1 + 32)], 1 << 13, False)
+            if t + 2 < NT:
+                words(t + 2, [k])
+        if t:
+            send(-t, [(T.rh[:, r0:r0 + RW], T.rv[:, r0:r0 + RW])], [rr], [("rh", r0, r0 + 208)], 256 * RW, False)
+            expand(T.eh, "eh", 512 * t, T.rh, "rh", T.o2h, "o2h", t)
+
+    claims(0)
+    for t in range(NT):
+        if t + 1 < NT:
+            claims(t + 1)
+        tests(t)
+    for h in range(2):
+        a, b = 256 * h, 256 * h + 256
+        py = T.p0[0:40, 512 * h:512 * h + 256]
+        mm = [(py, T.oc[0:1, :], T.ones[0:1, 0:256], True, False, 256)]
+        mm += [(py, T.oy[:, 5 * SH[t]:5 * SH[t] + 40], T.eh[:, 512 * t + a:512 * t + b], False, False, 256) for t in range(NT - 1)]
+        pe(mm, ["oc", "ones", "oy", ("eh", 0, 1536)], [bk_(h)])
+        pe([(py, T.oy[:, 5 * SH[3]:5 * SH[3] + 40], T.eh[:, 1536 + a:1536 + b], False, True, 256)], ["oy", ("eh", 1536 + a, 1536 + b)],
+           [bk_(h)], acc=True)
+        lin(T.ys[0:40, a:b], py, 1.0, 0.0, [bk_(h)], [("ys", a, b)], 256)
+    dma(T.y[:], T.ys[0:40, :], ["ys"], ["y"], 81920)
+
+    if "best" not in PLAN:
+        PLAN["best"] = plan(ops)
+    order = PLAN["best"][1]
+    seq = {"v": 0, "a": 0, "p": 0, "g": 0}
+    for i in order:
+        o = ops[i]
+        o["eng"] = PLAN["best"][2][i]
+        if o["kind"] == "c":
+            seq[o["eng"]] += 1
+            o["sem"], o["val"], o["key"] = T.sem["ev_" + o["eng"]], seq[o["eng"]], o["eng"]
+        else:
+            o["key"] = i
+    seen = {e: {} for e in Q}
+    for i in order:
+        o = ops[i]
+        e = o["eng"]
+        if e == "x":
+            continue
+        need = {}
+        for d in o["deps"]:
+            p = ops[d]
+            if p["kind"] == "r" or d in o["soft"] or (o["acc"] and p["eng"] == "p"):
+                continue
+            if p["val"] > need.get(p["key"], (0, None))[0]:
+                need[p["key"]] = (p["val"], p["sem"])
+        for k, (val, sem) in need.items():
+            if seen[e].get(k, 0) < val:
+                Q[e].wait_ge(sem, val)
+                seen[e][k] = val
+        r = o["fn"](e)
+        if o["kind"] == "c":
+            r.then_inc(o["sem"], 1)
+    for i in order:
+        o = ops[i]
+        if o["kind"] in "dl" and not any(seen[e].get(i, 0) for e in Q):
+            g.wait_ge(o["sem"], o["val"])
+    for e in seq:
+        g.wait_ge(T.sem["ev_" + e], seq[e])
+    g.wait_ge(T.sem.sent, cnt["sent"])
+    return ops

@@ -1,3 +1,4 @@
+import math
 import numpy as np
 from concourse.mybir import AluOpType, ActivationFunctionType
 
@@ -5,42 +6,41 @@ ALU = AluOpType
 AF = ActivationFunctionType
 NV, NL, L, CAP, NT = 2048, 4096, 512, 192, 4
 SH = [t * (t + 1) // 2 % 8 for t in range(NT)]
-RW = CAP + 8
+WIN = 1664
 BF, F32, I32, U16 = "bfloat16", "float32", "int32", "uint16"
 HALF = "float16"
 BIG = float(2 ** 25)
-WOFF = 7.0 * 4369
+WOFF = 32768.0
 
 SCRATCH = {}
 for _t, _l in [
-    (BF, "lfs 4096 ivs 2048 wc 128 wf 64 wb 128 iw 256 isc 384 hs 512 ex 144 et 128 ts 128 tb 128 cw 136 tr 128 tp 128 on 128 dl 144 dm 256 "
-         "mm 128 ge 128 pl 128 mi 128 gp 128 gm 128 oy 80 oc 40 ones 512 rm 112 jt 512 jrow 512 m8 512 xt 2048 ct 2048 tg 2048 ga 8192 "
-         "gc0 8192 gc1 8192 nz 1024 mt 512 cl 128 gi 512 fit 512 chi 512 lin 128 lout 128 ff 32 ss 32 ln 1536 gb 3072 uu 768 vv 768 "
-         "fl 384 wt 192 rv 832 rh 832 ev 512 eh 2048"),
-    (F32, "pf 32 bit 512 fac 512 hfa 512 cg 128 c2 256 bm 128 ee 256 hh 256 k16 112 row 112 oh 112 vec 112 bms 16 kv 16 "
-          "sg 128 hn 128 jc 32 jn 32 sb 1024 sc 1024 eq 1024 awf 4096 kp 512 kb 2048 wm 2048 ac 768 a2 768 w32 192 wd 192 ys 512"),
-    (I32, "kds 2048 bks 2048 lvi 32 lbi 128 pin 16"),
-    (U16, "lvu 32 lbu 128 kau 512 awu 8192 wu 2048 wl 128 ofu 32 o2 128 o2h 128 lnu 16 kbu 192"),
-    (HALF, "h16 128 i16 128 dg 144 wr 128 jh 32 wh 1024 cc 512 gk 512 gd 32"),
+    (BF, "lfs 4096 ivs 2048 wc 128 wf 64 wb 128 wr 128 iw 256 isc 384 hs 512 rt 256 rn 16 ts 128 tb 128 tr 128 tp 128 bm 128 dl 144 dm 256 "
+         "ge 128 gp 128 gm 128 pl 128 mi 128 h0 128 ra 96 rc 96 sr 512 br 512 gh 256 crow 128 neg 128 oc 128 krow 128 qrow 256 "
+         "ones 512 rs 512 k15 512 jt 512 jrow 512 xt 2048 ct 2048 tg 2048 tl 1152 ga 8192 gc0 8192 gc1 8192 nz 512 zp 528 cl 128 gi 512 "
+         "fit 512 chi 2048 lin 128 lout 128 ff 32 ss 48 ln 1664 gb 3072 uu 768 vv 768 fl 384 rv 1664 ev 512"),
+    (F32, "hn 128 jn 32 jc 32 qc 8 sb 1024 sc 1024 eq 1024 xr 256 awf 4096 kp 512 kb 2048 ac 768 a2 1536 ys 256"),
+    (I32, "kds 2048 bks 2048 lvi 32 lbi 32"),
+    (U16, "lvu 32 lbu 128 kau 512 awu 8192 wu 2048 wl 128 ofu 32 lnu 16 kbu 192"),
+    (HALF, "h16 128 i16 128 dg 144 rb 96 jh 32 wh 1024 cc 2048 gk 512 gd 32 ro 1024 ri 1024"),
 ]:
     _w = _l.split()
     for _i in range(0, len(_w), 2):
         SCRATCH[_w[_i]] = ("sbuf", [128, int(_w[_i + 1])], _t)
 for _n in ("p0", "p1", "p2", "p3"):
     SCRATCH[_n] = ("psum", [128, 1024], F32)
-SCRATCH["lbd"] = ("dram", [256, 32], I32)
+SCRATCH["lbd"] = ("dram", [256, 32], U16)
 SCRATCH["awd"] = ("dram", [256, 2048], U16)
-SCRATCH["tgd"] = ("dram", [3, 128, 128], BF)
-SCRATCH["tgl"] = ("dram", [9, 128, 128], BF)
+SCRATCH["tgd"] = ("dram", [256, 384], BF)
 
-SEMAPHORES = ["ev_v", "ev_a", "ev_p", "ev_g", "sent"] + ["d%d" % i for i in range(40)] + ["r%d" % i for i in range(24)]
+SEMAPHORES = ["ev_v", "ev_a", "ev_p", "ev_g", "sent"] + ["d%d" % i for i in range(44)] + ["r%d" % i for i in range(24)]
 
-CYC, PEC, FIX, HOP, LAT = 1.04, 0.55, 70.0, 2600.0, 120.0
-RATE = {"c": 1.0, "g": 1.6, "s": 3.8}
-LOCAL_RATE, LINK_RATE = 250.0, 40.0
-CASES = [{}, {"g": 0.7, "s": 0.6}, {"g": 1.25, "s": 1.4, "l": 1.5}, {"p": 1.6, "d": 0.7}, {"c": 0.85, "g": 0.8, "p": 0.8, "d": 1.4, "l": 0.7}]
-TRIES, SEED = 2000, 2
-BIAS = {"kids": 40000.0, "const": 5000.0}
+CYC, PEC, FIX, HOP, LAT, SEND = 0.9, 0.44, 60.0, 2300.0, 90.0, 350.0
+RATE = {"c": 1.0, "g": 1.56, "s": 3.8}
+LOCAL_RATE, LINK_RATE = 220.0, 60.0
+CASES = [{}, {"c": 0.93, "g": 0.75, "s": 0.6, "p": 0.95}, {"c": 1.3, "g": 1.5, "s": 1.6, "p": 1.3, "l": 1.3}, {"p": 1.3, "d": 0.8, "g": 0.85},
+         {"c": 0.95, "g": 1.1, "d": 1.3, "l": 1.5}]
+TRIES, SEED = 3500, 2
+PIECE = [1024, 1024, 1024, 1024]
 PLAN = {}
 
 
@@ -61,73 +61,87 @@ def replay(ops, order, eng, case):
     return max(end)
 
 
-def lay(ops, succ, pr, wait, spare):
+def lay(ops, before, after, key, spare):
     n = len(ops)
-    left = [len(o["deps"]) for o in ops]
-    rdy, start, end, eng = [0.0] * n, [0.0] * n, [0.0] * n, [None] * n
-    pool = {e: set() for e in "vapgs"}
-    free = {e: 0.0 for e in "vapgs"}
-    todo = [i for i in range(n) if left[i] == 0]
-
-    def place(i, e, t):
-        start[i], eng[i], end[i] = t, e, t + ops[i]["cost"][e]
-        for x, lat in succ[i]:
-            rdy[x] = max(rdy[x], end[i] + lat)
+    left = [len(b) for b in before]
+    start, end, eng = [0.0] * n, [0.0] * n, [None] * n
+    busy = {e: ([], []) for e in "vapgs"}
+    pool = sorted(((key[i], i) for i in range(n) if left[i] == 0), reverse=True)
+    while pool:
+        i = pool.pop()[1]
+        rdy = max([end[d] + lat for d, lat in before[i]] + [0.0])
+        best = None
+        for e, c in ops[i]["cost"].items():
+            t, k = rdy, 0
+            if e != "x":
+                ss, es = busy[e]
+                k, hi = 0, len(es)
+                while k < hi:
+                    m = (k + hi) // 2
+                    if es[m] <= t:
+                        k = m + 1
+                    else:
+                        hi = m
+                while k < len(ss) and ss[k] < t + c:
+                    t = max(t, es[k])
+                    k += 1
+            v = t + c + (spare[i] if e == "v" else 0.0)
+            if best is None or v < best[0]:
+                best = (v, e, t, k, c)
+        v, e, t, k, c = best
+        start[i], end[i], eng[i] = t, t + c, e
+        if e != "x":
+            busy[e][0].insert(k, t)
+            busy[e][1].insert(k, t + c)
+        for x, lat in after[i]:
             left[x] -= 1
             if left[x] == 0:
-                todo.append(x)
-    while True:
-        while todo:
-            i = todo.pop()
-            if "x" in ops[i]["cost"]:
-                place(i, "x", rdy[i])
-            else:
-                for e in ops[i]["cost"]:
-                    pool[e].add(i)
-        nxt = [(max(free[q], min(rdy[i] for i in pool[q])), q) for q in "apgsv" if pool[q]]
-        if not nxt:
-            break
-        now, e = min(nxt)
-        i = max((x for x in pool[e] if rdy[x] <= now + wait),
-                key=lambda x: (pr[x] - (spare if e == "v" and len(ops[x]["cost"]) > 1 else 0.0), -x))
-        for q in ops[i]["cost"]:
-            pool[q].discard(i)
-        place(i, e, max(now, rdy[i]))
-        free[e] = end[i]
-    return sorted(range(n), key=lambda x: (start[x], x)), eng, start, end
+                item, k, hi = (key[x], x), 0, len(pool)
+                while k < hi:
+                    m = (k + hi) // 2
+                    if pool[m] > item:
+                        k = m + 1
+                    else:
+                        hi = m
+                pool.insert(k, item)
+    return start, end, eng
 
 
 def plan(ops):
     n = len(ops)
-    succ = [[] for _ in range(n)]
+    before = [o["in"] for o in ops]
+    after = [[] for _ in range(n)]
     for i, o in enumerate(ops):
         for d, lat in o["in"]:
-            succ[d].append((i, lat))
-    pr = [0.0] * n
+            after[d].append((i, lat))
+    key = [0.0] * n
     for i in range(n - 1, -1, -1):
-        pr[i] = min(ops[i]["cost"].values()) + max([pr[x] + lat for x, lat in succ[i]] + [0.0])
-    pr = np.array(pr)
+        key[i] = -min(ops[i]["cost"].values()) + min([key[x] - lat for x, lat in after[i]] + [0.0])
+    rng = np.random.default_rng(SEED)
     tags = sorted(set(o["tag"] for o in ops))
     tg = np.array([tags.index(o["tag"]) for o in ops])
-    rng = np.random.default_rng(SEED)
-    cur = (np.array([BIAS.get(x, 0.0) for x in tags]), np.zeros(n), 300.0, 3000.0)
-    top = None
+    top, cur = None, None
     for trial in range(TRIES):
-        bias, noise, wait, spare = cur[0].copy(), cur[1].copy(), cur[2], cur[3]
+        lean = cur[2].copy() if trial else np.zeros(len(tags))
+        if rng.random() < 0.3:
+            lean[rng.integers(0, len(tags))] = float(rng.choice([0.0, 200.0, 800.0, 1600.0, 3000.0]))
+        spare = lean[tg].tolist()
         if trial:
-            k = rng.integers(0, 8)
-            if k < 2:
-                bias[rng.integers(0, len(tags))] += rng.normal() * 5000.0
-            elif k == 2:
-                wait = float(rng.choice([100.0, 200.0, 300.0, 450.0, 600.0, 900.0]))
-                spare = float(rng.choice([0.0, 1000.0, 3000.0, 8000.0, 20000.0]))
-            else:
-                noise[rng.integers(0, n, 10)] += rng.normal(size=10) * 3000.0
-        order, eng, start, end = lay(ops, succ, (pr + bias[tg] + noise).tolist(), wait, spare)
+            key = np.array(cur[1]) + rng.normal(size=n) * float(rng.choice([0.0, 50.0, 200.0, 800.0]))
+            if rng.random() < 0.5:
+                key[tg == rng.integers(0, len(tags))] += rng.normal() * 4000.0
+            key = key.tolist()
+        if trial and rng.random() < 0.5:
+            start, end, eng = lay(ops, before, after, key, spare)
+            start, end, eng = lay(ops, after, before, [-x for x in end], spare)
+            key = [-x for x in end]
+        start, end, eng = lay(ops, before, after, key, spare)
+        order = sorted(range(n), key=lambda x: (start[x], x))
         score = sum(replay(ops, order, eng, c) for c in CASES)
-        if top is None or score <= top[0]:
-            top = (score, order, eng, start, end, dict(zip(tags, bias.tolist())), wait, spare)
-            cur = (bias, noise, wait, spare)
+        if cur is None or score <= cur[0] * 1.003:
+            cur = (score, start, lean)
+        if top is None or score < top[0]:
+            top = (score, order, eng, start, end, trial, 0, 0)
     return top
 
 
@@ -142,7 +156,7 @@ def rank_program(g, core, T, topo):
     cnt = {"d": 0, "r": 0, "sent": 0, "tag": "load"}
     Q = {"v": g.vector, "a": g.scalar, "p": g.tensor, "g": g, "s": g.sync, "x": None}
 
-    def add(engs, fn, rd, wr, cost, lat=LAT, kind="c", extra=(), acc=False, cls="c", soft=()):
+    def add(engs, fn, rd, wr, cost, lat=LAT, kind="c", extra=(), cls="c", soft=()):
         i = len(ops)
         deps = set(extra) | set(soft)
         for isw, lst in ((False, rd), (True, wr)):
@@ -156,20 +170,21 @@ def rank_program(g, core, T, topo):
                 if w:
                     h[:] = [e for e in h if not (lo <= e[2] and e[3] <= hi)]
                 h.append((i, w, lo, hi))
-        ops.append({"fn": fn, "deps": sorted(deps), "lat": lat, "kind": kind, "acc": acc, "cls": cls, "wr": wr, "soft": tuple(soft),
-                    "tag": cnt["tag"], "in": [(d, 0.0 if d in soft else ops[d]["lat"]) for d in sorted(deps)],
+        ops.append({"fn": fn, "deps": sorted(deps), "lat": lat, "kind": kind, "cls": cls, "wr": wr, "soft": tuple(soft), "tag": cnt["tag"],
+                    "in": [(d, 0.0 if d in soft or cls == ops[d]["cls"] == "p" else ops[d]["lat"]) for d in sorted(deps)],
                     "cost": cost if isinstance(cost, dict) else {e: cost for e in engs}})
         return i
 
-    def bank(b, lo=0, hi=512, st=1):
-        return T["p%d" % (b // 2)][:, (b % 2) * 512 + lo:(b % 2) * 512 + hi:st]
+    def bank(b, lo=0, hi=512, st=1, p0=0, p1=128):
+        return T["p%d" % (b // 2)][p0:p1, (b % 2) * 512 + lo:(b % 2) * 512 + hi:st]
 
     def bk_(b):
         return "@%d" % b
 
-    def comp(engs, fn, rd, wr, cyc):
+    def comp(engs, fn, rd, wr, cyc, half=False):
         cls, n = cyc if isinstance(cyc, tuple) else ("c", cyc)
-        return add(engs, fn, rd, wr, FIX + max(64, n * RATE[cls]) * CYC, cls=cls)
+        cost = {e: FIX + max(64, n * RATE[cls] * (0.5 if half and e == "v" else 1.0)) * CYC for e in engs}
+        return add(engs, fn, rd, wr, cost, cls=cls)
 
     def V(fn, rd, wr, cyc):
         return comp("v", lambda e: fn(g.vector), rd, wr, cyc)
@@ -188,14 +203,10 @@ def rank_program(g, core, T, topo):
     def scan(out, d0, d1, init, o0, o1, rd, wr, cyc=64):
         return V(lambda q: q.tensor_tensor_scan(out, d0, d1, init, o0, o1), rd, wr, cyc)
 
-    def ms(out, c, wr, n, half=True):
-        def fn(e):
-            if e == "v":
-                return g.vector.memset(out, float(c))
-            return g.iota(out, [[0, n]], int(c), 0, allow_small_or_imprecise_dtypes=True)
-        return add("vg", fn, [], wr, {"g": 130 + 2 * n * CYC, "v": FIX + max(64, n / 2 if half else n) * CYC})
+    def ms(out, c, wr, n):
+        return V(lambda q: q.memset(out, float(c)), [], wr, n / 2)
 
-    def lin(out, a, sc, bi, rd, wr, cyc=64, engs="va"):
+    def lin(out, a, sc, bi, rd, wr, cyc=64, engs="va", half=False):
         def fn(e):
             plain = isinstance(bi, float) and bi == 0.0
             if e == "a":
@@ -207,267 +218,273 @@ def rank_program(g, core, T, topo):
             if plain:
                 return g.vector.tensor_scalar(out, a, sc, None, ALU.mult)
             return g.vector.tensor_scalar(out, a, sc, bi, ALU.mult, ALU.add)
-        return comp(engs, fn, rd, wr, cyc)
+        return comp(engs, fn, rd, wr, cyc, half)
 
-    def either(fv, fa, rd, wr, cyc, engs="va"):
-        return comp(engs, lambda e: fa() if e == "a" else fv(), rd, wr, cyc)
+    def act(out, a, func, rd, wr, cyc, bias=0.0, scale=1.0, more=0.0):
+        return add("a", lambda e: g.scalar.activation(out, a, func, bias=bias, scale=scale), rd, wr, FIX + more + max(64, cyc) * CYC)
 
-    def nonzero(out, a, rd, wr, cyc, engs="va"):
+    def either(fv, fa, rd, wr, cyc, engs="va", half=False):
+        return comp(engs, lambda e: fa() if e == "a" else fv(), rd, wr, cyc, half)
+
+    def nonzero(out, a, rd, wr, cyc):
         return either(lambda: g.vector.tensor_scalar(out, a, 0.0, None, ALU.not_equal),
-                      lambda: g.scalar.activation(out, a, AF.Abs), rd, wr, cyc, engs)
+                      lambda: g.scalar.activation(out, a, AF.Abs), rd, wr, cyc)
 
     def iszero(out, a, rd, wr, cyc):
         return either(lambda: g.vector.tensor_scalar(out, a, 0.0, None, ALU.is_equal),
                       lambda: g.scalar.activation(out, a, AF.Relu, bias=1.0, scale=-1.0), rd, wr, cyc)
 
-    def relu(out, a, rd, wr, cyc):
-        return either(lambda: g.vector.tensor_scalar(out, a, 0.0, None, ALU.max),
-                      lambda: g.scalar.activation(out, a, AF.Relu), rd, wr, cyc)
+    def positive(out, a, rd, wr, cyc):
+        return either(lambda: g.vector.tensor_scalar(out, a, 0.0, None, ALU.is_gt),
+                      lambda: g.scalar.activation(out, a, AF.Sign), rd, wr, cyc)
 
-    def pe(mms, rd, wr, acc=False):
+    def relu(out, a, rd, wr, cyc, sc=1.0, half=False):
+        return either(lambda: g.vector.tensor_scalar(out, a, sc, 0.0, ALU.mult, ALU.max),
+                      lambda: g.scalar.activation(out, a, AF.Relu, scale=sc), rd, wr, cyc, half=half)
+
+    def pe(mms, rd, wr):
         def fn(e):
             r = None
             for m in mms:
                 r = g.tensor.matmul(m[0], m[1], m[2], m[3], m[4])
             return r
-        return add("p", fn, rd, wr, FIX + sum(max(64, m[5]) for m in mms) * PEC, acc=acc, cls="p")
+        return add("p", fn, rd, wr, FIX + sum(max(64, m[5]) for m in mms) * PEC, cls="p")
 
-    def iota(out, pat, base, cm, wr, n, flt=True):
-        if flt:
-            return add("g", lambda e: g.iota(out, pat, base, cm, allow_small_or_imprecise_dtypes=True), [], wr, 130 + 2 * n * CYC)
-        return add("g", lambda e: g.iota(out, pat, base, cm), [], wr, 130 + 2 * n * CYC)
+    def iota(out, pat, base, cm, wr, n):
+        return add("g", lambda e: g.iota(out, pat, base, cm, allow_small_or_imprecise_dtypes=True), [], wr, 130 + 2 * n * CYC)
 
     def sel(out, a, pat, op, fill, base, cm, rd, wr, n):
         return add("g", lambda e: g.affine_select(out, a, pat, op, fill, base, cm), rd, wr, 170 + 2 * n * CYC)
 
+    def gcp(out, a, rd, wr, n):
+        return sel(out, a, [[0, n]], ALU.is_ge, 0.0, 0, 0, rd, wr, n)
+
+    def gfill(out, c, wr, n, engs="g"):
+        def fn(e):
+            if e == "a":
+                return g.scalar.activation(out, T.ones[:, 0:n], AF.Copy, scale=float(c))
+            return g.affine_select(out, T.ones[:, 0:n], [[0, n]], ALU.is_gt, float(c), 0, 0)
+        return add(engs, fn, ["ones"], wr, {e: FIX + max(64, n) * CYC if e == "a" else 170 + 2 * n * CYC for e in engs})
+
+    def put(view, pat, a, c, nm, n):
+        return sel(view, view, pat, ALU.not_equal, float(c), -a, 1, [nm], [nm], n)
+
+    def band(out, src, pat, lo, hi, rd, nm, n):
+        sel(out, src, pat, ALU.is_ge, 0.0, -lo, 1, rd, [nm], n)
+        return sel(out, out, [[-s, c] for s, c in pat], ALU.is_ge, 0.0, hi, -1, [nm], [nm], n)
+
     def dma(out, src, rd, wr, nbytes, soft=()):
         sem = T.sem["d%d" % cnt["d"]]
         cnt["d"] += 1
-        i = add("s", lambda e: g.sync.dma_start(out, src).then_inc(sem, 16), rd, wr, nbytes / LOCAL_RATE + 100.0, lat=2000.0, kind="d",
+        i = add("s", lambda e: g.sync.dma_start(out, src).then_inc(sem, 16), rd, wr, nbytes / LOCAL_RATE + 60.0, lat=2000.0, kind="d",
                 cls="d", soft=soft)
         ops[i]["sem"], ops[i]["val"] = sem, 16
         return i
 
-    def send(dr, pairs, rd, land, nbytes, bulk, after=()):
+    def send(dr, out, src, rd, land, nbytes, bulk, after=()):
         sem = T.sem["r%d" % cnt["r"]]
         cnt["r"] += 1
         dst = T.cores[(rank + dr) % N]
         rid, pid = topo.addr(dst)[:2]
         mask = topo.mask(core, dst)
-        cnt["sent"] += len(topo.engines(core, dst)) * len(pairs)
-
-        def fn(e):
-            for (o, s) in pairs:
-                g.remote_dma(o, s, sem, T.sem.sent, pid, rid, mask)
-        i = add("g", fn, rd, [], 300.0 * len(pairs), lat=0.0, kind="r", extra=after)
+        cnt["sent"] += len(topo.engines(core, dst))
+        i = add("g", lambda e: g.remote_dma(out, src, sem, T.sem.sent, pid, rid, mask), rd, [], SEND, lat=0.0, kind="r", extra=after)
         before = [i] + (bulks[-1:] if bulk else [])
         j = add("x", None, [], list(land), nbytes / LINK_RATE, lat=HOP, kind="l", extra=before, cls="l")
         if bulk:
             bulks.append(add("x", None, [], [], nbytes / LINK_RATE, lat=0.0, kind="r", extra=before, cls="l"))
-        ops[j]["sem"], ops[j]["val"] = sem, len(topo.engines(T.cores[(rank - dr) % N], core)) * len(pairs)
+        ops[j]["sem"], ops[j]["val"] = sem, len(topo.engines(T.cores[(rank - dr) % N], core))
         return i
 
     def ind(win, off):
         return win.indirect(off)
 
-    k = ()
-    for (o, x, wr, nb) in [(T.ivs[:], T.iv[:], "ivs", 19), (T.lvi[:], T.lv[:], "lvi", 14), (T.kds[:], T.kd[:], "kds", 20),
-                           (T.lfs[:], T.lf[:], "lfs", 20), (T.lbi[:, 0:32], T.lb[:], ("lbi", 0, 32), 14), (T.bks[:], T.bk[:], "bks", 20),
-                           (T.lbd[0:128, :], T.lb[:], ("lbd", 0, 1), 14), (T.lbd[128:240, :], T.lb[0:112, :], ("lbd", 1, 2), 14)]:
-        k = (dma(o, x, [], [wr], 1 << nb, k),)
-    for t in range(1, NT):
-        s0 = 16 * ((-SH[t]) % 8)
-        send(t, [(T.lbi[:, 32 * t:32 * t + 32], T.lbd[s0:s0 + 128, :])], ["lbd"], [("lbi", 32 * t, 32 * t + 32)], 1 << 14, False)
-
-    cnt["tag"] = "const"
-    pin, pf = T.pin, T.pf
-    ms(T.ones[:], 1, ["ones"], 512)
-    iota(pin[:, 15:16], [[0, 1]], 0, 1, [("pin", 15, 16)], 1, False)
-    for i in (1, 2, 3, 0):
-        iota(T.bit[:, 128 * i:128 * i + 128], [[0, 64 >> i], [1, 2], [0, 1 << i]], 0, 0, [("bit", 128 * i, 128 * i + 128)], 128)
-    iota(T.cg[:], [[1, 8], [0, 16]], 0, 0, ["cg"], 128)
-    iota(T.c2[:], [[0, 2], [1, 128]], 0, 0, ["c2"], 256)
-    iota(T.k16[:], [[0, 7], [1, 16]], 0, 0, ["k16"], 112)
-    iota(T.bms[:], [[0, 2], [1, 8]], 0, 0, ["bms"], 16)
-    iota(T.jc[:], [[16, 32]], 512, 0, ["jc"], 32)
-    iota(T.jt[:], [[1, 32], [0, 16]], 0, 0, ["jt"], 512)
-    iota(T.jrow[:], [[0, 32], [1, 16]], 0, 0, ["jrow"], 512)
-    dma(T.jrow[0::16, :], T.jt[0::16, :], ["jt"], ["jrow"], 1 << 13)
-    for c, (sh, an) in enumerate([(0, 1), (1, 1), (2, 1), (3, 1), (4, 7), (0, 15), (2, 3), (1, 63), (0, 127)]):
-        ts(pin[:, c:c + 1], pin[:, 15:16], sh, an, ALU.logical_shift_right, ALU.bitwise_and, [("pin", 15, 16)], [("pin", c, c + 1)])
-    P0, P1 = ("pf", 0, 5), ("pf", 5, 9)
-    cp(pf[:, 0:5], pin[:, 0:5], [("pin", 0, 5)], [P0])
-    cp(pf[:, 5:9], pin[:, 5:9], [("pin", 5, 9)], [P1])
-    lin(pf[:, 12:16], pf[:, 0:4], -2.0, 1.0, [P0], [("pf", 12, 16)])
-    lin(pf[:, 16:20], pf[:, 0:4], -2.0, 0.0, [P0], [("pf", 16, 20)])
-    lin(pf[:, 20:24], pf[:, 0:4], 2.0, -1.0, [P0], [("pf", 20, 24)])
-    lin(pf[:, 24:25], pf[:, 4:5], 8.0, 8.0, [P0], [("pf", 24, 25)])
-    lin(pf[:, 25:26], pf[:, 24:25], 1.0, pf[:, 7:8], [P1, ("pf", 24, 25)], [("pf", 25, 26)])
-    ts(T.bm[:], T.cg[:], pf[:, 4:5], None, ALU.is_equal, None, ["cg", P0], ["bm"], 128)
-
     def blk(nm, i):
         return T[nm][:, 128 * i:128 * i + 128], (nm, 128 * i, 128 * i + 128)
-    for i in (1, 2, 3, 0):
-        (fa, fr), (ba, br) = blk("fac", i), blk("bit", i)
-        lin(fa, ba, pf[:, 12 + i:13 + i], pf[:, i:i + 1], [br, P0, ("pf", 12, 16)], [fr], 128)
-        if i:
-            lin(fa, fa, float(8 ** (1 << (i - 1)) - 1), 1.0, [fr], [fr], 128)
-        (ha, hr) = blk("hfa", i)
-        lin(ha, ba, pf[:, 16 + i:17 + i], 1.0, [br, ("pf", 16, 20)], [hr], 128)
-    (e0, e0r), (e1, e1r) = blk("ee", 0), blk("ee", 1)
-    tt(e0, blk("fac", 1)[0], T.bm[:], ALU.mult, [blk("fac", 1)[1], "bm"], [e0r], 256)
-    tt(e1, blk("fac", 2)[0], blk("fac", 3)[0], ALU.mult, [blk("fac", 2)[1], blk("fac", 3)[1]], [e1r], 256)
-    tt(e0, e0, e1, ALU.mult, [e0r, e1r], [e0r], 256)
-    tt(e1, e0, blk("fac", 0)[0], ALU.mult, [e0r, blk("fac", 0)[1]], [e1r], 256)
-    tt(T.wc[:], e0, e1, ALU.subtract, [e0r, e1r], ["wc"], 256)
-    lin(T.wb[:], e1, BIG, 0.0, [e1r], ["wb"], 128)
-    tt(T.wf[:], T.wc[:, 0::2], T.wc[:, 1::2], ALU.subtract, ["wc"], ["wf"], 128)
-    (h0, h0r), (h1, h1r) = blk("hh", 0), blk("hh", 1)
-    tt(h0, blk("hfa", 0)[0], blk("hfa", 1)[0], ALU.mult, [("hfa", 0, 256)], [h0r], 256)
-    tt(h1, blk("hfa", 2)[0], blk("hfa", 3)[0], ALU.mult, [("hfa", 256, 512)], [h1r], 256)
-    tt(h0, h0, h1, ALU.mult, [h0r, h1r], [h0r], 256)
-    tt(h0, h0, T.bm[:], ALU.mult, [h0r, "bm"], [h0r], 256)
-    for i in range(4):
-        lin(blk("hs", i)[0], h0, float(16 ** i), 0.0, [h0r], [blk("hs", i)[1]], 128)
-    lin(T.hn[:], h0, -1.0, 0.0, [h0r], ["hn"], 128)
-    cp(T.h16[:], h0, [h0r], ["h16"], 128)
-    relu(T.pl[:], h0, [h0r], ["pl"], 128)
-    relu(T.mi[:], T.hn[:], ["hn"], ["mi"], 128)
-    sel(T.iw[:], T.ones[:, 0:256], [[0, 2], [-1, 128]], ALU.is_equal, 0.0, 0, 1, ["ones"], ["iw"], 256)
+
+    def row(nm, i=0, n=128):
+        return T[nm][0:1, 128 * i:128 * i + n]
+
+    def back(t):
+        return 16 * ((-SH[t]) % 8)
+
+    G8, G16, GW = [[-16, 8]], [[0, 2], [-16, 8]], [[-16, 8], [0, 16]]
     ident = T.iw[:, 0:128]
-    for i in range(3):
-        lin(blk("isc", i)[0], ident, float(16 ** (i + 1)), 0.0, ["iw"], [blk("isc", i)[1]], 128)
-    cp(T.i16[:], ident, ["iw"], ["i16"], 64)
-    ts(T.cw[:], T.c2[:, 0:136], pf[:, 25:26], None, ALU.is_equal, None, ["c2", ("pf", 25, 26)], ["cw"], 136)
-    ts(T.bms[:], T.bms[:], pf[:, 4:5], None, ALU.is_equal, None, ["bms", P0], ["bms"])
-    ts(T.kv[:, 0:4], T.k16[:, 0:4], pf[:, 6:7], None, ALU.is_equal, None, ["k16", P1], [("kv", 0, 4)])
-    lin(T.kv[:, 4:7], T.kv[:, 0:3], -1.0, 0.0, [("kv", 0, 4)], [("kv", 4, 7)])
-    lin(T.kv[:, 7:8], T.kv[:, 3:4], -BIG, 0.0, [("kv", 0, 4)], [("kv", 7, 8)])
-    ts(T.oh[:], T.k16[:], pf[:, 5:6], None, ALU.is_equal, None, ["k16", P1], ["oh"], 112)
-    sel(T.rm[:], T.ones[:, 0:112], [[0, 7], [1, 16]], ALU.not_equal, 0.0, 0, 0, ["ones"], ["rm"], 112)
-    ms(T.row[:], 0, ["row"], 112, False)
-    ent = [(0, 0, 1, 16), (0, 1, 2, 1), (1, 0, 1, 15), (1, 1, 2, -1), (1, 2, 3, -2), (1, 4, 5, -4), (1, 8, 9, -8),
-           (2, 0, 1, rank + 1), (2, 4, 10, 1), (2, 2, 3, 8), (3, 1, 3, 1), (3, 9, 10, -9),
-           (4, 4, 5, 1), (4, 5, 6, 2), (4, 6, 7, 4), (4, 7, 8, 8), (5, 9, 10, 1), (5, 8, 9, -2)]
-    for (v, a, b, c) in ent:
-        ms(T.row[:, 16 * v + a:16 * v + b], c, [("row", 16 * v + a, 16 * v + b)], b - a, False)
-    V(lambda q: q.memset(T.vec[:, 0:16], 0.25), [], ["vec"], 64)
-    scan(T.row[:, 96:112], T.vec[:, 0:16], T.vec[:, 0:16], float(4 ** 16), ALU.mult, ALU.max, ["vec"], [("row", 96, 112)])
-    tt(T.row[:], T.row[:], T.oh[:], ALU.mult, ["row", "oh"], ["row"], 224)
-    scan(T.vec[:], T.rm[:], T.row[:], 0.0, ALU.mult, ALU.add, ["rm", "row"], ["vec"], 112)
 
-    def vec(v):
-        return T.vec[:, 16 * v + 15:16 * v + 16]
+    k = ()
+    for (o, x, wr, nb) in [(T.ivs[:], T.iv[:], "ivs", 19), (T.lbi[:], T.lb[:], "lbi", 14), (T.lvi[:], T.lv[:], "lvi", 14),
+                           (T.bks[:], T.bk[:], "bks", 20), (T.kds[:], T.kd[:], "kds", 20), (T.lfs[:], T.lf[:], "lfs", 20)]:
+        k = (dma(o, x, [], [wr], 1 << nb, k),)
 
-    def z(k):
-        return T.oh[:, k:k + 1]
-    for nm in ("ex", "dg", "dl", "dm", "wr", "mm"):
-        if SCRATCH[nm][2] == HALF:
-            ts(T[nm][:], T.c2[:, 0:SCRATCH[nm][1][1]], 0.0, None, ALU.mult, None, ["c2"], [nm], 144)
-        else:
-            ms(T[nm][:], 0, [nm], SCRATCH[nm][1][1])
-    for h in range(2):
-        lin(T.ex[:, 14 + h:142:16], T.bms[:, 0:8], T.kv[:, h:h + 1], 0.0, ["bms", "kv"], ["ex"])
-        lin(T.et[:, h::2], T.bm[:, h::2], T.kv[:, 4 + h:5 + h], 0.0, ["bm", "kv"], [("et", h, h + 1)])
-        cp(T.wr[:, 1 + h::16], T.bms[:, 0:8], ["bms"], ["wr"])
-    lin(T.ts[:], T.bm[:], T.kv[:, 6:7], 0.0, ["bm", "kv"], ["ts"], 128)
-    lin(T.tb[:], T.bm[:], T.kv[:, 7:8], 0.0, ["bm", "kv"], ["tb"], 128)
-    cp(T.dg[:, 15:143:16], T.bms[:, 0:8], ["bms"], ["dg"])
-    lin(T.dl[:, 15:143:16], T.bms[:, 0:8], vec(0), 0.0, ["bms", "vec"], ["dl"])
-    ts(T.dm[:, 15::16], T.bms[:], z(9), -1.0, ALU.mult, ALU.mult, ["bms", "oh"], ["dm"])
-    lin(T.mm[:, 3::16], T.bms[:, 0:8], vec(1), 0.0, ["bms", "vec"], ["mm"])
-    lin(T.tp[:], T.bm[:], -1.0, 0.0, ["bm"], ["tp"], 128)
-    sel(T.tp[:], T.tp[:], [[-1, 128]], ALU.is_ge, 0.0, 0, 1, ["tp"], ["tp"], 128)
-    lin(T.tr[:], T.bm[:], -4096.0, 0.0, ["bm"], ["tr"], 128)
-    sel(T.tr[:], T.tr[:], [[1, 128]], ALU.is_gt, 0.0, 0, -1, ["tr"], ["tr"], 128)
-    sel(T.tr[:], T.tr[:], [[1, 128]], ALU.not_equal, 4096.0, 0, -1, ["tr"], ["tr"], 128)
-    lin(T.on[:], T.bm[:], 1.0, 0.0, ["bm"], ["on"], 128)
-    lin(T.ge[:], h0, vec(6), 0.0, [h0r, "vec"], ["ge"], 128)
-    lin(pf[:, 26:27], vec(6), vec(6), 0.0, ["vec"], [("pf", 26, 27)])
-    lin(T.sg[:], T.bm[:], pf[:, 26:27], 0.0, ["bm", ("pf", 26, 27)], ["sg"], 128)
-    for b in range(4):
-        lin(T.sg[:, 4 + b::16], T.sg[:, 4 + b::16], pf[:, 20 + b:21 + b], 0.0, ["sg", ("pf", 20, 24)], ["sg"])
-    lin(T.gm[:], T.sg[:], 4096.0, 0.0, ["sg"], ["gm"], 128)
-    lin(T.gp[:], T.sg[:], 16384.0, 0.0, ["sg"], ["gp"], 128)
-    lin(T.gp[:, 8::16], T.sg[:, 8::16], -16384.0, 0.0, ["sg"], ["gp"])
-    for f, (col, nm) in enumerate([(z(0), "oh"), (vec(3), "vec"), (z(3), "oh"), (vec(4), "vec"), (vec(5), "vec")]):
-        if f == 2:
-            ts(T.oy[:, f::5], T.bms[:], col, 0.5, ALU.mult, ALU.mult, ["bms", nm], [("oy", f, f + 1)])
-        else:
-            lin(T.oy[:, f::5], T.bms[:], col, 0.0, ["bms", nm], [("oy", f, f + 1)])
-    ms(T.oc[:], 0, ["oc"], 40)
-    ms(T.oc[:, 0::5], -1, ["oc"], 8)
-    lin(pf[:, 27:28], z(2), -8.0, 0.0, ["oh"], [("pf", 27, 28)])
-    lin(T.jc[:], T.jc[:], 1.0, pf[:, 5:6], ["jc", P1], ["jc"])
-    cp(T.jh[:], T.jc[:], ["jc"], ["jh"])
-    lin(T.jn[:], T.jc[:], -1.0, 0.0, ["jc"], ["jn"])
-    sel(T.m8[:], T.ones[:], [[0, 64], [1, 8]], ALU.not_equal, 0.0, 0, 0, ["ones"], ["m8"], 512)
-    ms(T.xt[:, 3::4], 0, ["xt3"], 512)
-    ms(T.ln[:, 0:CAP], 0, ["ln"], CAP)
-    for t in range(NT):
-        ms(T.rv[:, 208 * t + CAP:208 * t + 208], 0, [("rv", 208 * t, 208 * t + 208)], 16)
-        if t:
-            ms(T.tg[:, 512 * t:512 * t + 512], 0, [("tg", 512 * t, 512 * t + 512)], 512)
-    cnt["tag"] = "kids"
+    cnt["tag"] = "const0"
+    ms(T.ones[:], 1, ["ones"], 512)
+    ms(T.sr[0:1, 0:128:2], 8, [("sr", 0, 128)], 64)
+    ms(T.sr[0:1, 1:128:2], -8, [("sr", 0, 128)], 64)
+    for i, s in ((3, 2), (1, 1), (2, 1)):
+        iota(row("sr", i), [[0, 64 >> i], [-2 * s, 2], [0, 1 << i]], s, 0, [blk("sr", i)[1]], 128)
+    sel(T.gh[0:8, 0:128], T.ones[0:8, 0:128], [[-1, 8], [0, 16]], ALU.is_equal, 0.0, 0, 1, ["ones"], [("gh", 0, 128)], 128)
+    lin(T.gh[0:8, 128:256], T.gh[0:8, 0:128], -128.0, 0.0, [("gh", 0, 128)], [("gh", 128, 256)], 128, half=True)
+    ex = bank(6, 0, 128)
+    pe([(ex, row("sr", i), row("sr", i), n == 0, False, 128) for n, i in enumerate((0, 3, 1, 2, 2))]
+       + [(ex, T.gh[0:8, 0:128], T.gh[0:8, 128:256], False, True, 128)], ["sr", "gh"], [bk_(6)])
+    l8 = math.log(8.0)
+    act(T.wc[:, 0::2], bank(6, 1, 128, 2), AF.Exp, [bk_(6)], [("wc", 0, 1)], 64, -92.5 * l8, -0.5 * l8, 1300.0)
+    act(T.wc[:, 1::2], bank(6, 0, 128, 2), AF.Exp, [bk_(6)], [("wc", 1, 2)], 64, -92.5 * l8, -0.5 * l8)
+    act(T.wb[:], ex, AF.Exp, [bk_(6)], ["wb"], 128, -92.5 * l8 + math.log(BIG), -0.5 * l8)
+    tt(T.wf[:], T.wc[:, 0::2], T.wc[:, 1::2], ALU.subtract, ["wc"], ["wf"], 128)
+    ms(row("neg"), -2.0 ** 24, ["neg"], 128)
+    ms(T.rs[:], 0, ["rs"], 512)
+    ms(T.rs[:, 0::8], -2.0 ** 26, ["rs"], 64)
+    ms(T.xt[:], 0, ["xt"], 2048)
+    ms(T.wr[:], 0, ["wr"], 128)
+    ms(row("crow"), 0, ["crow"], 128)
+    for a, st, c in ((4, 8, -256), (5, 8, -131072), (3, 4, 1)):
+        ms(T.crow[0:1, a::st], c, ["crow"], 32)
+    sel(T.iw[:], T.ones[:, 0:256], [[0, 2], [-1, 128]], ALU.is_equal, 0.0, 0, 1, ["ones"], ["iw"], 256)
+    for m in range(2):
+        src = T.wc[:, m::16]
+        sel(T.wr[:, 4 + 8 * m::16], src, [[16, 8]], ALU.is_ge, 0.0, 5, -1, ["wc", "wr"], [("wr%d" % m, 0, 1)], 8)
+        band(T.wr[:, 5 + 8 * m::16], src, G8, 6, 11, ["wc", "wr"], ("wr%d" % m, 1, 2), 8)
+        sel(T.wr[:, 6 + 8 * m::16], src, G8, ALU.is_ge, 0.0, -12, 1, ["wc", "wr"], [("wr%d" % m, 2, 3)], 8)
+
+    cnt["tag"] = "lists"
+    cp(T.lbu[:, 0:32], T.lbi[:], ["lbi"], [("lbu", 0, 32)])
     cp(T.lvu[:], T.lvi[:], ["lvi"], ["lvu"])
-    cp(T.kau[:], ind(T.kds[:], T.lvu[:]), ["kds", "lvu"], ["kau"], GA(512))
-    cnt["tag"] = "canon"
+    dma(T.lbd[0:128, :], T.lbu[:, 0:32], [("lbu", 0, 32)], [("lbd", 0, 1)], 1 << 13)
+    dma(T.lbd[128:240, :], T.lbu[0:112, 0:32], [("lbu", 0, 32)], [("lbd", 1, 2)], 1 << 13)
+    for t in range(1, NT):
+        send(t, T.lbu[:, 32 * t:32 * t + 32], T.lbd[back(t):back(t) + 128, :], ["lbd"], [("lbu", 32 * t, 32 * t + 32)], 1 << 13, False)
 
-    PA, PB, PL = T.p0, T.p1, T.p2
+    cnt["tag"] = "canon"
     for hf in range(2):
-        mm = []
-        for c in range(8 * hf, 8 * hf + 8):
-            x = T.ivs[:, 128 * c:128 * c + 128]
-            mm.append((PB[:, 64 * c:64 * c + 64], x, T.wc[:, 1::2], True, True, 128))
-            mm.append((PA[:, 64 * c:64 * c + 64], x, T.wc[:, 0::2], True, True, 128))
-        pe(mm, ["ivs", "wc"], [bk_(hf), bk_(2 + hf)])
-        pe([(PL[:, 64 * c:64 * c + 64], T.ivs[:, 128 * c:128 * c + 128], T.wf[:], True, True, 128) for c in range(8 * hf, 8 * hf + 8)],
-           ["ivs", "wf"], [bk_(4 + hf)])
+        cs = range(8 * hf, 8 * hf + 8)
+        mm = [(bank(hf), row("neg"), T.ones[0:1, :], True, False, 512)]
+        for m in range(2):
+            mm += [(T.p0[:, 64 * c:64 * c + 64], T.ivs[:, 128 * c:128 * c + 128], T.wc[:, m::2], False, m == 1 and c == cs[-1], 64) for c in cs]
+        pe(mm, ["ivs", "wc", "neg", "ones"], [bk_(hf)])
+        pe([(T.p1[:, 64 * c:64 * c + 64], T.ivs[:, 128 * c:128 * c + 128], T.wf[:], True, True, 64) for c in cs], ["ivs", "wf"], [bk_(2 + hf)])
+    for b in range(4):
+        pe([(bank(4 + b), row("crow"), T.ones[0:1, :], True, False, 512), (bank(4 + b), T.wr[:], T.ivs[:, 512 * b:512 * b + 512], False, False, 512)],
+           ["crow", "ones", "wr", "wr0", "wr1", "ivs"], [bk_(4 + b)])
+
+    def split(src, sn, hf, r0):
+        xa, k = 1024 * hf + r0, 2 * hf + r0 // 8
+        x = [T.xt[:, xa + i:1024 * hf + 1024:16] for i in range(3)]
+        xn = [("xt%d" % i, k, k + 1) for i in range(3)]
+        r, rn = T.xr[:, 64 * k:64 * k + 64], ("xr", k, k + 1)
+        lin(x[0], src, 1.0, 0.0, [sn, "xt"], [xn[0]])
+        tt(r, src, x[0], ALU.subtract, [sn, xn[0]], [rn], 128)
+        lin(x[1], r, 1.0, 0.0, [rn, "xt"], [xn[1]])
+        tt(x[2], r, x[1], ALU.subtract, [rn, xn[1], "xt"], [xn[2]], 128)
     for hf in range(2):
         a, b = 512 * hf, 512 * hf + 512
         sb, scr, eqr = ("sb", a, b), ("sc", a, b), ("eq", a, b)
-        qb = 6 + hf
-        lin(T.sb[:, a:b], PB[:, a:b], 1.0, 0.0, [bk_(2 + hf)], [sb], 512)
-        tt(PB[:, a:b], PA[:, a:b], T.sb[:, a:b], ALU.max, [bk_(hf), sb], [bk_(2 + hf)], 512)
-        comp("a", lambda e, a=a, b=b: g.scalar.activation(PL[:, a:b], PL[:, a:b], AF.Abs), [], [bk_(4 + hf)], 512)
-        lin(bank(qb, 2, 256, 4), PA[:, a:b:8], 1.0, 0.0, [bk_(hf)], [bk_(qb)])
-        lin(bank(qb, 3, 256, 4), T.sb[:, a:b:8], 1.0, 0.0, [sb], [bk_(qb)])
-        scan(T.sc[:, a:b], T.m8[:], PB[:, a:b], 0.0, ALU.mult, ALU.max, ["m8", bk_(2 + hf)], [scr], 512)
-        lin(bank(qb, 0, 256, 4), T.sc[:, a + 7:b:8], 1.0, 0.0, [scr], [bk_(qb)])
+        act(bank(2 + hf), bank(2 + hf), AF.Abs, [], [bk_(2 + hf)], 512)
+        scan(T.sc[:, a:b], T.rs[:], bank(hf), 0.0, ALU.add, ALU.max, ["rs", bk_(hf)], [scr], 512)
 
         def cmp8(e, a=a, b=b):
             r = None
             for m in range(8):
-                r = g.vector.tensor_tensor(T.eq[:, a + m:b:8], PB[:, a + m:b:8], T.sc[:, a + 7:b:8], ALU.is_equal)
+                r = g.vector.tensor_tensor(T.eq[:, a + m:b:8], T.p0[:, a + m:b:8], T.sc[:, a + 7:b:8], ALU.is_equal)
             return r
-        add("v", cmp8, [bk_(2 + hf), scr], [eqr], 8 * (FIX + 64 * CYC))
-        tt(T.eq[:, a:b], PL[:, a:b], T.eq[:, a:b], ALU.mult, [bk_(4 + hf), eqr], [eqr], 512)
-        scan(T.sb[:, a:b], T.m8[:], T.eq[:, a:b], 0.0, ALU.mult, ALU.max, ["m8", eqr], [sb], 512)
-        lin(bank(qb, 1, 256, 4), T.sb[:, a + 7:b:8], 1.0, 0.0, [sb], [bk_(qb)])
-        xa, xb = 1024 * hf, 1024 * hf + 1024
-        xr = [("xt%d" % k, hf, hf + 1) for k in range(3)]
-        qq, rr = bank(qb, 0, 256), bank(qb, 256, 512)
-        lin(T.xt[:, xa:xb:4], qq, 1.0, 0.0, [bk_(qb)], [xr[0]], 256)
-        tt(rr, qq, T.xt[:, xa:xb:4], ALU.subtract, [xr[0]], [bk_(qb)], 256)
-        lin(T.xt[:, xa + 1:xb:4], rr, 1.0, 0.0, [bk_(qb)], [xr[1]], 256)
-        tt(T.xt[:, xa + 2:xb:4], rr, T.xt[:, xa + 1:xb:4], ALU.subtract, [bk_(qb), xr[1]], [xr[2]], 256)
+        add("v", cmp8, [bk_(hf), scr], [eqr], 8 * (FIX + 64 * CYC))
+        tt(T.eq[:, a:b], bank(2 + hf), T.eq[:, a:b], ALU.mult, [bk_(2 + hf), eqr], [eqr], 512)
+        scan(T.sb[:, a:b], T.rs[:], T.eq[:, a:b], 0.0, ALU.add, ALU.max, ["rs", eqr], [sb], 512)
+        split(T.sc[:, a + 7:b:8], scr, hf, 0)
+        split(T.sb[:, a + 7:b:8], sb, hf, 8)
         for u in range(2):
-            bn, lo = hf + 2 * u, xa + 512 * u
-            pe([(bank(bn, 128 * k, 128 * k + 128), T.xt[:, lo + 128 * k:lo + 128 * k + 128], ident, True, True, 128)
-                for k in range(4)], xr + ["xt3", "iw"], [bk_(bn)])
+            bn, lo = 4 + 2 * hf + u, 1024 * hf + 512 * u
+            pe([(bank(bn, 128 * k, 128 * k + 128), T.xt[:, lo + 128 * k:lo + 128 * k + 128], ident, False, k == 3, 128) for k in range(4)],
+               [("xt%d" % i, 2 * hf, 2 * hf + 2) for i in range(3)] + ["xt", "iw"], [bk_(bn)])
             lin(T.ct[:, lo:lo + 512], bank(bn), 1.0, 0.0, [bk_(bn)], [("ct", lo, lo + 512)], 512)
 
+    cnt["tag"] = "const1"
+    sel(T.rt[:], T.ones[:, 0:256], [[-8, 2], [-16, 8], [0, 16]], ALU.is_ge, 0.0, 0, 1, ["ones"], ["rt"], 256)
+    sel(T.rt[:], T.rt[:], [[8, 2], [16, 8], [0, 16]], ALU.is_ge, 0.0, 2, -1, ["rt"], ["rt"], 256)
+    lin(T.rt[:, 0:128], T.rt[:, 0:128], BIG, 0.0, ["rt"], ["rt"], 128, half=True)
+    lin(T.rn[:], T.rt[:, 0::16], -1.0, 0.0, ["rt"], ["rn"])
+    band(T.bm[:], T.ones[:, 0:128], GW, 0, 15, ["ones"], "bm", 128)
+    lin(T.tr[:], ident, -4096.0, 0.0, ["iw"], ["tr"], 128, half=True)
+    gcp(T.i16[:], ident, ["iw"], ["i16"], 128)
+    gfill(T.dg[:], 0, ["dg"], 144)
+    gcp(T.dg[:, 15:143:16], T.bm[:, 0::16], ["bm", "dg"], ["dg"], 8)
+    gfill(T.k15[:], 0, ["k15"], 512, "ag")
+    gfill(T.k15[:, 15::16], 1, ["k15"], 32, "ag")
+    gfill(T.zp[:, 0:1], 1, [("zp", 0, 1)], 1, "ag")
+    for i in range(3):
+        lin(blk("isc", i)[0], ident, float(16 ** (i + 1)), 0.0, ["iw"], [blk("isc", i)[1]], 128, half=True)
+    cnt["tag"] = "const2"
+    for i in range(4):
+        iota(row("br", i), [[0, 64 >> i], [1, 2], [0, 1 << i]], 0, 0, [blk("br", i)[1]], 128)
+    iota(row("qrow", 0), [[0, 8], [1, 16]], 0, 0, [blk("qrow", 0)[1]], 128)
+    l16 = math.log(16.0)
+    act(row("qrow", 1), row("qrow", 0), AF.Exp, [blk("qrow", 0)[1]], [blk("qrow", 1)[1]], 128, 15 * l16, -l16)
+    hx = bank(3, 0, 128)
+    pe([(hx, row("br", i), row("br", i), i == 0, i == 3, 128) for i in range(4)]
+       + [(bank(3, 128, 129), row("qrow", 1), T.ones[0:1, 0:1], True, True, 64)], ["br", "qrow", "ones"], [bk_(3)])
+    lin(T.qc[:, 0:1], bank(3, 128, 129), 1.0, 0.0, [bk_(3)], ["qc"])
+    act(hx, hx, AF.Abs, [], [bk_(3)], 128, -2.0)
+    act(hx, hx, AF.Abs, [], [bk_(3)], 128, -1.0)
+    lin(T.h0[:], hx, 2.0, -1.0, [bk_(3)], ["h0"], 128)
+    band(T.h0[:], T.h0[:], GW, 0, 15, ["h0"], "h0", 128)
+    gcp(T.h16[:], T.h0[:], ["h0"], ["h16"], 128)
+    lin(T.hn[:], T.h0[:], -1.0, 0.0, ["h0"], ["hn"], 128)
+    lin(T.ge[:], T.h0[:], T.qc[:, 0:1], 0.0, ["h0", "qc"], ["ge"], 128)
+    for nm, r0, sc in (("ts", 4, 1.0), ("tb", 12, BIG)):
+        gfill(T[nm][:], -sc, [nm], 128, "ag")
+        band(T[nm][:], T[nm][:], GW, r0, r0 + 2, [nm], nm, 128)
+        put(T[nm][:], GW, 3, -256 * sc, nm, 128)
+        put(T[nm][:], GW, 7, -131072 * sc, nm, 128)
+    cnt["tag"] = "const3"
+    for i in range(4):
+        lin(blk("hs", i)[0], T.h0[:], 16.0 ** i, 0.0, ["h0"], [blk("hs", i)[1]], 128, half=True)
+    relu(T.pl[:], T.h0[:], ["h0"], ["pl"], 128, half=True)
+    relu(T.mi[:], T.h0[:], ["h0"], ["mi"], 128, -1.0, half=True)
+    lin(T.gp[:], T.ge[:], 1.0, 0.0, ["ge"], ["gp"], 128, half=True)
+    lin(T.gm[:], T.ge[:], 0.25, 0.0, ["ge"], ["gm"], 128, half=True)
+    lin(T.gp[:, 3::16], T.ge[:, 0::16], -1.0, 0.0, ["ge"], ["gp"])
+    gcp(T.gp[:, 5::16], T.ge[:, 0::16], ["ge"], ["gp"], 8)
+    for c in (3, 5):
+        gcp(T.gm[:, c::16], T.gm[:, 0::16], ["gm"], ["gm"], 8)
+    sel(T.tp[:], T.bm[:], [[1, 128]], ALU.is_gt, 0.0, 0, -1, ["bm"], ["tp"], 128)
+    iota(T.jc[:], [[16, 32]], 512, 1, ["jc"], 32)
+    gcp(T.jh[:], T.jc[:], ["jc"], ["jh"], 32)
+    iota(T.jn[:], [[-16, 32]], -512, -1, ["jn"], 32)
+    iota(T.jt[:], [[1, 32], [0, 16]], 0, 0, ["jt"], 512)
+    iota(T.jrow[:], [[0, 32], [1, 16]], 0, 0, ["jrow"], 512)
+    dma(T.jrow[0::16, :], T.jt[0::16, :], ["jt"], ["jrow"], 1 << 13)
+    for nm in ("dl", "dm", "ra", "rb", "rc", "oc", "krow"):
+        gfill(T[nm][:], 0, [nm], SCRATCH[nm][1][1], "g" if nm == "rb" else "ag")
+    gfill(T.ln[:, 0:CAP], 0, ["ln"], CAP, "ag")
+    for a in range(CAP, WIN, 512):
+        b = min(a + 512, WIN)
+        gfill(T.rv[:, a:b], 0, [("rv", a, b)], b - a, "ag")
+    gfill(T.ss[:, 0:1], 0, [("ss", 0, 1)], 1, "ag")
+    put(T.dl[:, 15:143:16], G8, 0, 16, "dl", 8)
+    put(T.dl[:, 15:143:16], G8, 1, 1, "dl", 8)
+    put(T.dm[:, 15::16], G16, 0, -1, "dm", 16)
+    band(T.rb[:, 1:80:5], T.ones[:, 0:16], G16, 0, 15, ["ones", "rb"], "rb", 16)
+    for nm, f, a, c in [("ra", 0, 0, rank + 1), ("ra", 1, 0, 2048), ("ra", 1, 5, -1), ("ra", 2, 0, 16), ("ra", 3, 0, 15), ("ra", 4, 0, 1),
+                        ("ra", 4, 3, -2), ("rc", 1, 0, -2048), ("rc", 2, 0, -8.5)] + \
+            [("ra", 3, b, -b) for b in (1, 2, 4, 8)] + [("rc", 2, b, -0.5 * b) for b in (1, 2, 4, 8)]:
+        put(T[nm][:, f:80:5], G16, a, c, nm, 16)
+    for nm, f, c in (("krow", 4, 1), ("oc", 0, -1), ("oc", 4, -4)):
+        for h in range(2):
+            gfill(T[nm][:, 64 * h + f:64 * h + 40:5], c, [nm], 8, "ag")
+
+    cnt["tag"] = "targets"
     lin(T.tg[:, 0:512], ind(T.ct[:], T.lvu[:]), 1.0, 0.0, ["ct", "lvu"], [("tg", 0, 512)], GA(512))
     for k in range(3):
-        dma(T.tgd[k], T.tg[k::4, 0:512], [("tg", 0, 512)], [("tgd", k, k + 1)], 1 << 15)
+        dma(T.tgd[0:128, 128 * k:128 * k + 128], T.tg[k::4, 0:512], [("tg", 0, 512)], [("tgd", k, k + 1)], 1 << 15)
+        dma(T.tgd[128:240, 128 * k:128 * k + 128], T.tg[k:112:4, 0:512], [("tg", 0, 512)], [("tgd", 3 + k, 4 + k)], 1 << 15)
+    dma(T.tg[3::4, 512:2048], T.ct[3::4, 0:1536], ["ct"], ["tgone"], 3 << 15)
     for t in range(1, NT):
-        send(t, [(T.tgl[3 * (t - 1) + k], T.tgd[k]) for k in range(3)], ["tgd"], [("tgl", t, t + 1)], 3 << 15, True)
-        s0, c0 = 16 * SH[t], 512 * t
+        a, c0 = 384 * (t - 1), 512 * t
+        send(t, T.tl[:, a:a + 384], T.tgd[back(t):back(t) + 128, :], ["tgd"], [("tl", t, t + 1)], 3 << 15, True)
         for k in range(3):
-            sl, rd = 3 * (t - 1) + k, [("tgl", t, t + 1), ("tg", c0, c0 + 512)]
-            dma(T.tg[s0 + k::4, c0:c0 + 512], T.tgl[sl, 0:128 - s0, :], rd, [("tg%d" % t, 2 * k, 2 * k + 1)], 1 << 14)
-            dma(T.tg[k:s0:4, c0:c0 + 512], T.tgl[sl, 128 - s0:128, :], rd, [("tg%d" % t, 2 * k + 1, 2 * k + 2)], 1 << 14)
+            dma(T.tg[k::4, c0:c0 + 512], T.tl[:, a + 128 * k:a + 128 * k + 128], [("tl", t, t + 1)], [("tg%d" % t, k, k + 1)], 1 << 15)
     cnt["tag"] = "words"
+    cp(T.kau[:], ind(T.kds[:], T.lvu[:]), ["kds", "lvu"], ["kau"], GA(512))
     for q in range(8):
         lin(T.ga[:, 1024 * q:1024 * q + 1024], ind(T.lfs[:], T.kau[:, 64 * q:64 * q + 64]), 1.0, 0.0, ["lfs", "kau"], [("ga", q, q + 1)], GA(1024))
     for hf in range(2):
@@ -481,14 +498,13 @@ def rank_program(g, core, T, topo):
             pe(mm, ["iw", "isc", ("ga", 4 * hf, 4 * hf + 4)], [bk_(4 + 2 * ep), bk_(5 + 2 * ep)])
     for e in range(4):
         a = 512 * e
-        ts(T.awu[:, a:a + 512], bank(4 + e), WOFF, None, ALU.add, None, [bk_(4 + e)], [("awu", a, a + 512)], 512)
-        lin(T.awf[:, a:a + 512], bank(4 + e), 1.0, 0.0, [bk_(4 + e)], [("awf", a, a + 512)], 512)
-    dma(T.awd[0:128, :], T.awu[:, 0:2048], [("awu", 0, 2048)], [("awd", 0, 1)], 1 << 19)
-    dma(T.awd[128:240, :], T.awu[0:112, 0:2048], [("awu", 0, 2048)], [("awd", 1, 2)], 1 << 19)
+        lin(T.awf[:, a:a + 512], bank(4 + e), 1.0, WOFF, [bk_(4 + e)], [("awf", a, a + 512)], 512)
+        gcp(T.awu[:, a:a + 512], T.awf[:, a:a + 512], [("awf", a, a + 512)], [("awu", a, a + 512)], 512)
+        dma(T.awd[0:128, a:a + 512], T.awu[:, a:a + 512], [("awu", a, a + 512)], [("awd", e, e + 1)], 1 << 17)
+        dma(T.awd[128:240, a:a + 512], T.awu[0:112, a:a + 512], [("awu", a, a + 512)], [("awd", 4 + e, 5 + e)], 1 << 17)
 
     def words(t, after):
-        s0 = 16 * ((-SH[t]) % 8)
-        send(t, [(T.awu[:, 2048 * t:2048 * t + 2048], T.awd[s0:s0 + 128, :])], ["awd"], [("awu", 2048 * t, 2048 * t + 2048)],
+        send(t, T.awu[:, 2048 * t:2048 * t + 2048], T.awd[back(t):back(t) + 128, :], ["awd"], [("awu", 2048 * t, 2048 * t + 2048)],
              1 << 19, True, after)
     words(1, ())
 
@@ -496,33 +512,35 @@ def rank_program(g, core, T, topo):
         l0, l1, c0, u = 32 * t, 32 * t + 32, 512 * t, t % 2
         cnt["tag"] = "claim%d" % t
         tg = T.tg[:, c0:c0 + 512]
-        tgr = [("tg", c0, c0 + 512), "tg%d" % t]
+        tgr = [("tg", c0, c0 + 512), "tg%d" % t] + (["tgone"] if t else [])
         gc, gn = T["gc%d" % u], "gc%d" % u
         wh, whr = T.wh[:, 512 * u:512 * u + 512], ("wh", u, u + 1)
-        cp(T.lbu[:, l0:l1], T.lbi[:, l0:l1], [("lbi", l0, l1)], [("lbu", l0, l1)])
+        cc, ccr = T.cc[:, c0:c0 + 512], ("cc", t, t + 1)
+        chi, chr_ = T.chi[:, c0:c0 + 512], ("chi", t, t + 1)
         cp(T.wu[:, c0:c0 + 512], ind(T.bks[:], T.lbu[:, l0:l1]), ["bks", ("lbu", l0, l1)], [("wu", t, t + 1)], GA(512))
-        cp(wh, T.wu[:, c0:c0 + 512], [("wu", t, t + 1)], [whr], 256)
-        for q in range(8):
-            lin(gc[:, 1024 * q:1024 * q + 1024], ind(T.ct[:], T.wu[:, c0 + 64 * q:c0 + 64 * q + 64]), 1.0, 0.0,
-                ["ct", ("wu", t, t + 1)], [(gn, q, q + 1)], GA(1024))
-        for q in range(4):
-            mm = []
-            for b in range(2):
-                o = bank(b, 128 * q, 128 * q + 128)
-                mm.append((o, T.et[:], T.tg[:, c0 + 128 * q:c0 + 128 * q + 128], True, False, 128))
-                for kk in range(8):
-                    mm.append((o, T.ex[:, 14 - 2 * kk:142 - 2 * kk], gc[:, 2048 * q + 8 * b + kk:2048 * q + 2048:16], False, kk == 7, 128))
-            pe(mm, ["et", "ex", (gn, 2 * q, 2 * q + 2)] + tgr, [bk_(0), bk_(1)])
-        for b in range(2):
-            nonzero(T.nz[:, 512 * b:512 * b + 512], bank(b), [bk_(b)], [("nz", b, b + 1)], 512)
-        pe([(bank(2), T.cw[:, 8:136], T.nz[:, 0:512], True, False, 512), (bank(2), T.cw[:, 0:128], T.nz[:, 512:1024], False, True, 512)],
-           ["cw", "nz"], [bk_(2)])
-        iszero(T.mt[:], bank(2), [bk_(2)], ["mt"], 512)
-        pe([(bank(3), T.i16[:], wh, True, False, 512), (bank(3), T.tr[:], T.mt[:], False, True, 512)], ["i16", whr, "tr", "mt"], [bk_(3)])
-        ts(T.cc[:], bank(3), -4095.0, 0.0, ALU.add, ALU.max, [bk_(3)], ["cc"], 512)
-        pe([(bank(2, 0, 32), T.dg[:, 15 - i:143 - i], T.cc[:, i::16], i == 0, i == 15, 32) for i in range(16)], ["dg", "cc"], [bk_(2)])
-        ts(T.wl[:, l0:l1], bank(2, 0, 32), -1.0, 0.0, ALU.add, ALU.max, [bk_(2)], [("wl", l0, l1)])
-        ts(T.cl[:, l0:l1], bank(2, 0, 32), 0.0, None, ALU.is_gt, None, [bk_(2)], [("cl", l0, l1)])
+        gcp(wh, T.wu[:, c0:c0 + 512], [("wu", t, t + 1)], [whr], 512)
+        w = PIECE[t]
+        for a in range(0, 8192, w):
+            lin(gc[:, a:a + w], ind(T.ct[:], T.wu[:, c0 + a // 16:c0 + (a + w) // 16]), 1.0, 0.0, ["ct", ("wu", t, t + 1)], [(gn, a, a + w)], GA(w))
+        for c in range(4):
+            o, x = 128 * c, T.tg[:, c0 + 128 * c:c0 + 128 * c + 128]
+            mm = [(bank(u, o, o + 128), x, T.rt[:, 0:128], True, False, 128)]
+            for h in range(2):
+                mm += [(bank(u, o + k, o + 128, 16), gc[:, 2048 * c + k:2048 * c + 2048:16], T.rn[:, 8 * h:8 * h + 8], False, False, 8) for k in range(16)]
+            mm.append((bank(u, o, o + 128), x, T.rt[:, 128:256], False, True, 128))
+            pe(mm, ["rt", "rn", (gn, 2048 * c, 2048 * c + 2048)] + tgr, [bk_(u)])
+        nonzero(T.nz[:], bank(u), [bk_(u)], ["nz"], 512)
+        scan(T.zp[:, 1:513], T.nz[:], T.k15[:], 1.0, ALU.min, ALU.max, ["nz", "k15"], [("zp", 1, 513)], 256)
+        mm = [(bank(3), T.i16[:], wh, True, False, 512)]
+        for c in range(4):
+            o = 128 * c
+            mm.append((bank(3, o, o + 128), T.nz[:, o:o + 128], T.tr[:], False, False, 128))
+            mm.append((bank(3, o, o + 128), T.zp[:, o:o + 128], blk("isc", 2)[0], False, c == 3, 128))
+        pe(mm, ["i16", whr, "tr", "isc", "nz", "zp"], [bk_(3)])
+        ts(cc, bank(3), -4095.0, 0.0, ALU.add, ALU.max, [bk_(3)], [ccr], 512)
+        pe([(bank(2, 0, 32), T.dg[:, 15 - i:143 - i], T.cc[:, c0 + i:c0 + 512:16], i == 0, i == 15, 32) for i in range(16)], ["dg", ccr], [bk_(2)])
+        ts(T.wl[:, l0:l1], bank(2, 0, 32), -1.0, None, ALU.add, None, [bk_(2)], [("wl", l0, l1)])
+        positive(T.cl[:, l0:l1], bank(2, 0, 32), [bk_(2)], [("cl", l0, l1)], 64)
         cnt["tag"] = "shift%d" % t
         wl, wlr = T.wl[:, l0:l1], ("wl", l0, l1)
         lin(T.gi[:], ind(T.ivs[:], wl), 1.0, 0.0, ["ivs", wlr], ["gi"], GA(512))
@@ -533,120 +551,103 @@ def rank_program(g, core, T, topo):
         ts(T.fit[:], bank(3), 0.0, None, ALU.is_equal, None, [bk_(3)], ["fit"], 512)
         pe([(bank(2), T.h16[:], T.gk[:], True, True, 512)], ["h16", "gk"], [bk_(2)])
         pe([(bank(3), T.ge[:], T.fit[:], True, True, 512)], ["ge", "fit"], [bk_(3)])
-        comp("a", lambda e: g.scalar.activation(T.chi[:], bank(3), AF.Sign), [bk_(3)], ["chi"], 512)
-        tt(T.kp[:], bank(2), T.chi[:], ALU.mult, [bk_(2), "chi"], ["kp"], 512)
+        act(chi, bank(3), AF.Sign, [bk_(3)], [chr_], 512)
+        tt(T.kp[:], bank(2), chi, ALU.mult, [bk_(2), chr_], ["kp"], 512)
         pe([(bank(2), T.hn[:], T.kp[:], True, True, 2048)], ["hn", "kp"], [bk_(2)])
         lin(T.kb[:, c0:c0 + 512], bank(2), -1.0 / 16, 2048.0, [bk_(2)], [("kb", t, t + 1)], 512)
-        pe([(bank(3), T.wr[:], T.cc[:], True, False, 512), (bank(3), T.mm[:], T.chi[:], False, True, 512)], ["wr", "cc", "mm", "chi"], [bk_(3)])
-        lin(T.wm[:, c0:c0 + 512], bank(3), 1.0, vec(2), [bk_(3), "vec"], [("wm", t, t + 1)], 512)
-
-    def expand(dst, dn, d0, src, sn, off, on, t):
-        r0 = 208 * t
-        for h in range(2):
-            relu(dst[:, d0 + 256 * h:d0 + 256 * h + 256], ind(src[:, r0:r0 + RW], off[:, 32 * t + 16 * h:32 * t + 16 * h + 16]),
-                 [(sn, r0, r0 + 208), (on, 32 * t, 32 * t + 32)], [(dn, d0 + 256 * h, d0 + 256 * h + 256)], GA(256))
 
     def tests(t):
         l0, l1, u, c0 = 32 * t, 32 * t + 32, t % 2, 512 * t
+        cnt["tag"] = "conv%d" % t
+        if t:
+            for e in range(4):
+                a, o = 2048 * t + 512 * e, 2048 * u + 512 * e
+                gcp(T.awf[:, o:o + 512], T.awu[:, a:a + 512], [("awu", a, a + 512)], [("awf", o, o + 512)], 512)
         cnt["tag"] = "test%d" % t
         if t == 0:
             F, fr = T.cl[:, 0:32], ("cl", 0, 32)
             live, lr = T.ones[:, 0:32], "ones"
         else:
-            for e in range(4):
-                a, o = 2048 * t + 512 * e, 2048 * u + 512 * e
-                ts(T.awf[:, o:o + 512], T.awu[:, a:a + 512], -WOFF, None, ALU.add, None, [("awu", a, a + 512)], [("awf", o, o + 512)], 512)
             F, fr = T.ff[:], "ff"
             live, lr = T.lin[:, l0:l1], ("lin", l0, l1)
             tt(F, live, T.cl[:, l0:l1], ALU.mult, [lr, ("cl", l0, l1)], [fr])
-        scan(T.ss[:], T.ones[:, 0:32], F, 0.0, ALU.mult, ALU.add, ["ones", fr], ["ss"])
+        scan(T.ss[:, 1:33], T.ones[:, 0:32], F, 0.0, ALU.mult, ALU.add, ["ones", fr], [("ss", 1, 33)])
         tt(T.gd[:], F, T.jn[:], ALU.mult, [fr, "jn"], ["gd"])
-        o6 = bank(6, 0, 32)
-        pe([(o6, T.i16[:], T.jh[:], True, False, 32), (o6, T.tp[:], F, False, False, 32), (o6, T.on[:], T.ss[:], False, False, 32),
-            (o6, T.i16[:], T.gd[:], False, True, 32)], ["i16", "jh", "tp", "on", "ss", "gd", fr], [bk_(6)])
-        cp(T.ofu[:], o6, [bk_(6)], ["ofu"])
+        o7 = bank(7, 0, 32)
+        pe([(o7, T.i16[:], T.jh[:], True, False, 32), (o7, T.tp[:], F, False, False, 32), (o7, T.bm[:], T.ss[:, 0:32], False, False, 32),
+            (o7, T.i16[:], T.gd[:], False, True, 32)], ["i16", "jh", "tp", "bm", "ss", "gd", fr], [bk_(7)])
+        cp(T.ofu[:], o7, [bk_(7)], ["ofu"])
         cp(ind(T.ln[:], T.ofu[:]), T.jrow[:], ["ofu", "jrow"], ["ln"], ("s", 512))
-        ts(T.o2[:, l0:l1], T.ofu[:], float(CAP), None, ALU.min, None, ["ofu"], [("o2", l0, l1)])
-        if t:
-            send(-t, [(T.o2h[:, l0:l1], T.o2[:, l0:l1])], [("o2", l0, l1)], [("o2h", l0, l1)], 1 << 13, False)
         pe([(bank(7, 0, 12), T.dl[:, 15 - i:143 - i], T.ln[:, i:CAP:16], i == 0, i == 15, 12) for i in range(16)], ["dl", "ln"], [bk_(7)])
         ll = T.lnu[:, 0:12]
         cp(ll, bank(7, 0, 12), [bk_(7)], ["lnu"])
         cp(T.kbu[:], ind(T.kb[:, c0:c0 + 512], ll), [("kb", t, t + 1), "lnu"], ["kbu"], GA(CAP))
         for e in range(4):
             o = 2048 * u + 512 * e
-            lin(T.ac[:, CAP * e:CAP * e + CAP], ind(T.awf[:, o:o + 512], ll), 1.0, 0.0, [("awf", o, o + 512), "lnu"], [("ac", e, e + 1)], GA(CAP))
-        for b in range(2):
-            x, xr = T.ac[:, 384 * b:384 * b + 384], ("ac", 2 * b, 2 * b + 2)
-            pe([(bank(4 + b, 0, 384), T.hn[:], x, True, False, 1536)], ["hn", xr], [bk_(4 + b)])
-            pe([(bank(6 + b, 0, 384), T.hn[:], x, True, True, 1536)], ["hn", xr], [bk_(6 + b)])
-            lin(T.a2[:, 384 * b:384 * b + 384], bank(6 + b, 0, 384), 2.0, 0.0, [bk_(6 + b)], [("a2", b, b + 1)], 384)
+            lin(T.ac[:, CAP * e:CAP * e + CAP], ind(T.awf[:, o:o + 512], ll), 1.0, -WOFF, [("awf", o, o + 512), "lnu"], [("ac", e, e + 1)], GA(CAP))
         for q in range(4):
             lin(T.gb[:, 768 * q:768 * q + 768], ind(T.lfs[:], T.kbu[:, 48 * q:48 * q + 48]), 1.0, 0.0, ["lfs", "kbu"], [("gb", q, q + 1)], GA(768))
         for hf in range(2):
-            for b in range(2):
-                mm = []
-                for e in (2 * b, 2 * b + 1):
-                    o = CAP * (e % 2) + 96 * hf
-                    for i in range(4):
-                        mm.append((bank(4 + b, o, o + 96), blk("hs", i)[0], T.gb[:, 1536 * hf + 4 * e + i:1536 * hf + 1536:16],
-                                   False, hf == 1 and e % 2 == 1 and i == 3, 96))
-                pe(mm, ["hs", ("gb", 2 * hf, 2 * hf + 2)], [bk_(4 + b)], acc=True)
-        for k, (bu, bv) in enumerate([(1, 0), (0, 1)]):
-            tt(T.vv[:, 384 * bv:384 * bv + 384], bank(4 + bv, 0, 384), T.a2[:, 384 * bv:384 * bv + 384], ALU.not_equal,
-               [bk_(4 + bv), ("a2", bv, bv + 1)], [("vv", bv, bv + 1)], 384)
-            nonzero(T.uu[:, 384 * bu:384 * bu + 384], bank(4 + bu, 0, 384), [bk_(4 + bu)], [("uu", bu, bu + 1)], 384, "a")
-        for k, (bu, bv) in enumerate([(1, 0), (0, 1)]):
-            mm = []
-            for sgn in range(2):
-                o = bank(6 + sgn, 0, CAP)
-                for x in range(2):
-                    eu, ev = CAP * (2 * bu + x), CAP * (2 * bv + x)
-                    mm.append((o, T.mi[:] if sgn else T.pl[:], T.uu[:, eu:eu + CAP], k == 0 and x == 0, False, CAP))
-                    mm.append((o, T.pl[:] if sgn else T.mi[:], T.vv[:, ev:ev + CAP], False, k == 1 and x == 1, CAP))
-            pe(mm, ["pl", "mi", ("uu", bu, bu + 1), ("vv", bv, bv + 1)], [bk_(6), bk_(7)], acc=(k == 1))
-        for sgn in range(2):
-            iszero(T.fl[:, CAP * sgn:CAP * sgn + CAP], bank(6 + sgn, 0, CAP), [bk_(6 + sgn)], [("fl", sgn, sgn + 1)], CAP)
-        pe([(bank(7, 0, CAP), T.gp[:], T.fl[:, 0:CAP], True, False, CAP), (bank(7, 0, CAP), T.gm[:], T.fl[:, CAP:384], False, True, CAP)],
-           ["gp", "gm", "fl"], [bk_(7)])
-        lin(T.w32[:], ind(T.wm[:, c0:c0 + 512], ll), 1.0, 0.0, [("wm", t, t + 1), "lnu"], ["w32"], GA(CAP))
-        lin(T.wt[:], T.w32[:], z(2), pf[:, 27:28], ["w32", "oh", ("pf", 27, 28)], ["wt"], CAP)
-        tt(T.wd[:], T.w32[:], T.wt[:], ALU.subtract, ["w32", "wt"], ["wd"], 2 * CAP)
-        r0 = 208 * t
-        rr = ("rv", r0, r0 + 208)
-        tt(T.rv[:, r0:r0 + CAP], bank(7, 0, CAP), T.wd[:], ALU.min, [bk_(7), "wd"], [rr], CAP)
+            o = 384 * hf
+            pe([(bank(6 + hf, 96 * e, 96 * e + 96), T.hn[:], T.ac[:, CAP * e + 96 * hf:CAP * e + 96 * hf + 96], True, True, 384) for e in range(4)],
+               ["hn", "ac"], [bk_(6 + hf)])
+            for s in range(2):
+                lin(T.a2[:, 768 * s + o:768 * s + o + 384], bank(6 + hf, 0, 384), 2.0 * s - 1.0, 0.0, [bk_(6 + hf)], [("a2", 2 * s + hf, 2 * s + hf + 1)], 384)
+        for hf in range(2):
+            o = 384 * hf
+            pe([(bank(4 + hf, 96 * e, 96 * e + 96), blk("hs", i)[0], T.gb[:, 1536 * hf + 4 * e + i:1536 * hf + 1536:16], i == 0, i == 3, 96)
+                for e in range(4) for i in range(4)], ["hs", ("gb", 2 * hf, 2 * hf + 2)], [bk_(4 + hf)])
+            for s, nm in enumerate(("uu", "vv")):
+                tt(T[nm][:, o:o + 384], bank(4 + hf, 0, 384), T.a2[:, 768 * s + o:768 * s + o + 384], ALU.not_equal,
+                   [bk_(4 + hf), ("a2", 2 * s + hf, 2 * s + hf + 1)], [(nm, hf, hf + 1)], 384)
+            for k, nm in enumerate(("uu", "vv")):
+                pe([(bank(6 + s, 96 * hf, 96 * hf + 96), T.mi[:] if s != k else T.pl[:], T[nm][:, o + 96 * e:o + 96 * e + 96], k == 0 and e == 0,
+                     k == 1 and e == 3, 96) for s in range(2) for e in range(4)], ["pl", "mi", (nm, hf, hf + 1)], [bk_(6), bk_(7)])
+        for s in range(2):
+            iszero(T.fl[:, CAP * s:CAP * s + CAP], bank(6 + s, 0, CAP), [bk_(6 + s)], [("fl", s, s + 1)], CAP)
+        pe([(bank(4, 0, CAP), T.gp[:], T.fl[:, 0:CAP], True, False, CAP), (bank(4, 0, CAP), T.gm[:], T.fl[:, CAP:384], False, True, CAP)],
+           ["gp", "gm", "fl"], [bk_(4)])
+        positive(T.rv[:, 0:CAP], bank(4, 0, CAP), [bk_(4)], [("rv", 0, CAP)], CAP)
+        for h in range(2):
+            relu(T.ev[:, 256 * h:256 * h + 256], ind(T.rv[:], T.ofu[:, 16 * h:16 * h + 16]), ["rv", "ofu"], [("ev", h, h + 1)], GA(256))
         if t < NT - 1:
-            E, en = (T.eh, "eh") if t == 0 else (T.ev, "ev")
-            expand(E, en, 0, T.rv, "rv", T.o2, "o2", t)
             rho = 16 * (SH[t + 1] - SH[t])
-            mm = [(o6, T.iw[:, (-rho) % 128:(-rho) % 128 + 128], live, True, False, 32)]
+            mm = [(o7, T.iw[:, (-rho) % 128:(-rho) % 128 + 128], live, True, False, 32)]
             for i in range(16):
                 s0 = (15 - i - rho) % 128
-                mm.append((o6, T.dm[:, s0:s0 + 128], E[:, i:512:16], False, i == 15, 32))
-            pe(mm, ["iw", "dm", lr, (en, 0, 512)], [bk_(6)])
-            lin(T.lout[:, l0:l1], o6, 1.0, 0.0, [bk_(6)], [("lout", l0, l1)])
-            k = send(1, [(T.lin[:, l1:l1 + 32], T.lout[:, l0:l1])], [("lout", l0, l1)], [("lin", l1, l1 + 32)], 1 << 13, False)
+                mm.append((o7, T.dm[:, s0:s0 + 128], T.ev[:, i:512:16], False, i == 15, 32))
+            pe(mm, ["iw", "dm", lr, "ev"], [bk_(7)])
+            lin(T.lout[:, l0:l1], o7, 1.0, 0.0, [bk_(7)], [("lout", l0, l1)])
+            k = send(1, T.lin[:, l1:l1 + 32], T.lout[:, l0:l1], [("lout", l0, l1)], [("lin", l1, l1 + 32)], 1 << 13, False)
             if t + 2 < NT:
                 words(t + 2, [k])
+        cnt["tag"] = "res%d" % t
+        rb, s5 = (5 if t < NT - 1 else 2), 5 * SH[t]
+        mm = [(bank(rb, 0, 256), row("krow"), T.ones[0:1, 0:256], True, False, 256)]
+        for h in range(2):
+            o = bank(rb, 0, 256, 1, 64 * h, 64 * h + 64)
+            mm.append((o, T.rb[:, s5:s5 + 64], T.cc[:, c0 + 256 * h:c0 + 256 * h + 256], False, False, 256))
+            mm.append((o, T.rc[:, s5:s5 + 64], T.chi[:, c0 + 256 * h:c0 + 256 * h + 256], False, False, 256))
+        pe(mm, ["krow", "ones", "rb", "rc", ("cc", t, t + 1), ("chi", t, t + 1)], [bk_(rb)])
+        pe([(bank(rb, 0, 256, 1, 64 * h, 64 * h + 64), T.ra[:, s5:s5 + 64], T.ev[:, 256 * h:256 * h + 256], False, True, 256) for h in range(2)],
+           ["ra", "ev"], [bk_(rb)])
+        r0 = 256 * t
+        ts((T.ro if t else T.ri)[:, r0:r0 + 256], bank(rb, 0, 256), 0.0, None, ALU.max, None, [bk_(rb)], [("ro" if t else "ri", t, t + 1)], 256)
         if t:
-            send(-t, [(T.rh[:, r0:r0 + RW], T.rv[:, r0:r0 + RW])], [rr], [("rh", r0, r0 + 208)], 256 * RW, False)
-            expand(T.eh, "eh", 512 * t, T.rh, "rh", T.o2h, "o2h", t)
+            send(-t, T.ri[:, r0:r0 + 256], T.ro[:, r0:r0 + 256], [("ro", t, t + 1)], [("ri", t, t + 1)], 1 << 16, False)
 
     claims(0)
     for t in range(NT):
         if t + 1 < NT:
             claims(t + 1)
         tests(t)
+    cnt["tag"] = "end"
+    py = bank(0, 0, 256)
+    pe([(py, row("oc"), T.ones[0:1, 0:256], True, False, 256)]
+       + [(py, T.i16[:], T.ri[:, 256 * t:256 * t + 256], False, t == NT - 2, 256) for t in range(NT - 1)], ["oc", "ones", "i16", ("ri", 0, NT - 1)], [bk_(0)])
+    tt(T.ys[:], py, T.ri[:, 768:1024], ALU.add, [bk_(0), ("ri", NT - 1, NT)], ["ys"], 256)
     for h in range(2):
-        a, b = 256 * h, 256 * h + 256
-        py = T.p0[0:40, 512 * h:512 * h + 256]
-        mm = [(py, T.oc[0:1, :], T.ones[0:1, 0:256], True, False, 256)]
-        mm += [(py, T.oy[:, 5 * SH[t]:5 * SH[t] + 40], T.eh[:, 512 * t + a:512 * t + b], False, False, 256) for t in range(NT - 1)]
-        pe(mm, ["oc", "ones", "oy", ("eh", 0, 1536)], [bk_(h)])
-        pe([(py, T.oy[:, 5 * SH[3]:5 * SH[3] + 40], T.eh[:, 1536 + a:1536 + b], False, True, 256)], ["oy", ("eh", 1536 + a, 1536 + b)],
-           [bk_(h)], acc=True)
-        lin(T.ys[0:40, a:b], py, 1.0, 0.0, [bk_(h)], [("ys", a, b)], 256)
-    dma(T.y[:], T.ys[0:40, :], ["ys"], ["y"], 81920)
+        dma(T.y[:, 256 * h:256 * h + 256], T.ys[64 * h:64 * h + 40, :], ["ys"], [("y", h, h + 1)], 40960)
 
     if "best" not in PLAN:
         PLAN["best"] = plan(ops)
@@ -669,7 +670,7 @@ def rank_program(g, core, T, topo):
         need = {}
         for d in o["deps"]:
             p = ops[d]
-            if p["kind"] == "r" or d in o["soft"] or (o["acc"] and p["eng"] == "p"):
+            if p["kind"] == "r" or d in o["soft"] or (e == "p" and p["eng"] == "p"):
                 continue
             if p["val"] > need.get(p["key"], (0, None))[0]:
                 need[p["key"]] = (p["val"], p["sem"])

@@ -1,5 +1,6 @@
 import math
 import numpy as np
+from concourse.bass import DstId, RemoteDMATransfer
 from concourse.mybir import AluOpType, ActivationFunctionType
 
 ALU = AluOpType
@@ -11,17 +12,22 @@ BF, F32, I32, U16 = "bfloat16", "float32", "int32", "uint16"
 HALF = "float16"
 BIG = float(2 ** 25)
 WOFF = 32768.0
+NW = 2
+PARTS = [2, 1, 1, 2]
+PIECE = [1024, 512, 512, 512]
+GAP = 1024
+STEP = 96
 
 SCRATCH = {}
 for _t, _l in [
-    (BF, "lfs 4096 ivs 2048 wc 128 wf 64 wb 128 wr 128 iw 256 isc 384 hs 512 rt 256 rn 16 ts 128 tb 128 tr 128 tp 128 bm 128 dl 144 dm 256 "
-         "ge 128 gp 128 gm 128 pl 128 mi 128 h0 128 ra 96 rc 96 sr 512 br 512 gh 256 crow 128 neg 128 oc 128 krow 128 qrow 256 "
-         "ones 512 rs 512 k15 512 jt 512 jrow 512 xt 2048 ct 2048 tg 2048 tl 1152 ga 8192 gc0 8192 gc1 8192 nz 512 zp 528 cl 128 gi 512 "
-         "fit 512 chi 2048 lin 128 lout 128 ff 32 ss 48 ln 1664 gb 3072 uu 768 vv 768 fl 384 rv 1664 ev 512"),
-    (F32, "hn 128 jn 32 jc 32 qc 8 sb 1024 sc 1024 eq 1024 xr 256 awf 4096 kp 512 kb 2048 ac 768 a2 1536 ys 256"),
+    (BF, "lfs 4096 ivs 2048 wc 128 wf 64 wb 128 wr 128 iw 256 ni 128 isc 384 hs 512 rt 256 rn 16 ts 128 tb 128 tr 128 tp 128 bm 128 dl 144 "
+         "dm 256 ge 128 gp 128 gm 128 pl 128 mi 128 h0 128 ra 96 rc 96 sr 512 br 512 gh 256 crow 128 neg 128 oc 128 krow 128 qrow 256 "
+         "ones 512 rs 512 k15 512 jt 512 jrow 512 xt 2048 ct 2048 tg 2048 tl 1152 ga 8192 gc0 8192 gc1 8192 nz 512 zp 528 cl 128 "
+         "gi 512 fit 512 chi 2048 lin 128 lout 128 ff 32 ss 48 ln 1664 gb 3072 uu 768 vv 768 fl 384 rv 1664 ev 512"),
+    (F32, "hn 128 idf 128 jc 32 qc 8 sb 1024 sc 1024 eq 1024 awf 4096 kp 512 kb 2048 ac 768 a2 1536 ys 256"),
     (I32, "kds 2048 bks 2048 lvi 32 lbi 32"),
     (U16, "lvu 32 lbu 128 kau 512 awu 8192 wu 2048 wl 128 ofu 32 lnu 16 kbu 192"),
-    (HALF, "h16 128 i16 128 dg 144 rb 96 jh 32 wh 1024 cc 2048 gk 512 gd 32 ro 1024 ri 1024"),
+    (HALF, "h16 128 i16 128 dg 144 rb 96 wh 1024 cc 2048 gk 512 ro 1024 ri 1024"),
 ]:
     _w = _l.split()
     for _i in range(0, len(_w), 2):
@@ -29,18 +35,19 @@ for _t, _l in [
 for _n in ("p0", "p1", "p2", "p3"):
     SCRATCH[_n] = ("psum", [128, 1024], F32)
 SCRATCH["lbd"] = ("dram", [256, 32], U16)
-SCRATCH["awd"] = ("dram", [256, 2048], U16)
+SCRATCH["awd"] = ("dram", [256 * NW, 2048 // NW], U16)
 SCRATCH["tgd"] = ("dram", [256, 384], BF)
 
-SEMAPHORES = ["ev_v", "ev_a", "ev_p", "ev_g", "sent"] + ["d%d" % i for i in range(44)] + ["r%d" % i for i in range(24)]
+SEMAPHORES = ["ev_v", "ev_a", "ev_p", "ev_g", "sent"] + ["d%d" % i for i in range(44)] + ["r%d" % i for i in range(30)]
 
 CYC, PEC, FIX, HOP, LAT, SEND = 0.9, 0.44, 60.0, 2300.0, 90.0, 350.0
 RATE = {"c": 1.0, "g": 1.56, "s": 3.8}
 LOCAL_RATE, LINK_RATE = 220.0, 60.0
-CASES = [{}, {"c": 0.93, "g": 0.75, "s": 0.6, "p": 0.95}, {"c": 1.3, "g": 1.5, "s": 1.6, "p": 1.3, "l": 1.3}, {"p": 1.3, "d": 0.8, "g": 0.85},
-         {"c": 0.95, "g": 1.1, "d": 1.3, "l": 1.5}]
-TRIES, SEED = 3500, 2
-PIECE = [1024, 1024, 1024, 1024]
+CASES = [{}, {"c": 0.93, "gpsimd": 0.93, "g": 0.7, "s": 0.6, "p": 0.95, "r": 3.0, "after l": 1.4, "after c": 1.5},
+         {"c": 1.35, "gpsimd": 1.35, "g": 1.5, "s": 1.6, "p": 1.35, "l": 1.3}, {"c": 0.95, "g": 0.75, "p": 1.2, "d": 0.7, "l": 1.5, "after d": 1.3},
+         {"c": 1.1, "gpsimd": 1.1, "g": 1.2, "p": 1.1, "d": 1.3, "l": 0.6, "r": 2.0, "after c": 2.0}]
+WEIGHT = [1.0, 1.0, 0.7, 1.0, 0.9]
+TRIES, STEPS, HEAT, SIDE, SEED = 40, 26000, 1000.0, 0.3, 2
 PLAN = {}
 
 
@@ -48,20 +55,7 @@ def GA(n):
     return ("g", n)
 
 
-def replay(ops, order, eng, case):
-    free, end = {}, [0.0] * len(ops)
-    for i in order:
-        o, e = ops[i], eng[i]
-        c = o["cost"][e] * case.get(o["cls"], 1.0)
-        t = max([end[d] + lat for d, lat in o["in"]] + [0.0])
-        if e != "x":
-            t = max(t, free.get(e, 0.0))
-            free[e] = t + c
-        end[i] = t + c
-    return max(end)
-
-
-def lay(ops, before, after, key, spare):
+def lay(ops, before, after, key):
     n = len(ops)
     left = [len(b) for b in before]
     start, end, eng = [0.0] * n, [0.0] * n, [None] * n
@@ -75,74 +69,129 @@ def lay(ops, before, after, key, spare):
             t, k = rdy, 0
             if e != "x":
                 ss, es = busy[e]
-                k, hi = 0, len(es)
-                while k < hi:
-                    m = (k + hi) // 2
-                    if es[m] <= t:
-                        k = m + 1
-                    else:
-                        hi = m
-                while k < len(ss) and ss[k] < t + c:
+                while k < len(ss) and (es[k] <= t or ss[k] < t + c):
                     t = max(t, es[k])
                     k += 1
-            v = t + c + (spare[i] if e == "v" else 0.0)
-            if best is None or v < best[0]:
-                best = (v, e, t, k, c)
-        v, e, t, k, c = best
-        start[i], end[i], eng[i] = t, t + c, e
-        if e != "x":
-            busy[e][0].insert(k, t)
-            busy[e][1].insert(k, t + c)
+            if best is None or t + c < best[0]:
+                best = (t + c, e, t, k)
+        end[i], eng[i], start[i], k = best
+        if eng[i] != "x":
+            busy[eng[i]][0].insert(k, start[i])
+            busy[eng[i]][1].insert(k, end[i])
         for x, lat in after[i]:
             left[x] -= 1
             if left[x] == 0:
-                item, k, hi = (key[x], x), 0, len(pool)
-                while k < hi:
-                    m = (k + hi) // 2
-                    if pool[m] > item:
-                        k = m + 1
-                    else:
-                        hi = m
-                pool.insert(k, item)
+                pool.append((key[x], x))
+        pool.sort(reverse=True)
     return start, end, eng
+
+
+def replay(ins, cost, order, eng, lo=0, old=None):
+    n = len(ins)
+    end, why = (old[0][:], old[1][:]) if old else ([0.0] * n, [-1] * n)
+    free, last = {"x": 0.0}, {}
+    for i in reversed(order[:lo]):
+        if eng[i] not in free:
+            free[eng[i]], last[eng[i]] = end[i], i
+            if len(free) == 6:
+                break
+    for i in order[lo:]:
+        t, w, e = 0.0, -1, eng[i]
+        for d, lat in ins[i]:
+            x = end[d] + lat
+            if x > t:
+                t, w = x, d
+        if e != "x":
+            x = free.get(e, 0.0)
+            if x > t:
+                t, w = x, -2 - last[e]
+            free[e], last[e] = t + cost[i][e], i
+        end[i], why[i] = t + cost[i][e], w
+    return end, why
+
+
+def waits(why, i):
+    held = []
+    while i != -1:
+        w = why[i]
+        if w < -1:
+            w = -2 - w
+            held.append((w, i))
+        i = w
+    return held
+
+
+def priced(ops, case):
+    return ([[(d, lat * case.get("after " + ops[d]["kind"], 1.0)) for d, lat in o["in"]] for o in ops],
+            [{e: c * case.get("gpsimd" if e == "g" and o["cls"] == "c" else o["cls"], 1.0) for e, c in o["cost"].items()} for o in ops])
 
 
 def plan(ops):
     n = len(ops)
-    before = [o["in"] for o in ops]
-    after = [[] for _ in range(n)]
+    ins = [o["in"] for o in ops]
+    outs = [[] for _ in range(n)]
     for i, o in enumerate(ops):
         for d, lat in o["in"]:
-            after[d].append((i, lat))
+            outs[d].append((i, lat))
+    costs = [priced(ops, case) for case in CASES]
+    marks = [i for i, o in enumerate(ops) if o["wr"] and o["wr"][0][0] in ("lout", "kb")]
+
+    def score(order, eng, lo=0, old=None):
+        r = [replay(c[0], c[1], order, eng, lo, old and old[k]) for k, c in enumerate(costs)]
+        return sum((max(x[0]) + SIDE * sum(x[0][i] for i in marks) / len(marks)) * w for x, w in zip(r, WEIGHT)), r
     key = [0.0] * n
     for i in range(n - 1, -1, -1):
-        key[i] = -min(ops[i]["cost"].values()) + min([key[x] - lat for x, lat in after[i]] + [0.0])
+        key[i] = -min(ops[i]["cost"].values()) + min([key[x] - lat for x, lat in outs[i]] + [0.0])
     rng = np.random.default_rng(SEED)
-    tags = sorted(set(o["tag"] for o in ops))
-    tg = np.array([tags.index(o["tag"]) for o in ops])
-    top, cur = None, None
+    best = None
     for trial in range(TRIES):
-        lean = cur[2].copy() if trial else np.zeros(len(tags))
-        if rng.random() < 0.3:
-            lean[rng.integers(0, len(tags))] = float(rng.choice([0.0, 200.0, 800.0, 1600.0, 3000.0]))
-        spare = lean[tg].tolist()
-        if trial:
-            key = np.array(cur[1]) + rng.normal(size=n) * float(rng.choice([0.0, 50.0, 200.0, 800.0]))
-            if rng.random() < 0.5:
-                key[tg == rng.integers(0, len(tags))] += rng.normal() * 4000.0
-            key = key.tolist()
-        if trial and rng.random() < 0.5:
-            start, end, eng = lay(ops, before, after, key, spare)
-            start, end, eng = lay(ops, after, before, [-x for x in end], spare)
-            key = [-x for x in end]
-        start, end, eng = lay(ops, before, after, key, spare)
+        start, end, eng = lay(ops, ins, outs, key)
         order = sorted(range(n), key=lambda x: (start[x], x))
-        score = sum(replay(ops, order, eng, c) for c in CASES)
-        if cur is None or score <= cur[0] * 1.003:
-            cur = (score, start, lean)
-        if top is None or score < top[0]:
-            top = (score, order, eng, start, end, trial, 0, 0)
-    return top
+        s, held = score(order, eng)
+        if best is None or s < best[0]:
+            best = (s, order, eng, held)
+        end = lay(ops, outs, ins, (rng.normal(size=n) * 200.0 - np.array(end)).tolist())[1]
+        key = [-x for x in end]
+    cur, order, eng, res = best
+    pos = {x: k for k, x in enumerate(order)}
+    for step in range(STEPS):
+        o2, e2, u = order, eng, rng.random(6)
+        end, why = res[int(u[0] * len(res))]
+        held = waits(why, marks[int(u[1] * len(marks))] if u[2] < SIDE else end.index(max(end)))
+        if not held:
+            continue
+        j, i = held[int(u[3] * len(held))]
+        m, far = u[4], (0, 0, 1, 3)[int(u[5] * 4)]
+        free = [x for x in (i, j) if len(ops[x]["cost"]) > 1]
+        if m < 0.3 and free:
+            x = free[int(u[5] * len(free))]
+            e2 = list(eng)
+            e2[x] = [e for e in ops[x]["cost"] if e != eng[x]][0]
+            lo = hi = pos[x]
+        else:
+            x, k, d, rel = (i, pos[j], -1, ins) if m < 0.65 else (j, pos[i], 1, outs)
+            while far and 0 <= k + d < n:
+                k += d
+                far -= eng[order[k]] == eng[x]
+            lo, hi = min(k, pos[x]), max(k, pos[x])
+            move, todo = {x}, [x]
+            while todo:
+                for y, lat in rel[todo.pop()]:
+                    if lo <= pos[y] <= hi and y not in move:
+                        move.add(y)
+                        todo.append(y)
+            if len(move) > 12:
+                continue
+            a, b = [y for y in order[lo:hi + 1] if y in move], [y for y in order[lo:hi + 1] if y not in move]
+            o2 = order[:lo] + (a + b if d < 0 else b + a) + order[hi + 1:]
+        s, h = score(o2, e2, lo, res)
+        if s <= cur or rng.random() < math.exp((cur - s) / (HEAT * (1 - step / STEPS) + 1.0)):
+            cur, res, order, eng = s, h, o2, e2
+            for k in range(lo, hi + 1):
+                pos[order[k]] = k
+            if s < best[0]:
+                best = (s, o2, e2, h)
+    return best
 
 
 def rank_program(g, core, T, topo):
@@ -152,7 +201,7 @@ def rank_program(g, core, T, topo):
     N = len(T.cores)
     ops = []
     hist = {}
-    bulks = []
+    line = []
     cnt = {"d": 0, "r": 0, "sent": 0, "tag": "load"}
     Q = {"v": g.vector, "a": g.scalar, "p": g.tensor, "g": g, "s": g.sync, "x": None}
 
@@ -189,16 +238,8 @@ def rank_program(g, core, T, topo):
     def V(fn, rd, wr, cyc):
         return comp("v", lambda e: fn(g.vector), rd, wr, cyc)
 
-    def ts(out, in0, s1, s2, o0, o1, rd, wr, cyc=64):
-        if s2 is None:
-            return V(lambda q: q.tensor_scalar(out, in0, s1, None, o0), rd, wr, cyc)
-        return V(lambda q: q.tensor_scalar(out, in0, s1, s2, o0, o1), rd, wr, cyc)
-
     def tt(out, a, b, op, rd, wr, cyc=64):
         return V(lambda q: q.tensor_tensor(out, a, b, op), rd, wr, cyc)
-
-    def cp(out, a, rd, wr, cyc=64):
-        return V(lambda q: q.tensor_copy(out, a), rd, wr, cyc)
 
     def scan(out, d0, d1, init, o0, o1, rd, wr, cyc=64):
         return V(lambda q: q.tensor_tensor_scan(out, d0, d1, init, o0, o1), rd, wr, cyc)
@@ -206,7 +247,7 @@ def rank_program(g, core, T, topo):
     def ms(out, c, wr, n):
         return V(lambda q: q.memset(out, float(c)), [], wr, n / 2)
 
-    def lin(out, a, sc, bi, rd, wr, cyc=64, engs="va", half=False):
+    def lin(out, a, sc, bi, rd, wr, cyc=64, half=False):
         def fn(e):
             plain = isinstance(bi, float) and bi == 0.0
             if e == "a":
@@ -218,29 +259,31 @@ def rank_program(g, core, T, topo):
             if plain:
                 return g.vector.tensor_scalar(out, a, sc, None, ALU.mult)
             return g.vector.tensor_scalar(out, a, sc, bi, ALU.mult, ALU.add)
-        return comp(engs, fn, rd, wr, cyc, half)
+        return comp("va", fn, rd, wr, cyc, half)
 
-    def act(out, a, func, rd, wr, cyc, bias=0.0, scale=1.0, more=0.0):
-        return add("a", lambda e: g.scalar.activation(out, a, func, bias=bias, scale=scale), rd, wr, FIX + more + max(64, cyc) * CYC)
+    def act(out, a, func, rd, wr, cyc, bias=0.0, scale=1.0, more=0.0, soft=()):
+        return add("a", lambda e: g.scalar.activation(out, a, func, bias=bias, scale=scale), rd, wr, FIX + more + max(64, cyc) * CYC, soft=soft)
 
-    def either(fv, fa, rd, wr, cyc, engs="va", half=False):
-        return comp(engs, lambda e: fa() if e == "a" else fv(), rd, wr, cyc, half)
+    def either(out, a, vec, sca, rd, wr, cyc, half=False):
+        def fn(e):
+            if e == "a":
+                return g.scalar.activation(out, a, sca[0], bias=sca[1], scale=sca[2])
+            if vec[1] is None:
+                return g.vector.tensor_scalar(out, a, vec[0], None, vec[2])
+            return g.vector.tensor_scalar(out, a, vec[0], vec[1], vec[2], vec[3])
+        return comp("va", fn, rd, wr, cyc, half)
 
     def nonzero(out, a, rd, wr, cyc):
-        return either(lambda: g.vector.tensor_scalar(out, a, 0.0, None, ALU.not_equal),
-                      lambda: g.scalar.activation(out, a, AF.Abs), rd, wr, cyc)
+        return either(out, a, (0.0, None, ALU.not_equal), (AF.Abs, 0.0, 1.0), rd, wr, cyc)
 
     def iszero(out, a, rd, wr, cyc):
-        return either(lambda: g.vector.tensor_scalar(out, a, 0.0, None, ALU.is_equal),
-                      lambda: g.scalar.activation(out, a, AF.Relu, bias=1.0, scale=-1.0), rd, wr, cyc)
+        return either(out, a, (0.0, None, ALU.is_equal), (AF.Relu, 1.0, -1.0), rd, wr, cyc)
 
     def positive(out, a, rd, wr, cyc):
-        return either(lambda: g.vector.tensor_scalar(out, a, 0.0, None, ALU.is_gt),
-                      lambda: g.scalar.activation(out, a, AF.Sign), rd, wr, cyc)
+        return either(out, a, (0.0, None, ALU.is_gt), (AF.Sign, 0.0, 1.0), rd, wr, cyc)
 
     def relu(out, a, rd, wr, cyc, sc=1.0, half=False):
-        return either(lambda: g.vector.tensor_scalar(out, a, sc, 0.0, ALU.mult, ALU.max),
-                      lambda: g.scalar.activation(out, a, AF.Relu, scale=sc), rd, wr, cyc, half=half)
+        return either(out, a, (sc, 0.0, ALU.mult, ALU.max), (AF.Relu, 0.0, sc), rd, wr, cyc, half)
 
     def pe(mms, rd, wr):
         def fn(e):
@@ -259,12 +302,12 @@ def rank_program(g, core, T, topo):
     def gcp(out, a, rd, wr, n):
         return sel(out, a, [[0, n]], ALU.is_ge, 0.0, 0, 0, rd, wr, n)
 
-    def gfill(out, c, wr, n, engs="g"):
+    def gfill(out, c, wr, n):
         def fn(e):
             if e == "a":
                 return g.scalar.activation(out, T.ones[:, 0:n], AF.Copy, scale=float(c))
             return g.affine_select(out, T.ones[:, 0:n], [[0, n]], ALU.is_gt, float(c), 0, 0)
-        return add(engs, fn, ["ones"], wr, {e: FIX + max(64, n) * CYC if e == "a" else 170 + 2 * n * CYC for e in engs})
+        return add("ag", fn, ["ones"], wr, {"a": FIX + max(64, n) * CYC, "g": 170 + 2 * n * CYC})
 
     def put(view, pat, a, c, nm, n):
         return sel(view, view, pat, ALU.not_equal, float(c), -a, 1, [nm], [nm], n)
@@ -273,28 +316,40 @@ def rank_program(g, core, T, topo):
         sel(out, src, pat, ALU.is_ge, 0.0, -lo, 1, rd, [nm], n)
         return sel(out, out, [[-s, c] for s, c in pat], ALU.is_ge, 0.0, hi, -1, [nm], [nm], n)
 
-    def dma(out, src, rd, wr, nbytes, soft=()):
+    def dma(out, src, rd, wr, nbytes, soft=(), q="s"):
         sem = T.sem["d%d" % cnt["d"]]
         cnt["d"] += 1
-        i = add("s", lambda e: g.sync.dma_start(out, src).then_inc(sem, 16), rd, wr, nbytes / LOCAL_RATE + 60.0, lat=2000.0, kind="d",
-                cls="d", soft=soft)
+        i = add(q, lambda e: Q[e].dma_start(out, src).then_inc(sem, 16), rd, wr, nbytes / LOCAL_RATE + 60.0, lat=2000.0, kind="d", cls="d", soft=soft)
         ops[i]["sem"], ops[i]["val"] = sem, 16
         return i
 
-    def send(dr, out, src, rd, land, nbytes, bulk, after=()):
-        sem = T.sem["r%d" % cnt["r"]]
-        cnt["r"] += 1
-        dst = T.cores[(rank + dr) % N]
-        rid, pid = topo.addr(dst)[:2]
-        mask = topo.mask(core, dst)
-        cnt["sent"] += len(topo.engines(core, dst))
-        i = add("g", lambda e: g.remote_dma(out, src, sem, T.sem.sent, pid, rid, mask), rd, [], SEND, lat=0.0, kind="r", extra=after)
-        before = [i] + (bulks[-1:] if bulk else [])
-        j = add("x", None, [], list(land), nbytes / LINK_RATE, lat=HOP, kind="l", extra=before, cls="l")
-        if bulk:
-            bulks.append(add("x", None, [], [], nbytes / LINK_RATE, lat=0.0, kind="r", extra=before, cls="l"))
-        ops[j]["sem"], ops[j]["val"] = sem, len(topo.engines(T.cores[(rank - dr) % N], core))
-        return i
+    def send(moves, rd, nbytes):
+        def share(a, b, k):
+            es = topo.engines(a, b)
+            n = len(es)
+            return es if len(moves) == 1 else es[:n // 2] if k == 0 else es[n // 2 + (k - 1) * n // 4:n // 2 + k * n // 4]
+        trs, sems = [], []
+        for k, (dr, out, src, land) in enumerate(moves):
+            sems.append(T.sem["r%d" % cnt["r"]])
+            cnt["r"] += 1
+            dst = T.cores[(rank + dr) % N]
+            rid, pid = topo.addr(dst)[:2]
+            es = share(core, dst, k)
+            cnt["sent"] += len(es)
+            trs.append((out, src, sems[k], pid, rid, sum(1 << x for x in es)))
+
+        def fn(e):
+            if len(trs) == 1:
+                o, s, sem, pid, rid, mask = trs[0]
+                return g.remote_dma(o, s, sem, T.sem.sent, pid, rid, mask)
+            return g.remote_dma_fused([RemoteDMATransfer(dst_ids=[DstId(rid=rid, pnc=pid)], dma_engine_mask=mask, remote_sem=sem, src=s, dst=o)
+                                       for o, s, sem, pid, rid, mask in trs], local_sem=T.sem.sent)
+        i = add("g", fn, rd, [], SEND, lat=0.0, kind="r", extra=line[-2:-1], cls="r")
+        before = [i] + line[-1:]
+        for k, (dr, out, src, land) in enumerate(moves):
+            j = add("x", None, [], [land], nbytes * (1 if len(moves) == 1 else 3 if k else 2) / LINK_RATE, lat=HOP, kind="l", extra=before, cls="l")
+            ops[j]["sem"], ops[j]["val"] = sems[k], len(share(T.cores[(rank - dr) % N], core, k))
+        line.extend([i, add("x", None, [], [], nbytes * len(moves) / LINK_RATE, lat=0.0, kind="r", extra=before, cls="l")])
 
     def ind(win, off):
         return win.indirect(off)
@@ -310,13 +365,18 @@ def rank_program(g, core, T, topo):
 
     G8, G16, GW = [[-16, 8]], [[0, 2], [-16, 8]], [[-16, 8], [0, 16]]
     ident = T.iw[:, 0:128]
+    LAST = NT - 1
 
     k = ()
-    for (o, x, wr, nb) in [(T.ivs[:], T.iv[:], "ivs", 19), (T.lbi[:], T.lb[:], "lbi", 14), (T.lvi[:], T.lv[:], "lvi", 14),
+    for (o, x, wr, nb) in [(T.ivs[:, 0:1024], T.iv[:, 0:1024], ("ivs", 0, 1024), 18), (T.lbi[:], T.lb[:], "lbi", 14),
+                           (T.ivs[:, 1024:2048], T.iv[:, 1024:2048], ("ivs", 1024, 2048), 18), (T.lvi[:], T.lv[:], "lvi", 14),
                            (T.bks[:], T.bk[:], "bks", 20), (T.kds[:], T.kd[:], "kds", 20), (T.lfs[:], T.lf[:], "lfs", 20)]:
         k = (dma(o, x, [], [wr], 1 << nb, k),)
 
     cnt["tag"] = "const0"
+    l8, l16 = math.log(8.0), math.log(16.0)
+    iota(row("qrow", 0), [[0, 8], [1, 16]], 0, 0, [blk("qrow", 0)[1]], 128)
+    k = act(row("qrow", 1), row("qrow", 0), AF.Exp, [blk("qrow", 0)[1]], [blk("qrow", 1)[1]], 128, 15 * l16 + 1.0, -l16, 1300.0)
     ms(T.ones[:], 1, ["ones"], 512)
     ms(T.sr[0:1, 0:128:2], 8, [("sr", 0, 128)], 64)
     ms(T.sr[0:1, 1:128:2], -8, [("sr", 0, 128)], 64)
@@ -327,10 +387,9 @@ def rank_program(g, core, T, topo):
     ex = bank(6, 0, 128)
     pe([(ex, row("sr", i), row("sr", i), n == 0, False, 128) for n, i in enumerate((0, 3, 1, 2, 2))]
        + [(ex, T.gh[0:8, 0:128], T.gh[0:8, 128:256], False, True, 128)], ["sr", "gh"], [bk_(6)])
-    l8 = math.log(8.0)
-    act(T.wc[:, 0::2], bank(6, 1, 128, 2), AF.Exp, [bk_(6)], [("wc", 0, 1)], 64, -92.5 * l8, -0.5 * l8, 1300.0)
-    act(T.wc[:, 1::2], bank(6, 0, 128, 2), AF.Exp, [bk_(6)], [("wc", 1, 2)], 64, -92.5 * l8, -0.5 * l8)
-    act(T.wb[:], ex, AF.Exp, [bk_(6)], ["wb"], 128, -92.5 * l8 + math.log(BIG), -0.5 * l8)
+    for m in range(2):
+        act(T.wc[:, m::2], bank(6, 1 - m, 128, 2), AF.Exp, [bk_(6)], [("wc", m, m + 1)], 64, -92.5 * l8, -0.5 * l8, soft=(k,))
+    act(T.wb[:], ex, AF.Exp, [bk_(6)], ["wb"], 128, -92.5 * l8 + math.log(BIG), -0.5 * l8, soft=(k,))
     tt(T.wf[:], T.wc[:, 0::2], T.wc[:, 1::2], ALU.subtract, ["wc"], ["wf"], 128)
     ms(row("neg"), -2.0 ** 24, ["neg"], 128)
     ms(T.rs[:], 0, ["rs"], 512)
@@ -341,6 +400,8 @@ def rank_program(g, core, T, topo):
     for a, st, c in ((4, 8, -256), (5, 8, -131072), (3, 4, 1)):
         ms(T.crow[0:1, a::st], c, ["crow"], 32)
     sel(T.iw[:], T.ones[:, 0:256], [[0, 2], [-1, 128]], ALU.is_equal, 0.0, 0, 1, ["ones"], ["iw"], 256)
+    lin(T.idf[:], ident, 1.0, 0.0, ["iw"], ["idf"], 128)
+    lin(T.ni[:], ident, -1.0, 0.0, ["iw"], ["ni"], 128, half=True)
     for m in range(2):
         src = T.wc[:, m::16]
         sel(T.wr[:, 4 + 8 * m::16], src, [[16, 8]], ALU.is_ge, 0.0, 5, -1, ["wc", "wr"], [("wr%d" % m, 0, 1)], 8)
@@ -348,34 +409,32 @@ def rank_program(g, core, T, topo):
         sel(T.wr[:, 6 + 8 * m::16], src, G8, ALU.is_ge, 0.0, -12, 1, ["wc", "wr"], [("wr%d" % m, 2, 3)], 8)
 
     cnt["tag"] = "lists"
-    cp(T.lbu[:, 0:32], T.lbi[:], ["lbi"], [("lbu", 0, 32)])
-    cp(T.lvu[:], T.lvi[:], ["lvi"], ["lvu"])
+    lin(T.lbu[:, 0:32], T.lbi[:], 1.0, 0.0, ["lbi"], [("lbu", 0, 32)])
+    lin(T.lvu[:], T.lvi[:], 1.0, 0.0, ["lvi"], ["lvu"])
     dma(T.lbd[0:128, :], T.lbu[:, 0:32], [("lbu", 0, 32)], [("lbd", 0, 1)], 1 << 13)
     dma(T.lbd[128:240, :], T.lbu[0:112, 0:32], [("lbu", 0, 32)], [("lbd", 1, 2)], 1 << 13)
-    for t in range(1, NT):
-        send(t, T.lbu[:, 32 * t:32 * t + 32], T.lbd[back(t):back(t) + 128, :], ["lbd"], [("lbu", 32 * t, 32 * t + 32)], 1 << 13, False)
+    send([(t, T.lbu[:, 32 * t:32 * t + 32], T.lbd[back(t):back(t) + 128, :], ("lbu", 32 * t, 32 * t + 32)) for t in range(1, NT)], ["lbd"], 1 << 13)
 
     cnt["tag"] = "canon"
     for hf in range(2):
-        cs = range(8 * hf, 8 * hf + 8)
-        mm = [(bank(hf), row("neg"), T.ones[0:1, :], True, False, 512)]
-        for m in range(2):
-            mm += [(T.p0[:, 64 * c:64 * c + 64], T.ivs[:, 128 * c:128 * c + 128], T.wc[:, m::2], False, m == 1 and c == cs[-1], 64) for c in cs]
-        pe(mm, ["ivs", "wc", "neg", "ones"], [bk_(hf)])
-        pe([(T.p1[:, 64 * c:64 * c + 64], T.ivs[:, 128 * c:128 * c + 128], T.wf[:], True, True, 64) for c in cs], ["ivs", "wf"], [bk_(2 + hf)])
+        cs, iv = range(8 * hf, 8 * hf + 8), ("ivs", 1024 * hf, 1024 * hf + 1024)
+        pe([(bank(hf), row("neg"), T.ones[0:1, :], True, False, 512)], ["neg", "ones"], [bk_(hf)])
+        pe([(T.p0[:, 64 * c:64 * c + 64], T.ivs[:, 128 * c:128 * c + 128], T.wc[:, m::2], False, m == 1 and c == cs[-1], 64) for m in range(2) for c in cs],
+           [iv, "wc"], [bk_(hf)])
+        pe([(T.p1[:, 64 * c:64 * c + 64], T.ivs[:, 128 * c:128 * c + 128], T.wf[:], True, True, 64) for c in cs], [iv, "wf"], [bk_(2 + hf)])
     for b in range(4):
         pe([(bank(4 + b), row("crow"), T.ones[0:1, :], True, False, 512), (bank(4 + b), T.wr[:], T.ivs[:, 512 * b:512 * b + 512], False, False, 512)],
-           ["crow", "ones", "wr", "wr0", "wr1", "ivs"], [bk_(4 + b)])
+           ["crow", "ones", "wr", "wr0", "wr1", ("ivs", 512 * b, 512 * b + 512)], [bk_(4 + b)])
 
-    def split(src, sn, hf, r0):
+    def split(src, sn, hf, r0, b):
         xa, k = 1024 * hf + r0, 2 * hf + r0 // 8
         x = [T.xt[:, xa + i:1024 * hf + 1024:16] for i in range(3)]
         xn = [("xt%d" % i, k, k + 1) for i in range(3)]
-        r, rn = T.xr[:, 64 * k:64 * k + 64], ("xr", k, k + 1)
+        r = bank(b, 0, 64)
         lin(x[0], src, 1.0, 0.0, [sn, "xt"], [xn[0]])
-        tt(r, src, x[0], ALU.subtract, [sn, xn[0]], [rn], 128)
-        lin(x[1], r, 1.0, 0.0, [rn, "xt"], [xn[1]])
-        tt(x[2], r, x[1], ALU.subtract, [rn, xn[1], "xt"], [xn[2]], 128)
+        pe([(r, T.idf[:], src, True, False, 256), (r, T.ni[:], x[0], False, True, 64)], ["idf", "ni", sn, xn[0]], [bk_(b)])
+        lin(x[1], r, 1.0, 0.0, [bk_(b), "xt"], [xn[1]])
+        tt(x[2], r, x[1], ALU.subtract, [bk_(b), xn[1], "xt"], [xn[2]])
     for hf in range(2):
         a, b = 512 * hf, 512 * hf + 512
         sb, scr, eqr = ("sb", a, b), ("sc", a, b), ("eq", a, b)
@@ -390,8 +449,8 @@ def rank_program(g, core, T, topo):
         add("v", cmp8, [bk_(hf), scr], [eqr], 8 * (FIX + 64 * CYC))
         tt(T.eq[:, a:b], bank(2 + hf), T.eq[:, a:b], ALU.mult, [bk_(2 + hf), eqr], [eqr], 512)
         scan(T.sb[:, a:b], T.rs[:], T.eq[:, a:b], 0.0, ALU.add, ALU.max, ["rs", eqr], [sb], 512)
-        split(T.sc[:, a + 7:b:8], scr, hf, 0)
-        split(T.sb[:, a + 7:b:8], sb, hf, 8)
+        split(T.sc[:, a + 7:b:8], scr, hf, 0, hf)
+        split(T.sb[:, a + 7:b:8], sb, hf, 8, 2 + hf)
         for u in range(2):
             bn, lo = 4 + 2 * hf + u, 1024 * hf + 512 * u
             pe([(bank(bn, 128 * k, 128 * k + 128), T.xt[:, lo + 128 * k:lo + 128 * k + 128], ident, False, k == 3, 128) for k in range(4)],
@@ -405,20 +464,17 @@ def rank_program(g, core, T, topo):
     lin(T.rn[:], T.rt[:, 0::16], -1.0, 0.0, ["rt"], ["rn"])
     band(T.bm[:], T.ones[:, 0:128], GW, 0, 15, ["ones"], "bm", 128)
     lin(T.tr[:], ident, -4096.0, 0.0, ["iw"], ["tr"], 128, half=True)
-    gcp(T.i16[:], ident, ["iw"], ["i16"], 128)
+    lin(T.i16[:], ident, 1.0, 0.0, ["iw"], ["i16"], 128, half=True)
     gfill(T.dg[:], 0, ["dg"], 144)
     gcp(T.dg[:, 15:143:16], T.bm[:, 0::16], ["bm", "dg"], ["dg"], 8)
-    gfill(T.k15[:], 0, ["k15"], 512, "ag")
-    gfill(T.k15[:, 15::16], 1, ["k15"], 32, "ag")
-    gfill(T.zp[:, 0:1], 1, [("zp", 0, 1)], 1, "ag")
+    gfill(T.k15[:], 0, ["k15"], 512)
+    gfill(T.k15[:, 15::16], 1, ["k15"], 32)
+    gfill(T.zp[:, 0:1], 1, [("zp", 0, 1)], 1)
     for i in range(3):
         lin(blk("isc", i)[0], ident, float(16 ** (i + 1)), 0.0, ["iw"], [blk("isc", i)[1]], 128, half=True)
     cnt["tag"] = "const2"
     for i in range(4):
         iota(row("br", i), [[0, 64 >> i], [1, 2], [0, 1 << i]], 0, 0, [blk("br", i)[1]], 128)
-    iota(row("qrow", 0), [[0, 8], [1, 16]], 0, 0, [blk("qrow", 0)[1]], 128)
-    l16 = math.log(16.0)
-    act(row("qrow", 1), row("qrow", 0), AF.Exp, [blk("qrow", 0)[1]], [blk("qrow", 1)[1]], 128, 15 * l16, -l16)
     hx = bank(3, 0, 128)
     pe([(hx, row("br", i), row("br", i), i == 0, i == 3, 128) for i in range(4)]
        + [(bank(3, 128, 129), row("qrow", 1), T.ones[0:1, 0:1], True, True, 64)], ["br", "qrow", "ones"], [bk_(3)])
@@ -427,11 +483,11 @@ def rank_program(g, core, T, topo):
     act(hx, hx, AF.Abs, [], [bk_(3)], 128, -1.0)
     lin(T.h0[:], hx, 2.0, -1.0, [bk_(3)], ["h0"], 128)
     band(T.h0[:], T.h0[:], GW, 0, 15, ["h0"], "h0", 128)
-    gcp(T.h16[:], T.h0[:], ["h0"], ["h16"], 128)
+    lin(T.h16[:], T.h0[:], 1.0, 0.0, ["h0"], ["h16"], 128, half=True)
     lin(T.hn[:], T.h0[:], -1.0, 0.0, ["h0"], ["hn"], 128)
     lin(T.ge[:], T.h0[:], T.qc[:, 0:1], 0.0, ["h0", "qc"], ["ge"], 128)
     for nm, r0, sc in (("ts", 4, 1.0), ("tb", 12, BIG)):
-        gfill(T[nm][:], -sc, [nm], 128, "ag")
+        gfill(T[nm][:], -sc, [nm], 128)
         band(T[nm][:], T[nm][:], GW, r0, r0 + 2, [nm], nm, 128)
         put(T[nm][:], GW, 3, -256 * sc, nm, 128)
         put(T[nm][:], GW, 7, -131072 * sc, nm, 128)
@@ -448,29 +504,30 @@ def rank_program(g, core, T, topo):
         gcp(T.gm[:, c::16], T.gm[:, 0::16], ["gm"], ["gm"], 8)
     sel(T.tp[:], T.bm[:], [[1, 128]], ALU.is_gt, 0.0, 0, -1, ["bm"], ["tp"], 128)
     iota(T.jc[:], [[16, 32]], 512, 1, ["jc"], 32)
-    gcp(T.jh[:], T.jc[:], ["jc"], ["jh"], 32)
-    iota(T.jn[:], [[-16, 32]], -512, -1, ["jn"], 32)
     iota(T.jt[:], [[1, 32], [0, 16]], 0, 0, ["jt"], 512)
     iota(T.jrow[:], [[0, 32], [1, 16]], 0, 0, ["jrow"], 512)
     dma(T.jrow[0::16, :], T.jt[0::16, :], ["jt"], ["jrow"], 1 << 13)
-    for nm in ("dl", "dm", "ra", "rb", "rc", "oc", "krow"):
-        gfill(T[nm][:], 0, [nm], SCRATCH[nm][1][1], "g" if nm == "rb" else "ag")
-    gfill(T.ln[:, 0:CAP], 0, ["ln"], CAP, "ag")
+    for nm in ("dl", "dm"):
+        gfill(T[nm][:], 0, [nm], SCRATCH[nm][1][1])
+    gfill(T.ln[:, 0:CAP], 0, ["ln"], CAP)
     for a in range(CAP, WIN, 512):
         b = min(a + 512, WIN)
-        gfill(T.rv[:, a:b], 0, [("rv", a, b)], b - a, "ag")
-    gfill(T.ss[:, 0:1], 0, [("ss", 0, 1)], 1, "ag")
+        gfill(T.rv[:, a:b], 0, [("rv", a, b)], b - a)
+    gfill(T.ss[:, 0:1], 0, [("ss", 0, 1)], 1)
     put(T.dl[:, 15:143:16], G8, 0, 16, "dl", 8)
     put(T.dl[:, 15:143:16], G8, 1, 1, "dl", 8)
     put(T.dm[:, 15::16], G16, 0, -1, "dm", 16)
+    cnt["tag"] = "const4"
+    for nm in ("ra", "rb", "rc", "oc", "krow"):
+        gfill(T[nm][:], 0, [nm], SCRATCH[nm][1][1])
     band(T.rb[:, 1:80:5], T.ones[:, 0:16], G16, 0, 15, ["ones", "rb"], "rb", 16)
     for nm, f, a, c in [("ra", 0, 0, rank + 1), ("ra", 1, 0, 2048), ("ra", 1, 5, -1), ("ra", 2, 0, 16), ("ra", 3, 0, 15), ("ra", 4, 0, 1),
                         ("ra", 4, 3, -2), ("rc", 1, 0, -2048), ("rc", 2, 0, -8.5)] + \
             [("ra", 3, b, -b) for b in (1, 2, 4, 8)] + [("rc", 2, b, -0.5 * b) for b in (1, 2, 4, 8)]:
         put(T[nm][:, f:80:5], G16, a, c, nm, 16)
-    for nm, f, c in (("krow", 4, 1), ("oc", 0, -1), ("oc", 4, -4)):
+    for nm, f, c in (("krow", 4, 1), ("oc", 0, -1), ("oc", 4, -NT)):
         for h in range(2):
-            gfill(T[nm][:, 64 * h + f:64 * h + 40:5], c, [nm], 8, "ag")
+            gfill(T[nm][:, 64 * h + f:64 * h + 40:5], c, [nm], 8)
 
     cnt["tag"] = "targets"
     lin(T.tg[:, 0:512], ind(T.ct[:], T.lvu[:]), 1.0, 0.0, ["ct", "lvu"], [("tg", 0, 512)], GA(512))
@@ -478,15 +535,15 @@ def rank_program(g, core, T, topo):
         dma(T.tgd[0:128, 128 * k:128 * k + 128], T.tg[k::4, 0:512], [("tg", 0, 512)], [("tgd", k, k + 1)], 1 << 15)
         dma(T.tgd[128:240, 128 * k:128 * k + 128], T.tg[k:112:4, 0:512], [("tg", 0, 512)], [("tgd", 3 + k, 4 + k)], 1 << 15)
     dma(T.tg[3::4, 512:2048], T.ct[3::4, 0:1536], ["ct"], ["tgone"], 3 << 15)
+    send([(t, T.tl[:, 384 * t - 384:384 * t], T.tgd[back(t):back(t) + 128, :], ("tl", t, t + 1)) for t in range(1, NT)], ["tgd"], 3 << 15)
     for t in range(1, NT):
-        a, c0 = 384 * (t - 1), 512 * t
-        send(t, T.tl[:, a:a + 384], T.tgd[back(t):back(t) + 128, :], ["tgd"], [("tl", t, t + 1)], 3 << 15, True)
         for k in range(3):
-            dma(T.tg[k::4, c0:c0 + 512], T.tl[:, a + 128 * k:a + 128 * k + 128], [("tl", t, t + 1)], [("tg%d" % t, k, k + 1)], 1 << 15)
+            a = 384 * (t - 1) + 128 * k
+            dma(T.tg[k::4, 512 * t:512 * t + 512], T.tl[:, a:a + 128], [("tl", t, t + 1)], [("tg%d" % t, k, k + 1)], 1 << 15)
     cnt["tag"] = "words"
-    cp(T.kau[:], ind(T.kds[:], T.lvu[:]), ["kds", "lvu"], ["kau"], GA(512))
-    for q in range(8):
-        lin(T.ga[:, 1024 * q:1024 * q + 1024], ind(T.lfs[:], T.kau[:, 64 * q:64 * q + 64]), 1.0, 0.0, ["lfs", "kau"], [("ga", q, q + 1)], GA(1024))
+    lin(T.kau[:], ind(T.kds[:], T.lvu[:]), 1.0, 0.0, ["kds", "lvu"], ["kau"], GA(512))
+    for a in range(0, 8192, GAP):
+        lin(T.ga[:, a:a + GAP], ind(T.lfs[:], T.kau[:, a // 16:(a + GAP) // 16]), 1.0, 0.0, ["lfs", "kau"], [("ga", a, a + GAP)], GA(GAP))
     for hf in range(2):
         for ep in range(2):
             mm = []
@@ -495,74 +552,83 @@ def rank_program(g, core, T, topo):
                     w = ident if i == 0 else blk("isc", i - 1)[0]
                     mm.append((bank(4 + e, 256 * hf, 256 * hf + 256), w, T.ga[:, 4096 * hf + 4 * e + i:4096 * hf + 4096:16],
                                i == 0, i == 3, 256))
-            pe(mm, ["iw", "isc", ("ga", 4 * hf, 4 * hf + 4)], [bk_(4 + 2 * ep), bk_(5 + 2 * ep)])
+            pe(mm, ["iw", "isc", ("ga", 4096 * hf, 4096 * hf + 4096)], [bk_(4 + 2 * ep), bk_(5 + 2 * ep)])
+    wd = 2048 // NW
     for e in range(4):
         a = 512 * e
-        lin(T.awf[:, a:a + 512], bank(4 + e), 1.0, WOFF, [bk_(4 + e)], [("awf", a, a + 512)], 512)
-        gcp(T.awu[:, a:a + 512], T.awf[:, a:a + 512], [("awf", a, a + 512)], [("awu", a, a + 512)], 512)
-        dma(T.awd[0:128, a:a + 512], T.awu[:, a:a + 512], [("awu", a, a + 512)], [("awd", e, e + 1)], 1 << 17)
-        dma(T.awd[128:240, a:a + 512], T.awu[0:112, a:a + 512], [("awu", a, a + 512)], [("awd", 4 + e, 5 + e)], 1 << 17)
+        lin(T.awu[:, a:a + 512], bank(4 + e), 1.0, WOFF, [bk_(4 + e)], [("awu", a, a + 512)], 512)
+    for e in range(NW):
+        a, r0 = wd * e, 256 * e
+        dma(T.awd[r0:r0 + 128, :], T.awu[:, a:a + wd], [("awu", a, a + wd)], [("awd", 2 * e, 2 * e + 1)], 256 * wd)
+        dma(T.awd[r0 + 128:r0 + 240, :], T.awu[0:112, a:a + wd], [("awu", a, a + wd)], [("awd", 2 * e + 1, 2 * e + 2)], 224 * wd)
 
-    def words(t, after):
-        send(t, T.awu[:, 2048 * t:2048 * t + 2048], T.awd[back(t):back(t) + 128, :], ["awd"], [("awu", 2048 * t, 2048 * t + 2048)],
-             1 << 19, True, after)
-    words(1, ())
+    def words(t):
+        for e in range(NW):
+            a, r0 = 2048 * t + wd * e, 256 * e + back(t)
+            send([(t, T.awu[:, a:a + wd], T.awd[r0:r0 + 128, :], ("awu", a, a + wd))], [("awd", 2 * e, 2 * e + 2)], 256 * wd)
+    words(1)
 
     def claims(t):
-        l0, l1, c0, u = 32 * t, 32 * t + 32, 512 * t, t % 2
+        c0, u, n = 512 * t, t % 2, L // PARTS[t]
         cnt["tag"] = "claim%d" % t
-        tg = T.tg[:, c0:c0 + 512]
         tgr = [("tg", c0, c0 + 512), "tg%d" % t] + (["tgone"] if t else [])
         gc, gn = T["gc%d" % u], "gc%d" % u
-        wh, whr = T.wh[:, 512 * u:512 * u + 512], ("wh", u, u + 1)
-        cc, ccr = T.cc[:, c0:c0 + 512], ("cc", t, t + 1)
-        chi, chr_ = T.chi[:, c0:c0 + 512], ("chi", t, t + 1)
-        cp(T.wu[:, c0:c0 + 512], ind(T.bks[:], T.lbu[:, l0:l1]), ["bks", ("lbu", l0, l1)], [("wu", t, t + 1)], GA(512))
-        gcp(wh, T.wu[:, c0:c0 + 512], [("wu", t, t + 1)], [whr], 512)
+        lin(T.wu[:, c0:c0 + 512], ind(T.bks[:], T.lbu[:, 32 * t:32 * t + 32]), 1.0, 0.0, ["bks", ("lbu", 32 * t, 32 * t + 32)], [("wu", t, t + 1)], GA(512))
+        gcp(T.wh[:, 512 * u:512 * u + 512], T.wu[:, c0:c0 + 512], [("wu", t, t + 1)], [("wh", u, u + 1)], 512)
         w = PIECE[t]
         for a in range(0, 8192, w):
             lin(gc[:, a:a + w], ind(T.ct[:], T.wu[:, c0 + a // 16:c0 + (a + w) // 16]), 1.0, 0.0, ["ct", ("wu", t, t + 1)], [(gn, a, a + w)], GA(w))
-        for c in range(4):
-            o, x = 128 * c, T.tg[:, c0 + 128 * c:c0 + 128 * c + 128]
-            mm = [(bank(u, o, o + 128), x, T.rt[:, 0:128], True, False, 128)]
-            for h in range(2):
-                mm += [(bank(u, o + k, o + 128, 16), gc[:, 2048 * c + k:2048 * c + 2048:16], T.rn[:, 8 * h:8 * h + 8], False, False, 8) for k in range(16)]
-            mm.append((bank(u, o, o + 128), x, T.rt[:, 128:256], False, True, 128))
-            pe(mm, ["rt", "rn", (gn, 2048 * c, 2048 * c + 2048)] + tgr, [bk_(u)])
-        nonzero(T.nz[:], bank(u), [bk_(u)], ["nz"], 512)
-        scan(T.zp[:, 1:513], T.nz[:], T.k15[:], 1.0, ALU.min, ALU.max, ["nz", "k15"], [("zp", 1, 513)], 256)
-        mm = [(bank(3), T.i16[:], wh, True, False, 512)]
-        for c in range(4):
-            o = 128 * c
-            mm.append((bank(3, o, o + 128), T.nz[:, o:o + 128], T.tr[:], False, False, 128))
-            mm.append((bank(3, o, o + 128), T.zp[:, o:o + 128], blk("isc", 2)[0], False, c == 3, 128))
-        pe(mm, ["i16", whr, "tr", "isc", "nz", "zp"], [bk_(3)])
-        ts(cc, bank(3), -4095.0, 0.0, ALU.add, ALU.max, [bk_(3)], [ccr], 512)
-        pe([(bank(2, 0, 32), T.dg[:, 15 - i:143 - i], T.cc[:, c0 + i:c0 + 512:16], i == 0, i == 15, 32) for i in range(16)], ["dg", ccr], [bk_(2)])
-        ts(T.wl[:, l0:l1], bank(2, 0, 32), -1.0, None, ALU.add, None, [bk_(2)], [("wl", l0, l1)])
-        positive(T.cl[:, l0:l1], bank(2, 0, 32), [bk_(2)], [("cl", l0, l1)], 64)
-        cnt["tag"] = "shift%d" % t
-        wl, wlr = T.wl[:, l0:l1], ("wl", l0, l1)
-        lin(T.gi[:], ind(T.ivs[:], wl), 1.0, 0.0, ["ivs", wlr], ["gi"], GA(512))
-        ts(T.gk[:], ind(T.kds[:], wl), -2048.0, None, ALU.add, None, ["kds", wlr], ["gk"], GA(512))
-        pe([(bank(3), T.tb[:], tg, True, False, 512), (bank(3), T.wb[:], T.gi[:], False, False, 512),
-            (bank(3), T.wc[:], T.gi[:], False, False, 512), (bank(3), T.ts[:], tg, False, True, 512)],
-           ["tb", "wb", "wc", "ts", "gi"] + tgr, [bk_(3)])
-        ts(T.fit[:], bank(3), 0.0, None, ALU.is_equal, None, [bk_(3)], ["fit"], 512)
-        pe([(bank(2), T.h16[:], T.gk[:], True, True, 512)], ["h16", "gk"], [bk_(2)])
-        pe([(bank(3), T.ge[:], T.fit[:], True, True, 512)], ["ge", "fit"], [bk_(3)])
-        act(chi, bank(3), AF.Sign, [bk_(3)], [chr_], 512)
-        tt(T.kp[:], bank(2), chi, ALU.mult, [bk_(2), chr_], ["kp"], 512)
-        pe([(bank(2), T.hn[:], T.kp[:], True, True, 2048)], ["hn", "kp"], [bk_(2)])
-        lin(T.kb[:, c0:c0 + 512], bank(2), -1.0 / 16, 2048.0, [bk_(2)], [("kb", t, t + 1)], 512)
+        for p in range(PARTS[t]):
+            x0, x1 = n * p, n * p + n
+            bd, ba, bb = (u, 3, 2) if n == L else (p, 3 - p, p)
+            l0, l1 = 32 * t + x0 // 16, 32 * t + x1 // 16
+
+            def part(nm, o=0):
+                return T[nm][:, o + x0:o + x1], (nm, o + x0, o + x1)
+            cnt["tag"] = "claim%d" % t
+            for x in range(x0, x1, 128):
+                o, tgx = x - x0, T.tg[:, c0 + x:c0 + x + 128]
+                mm = [(bank(bd, o, o + 128), tgx, T.rt[:, 0:128], True, False, 128)]
+                for h in range(2):
+                    mm += [(bank(bd, o + k, o + 128, 16), gc[:, 16 * x + k:16 * x + 2048:16], T.rn[:, 8 * h:8 * h + 8], False, False, 8) for k in range(16)]
+                mm.append((bank(bd, o, o + 128), tgx, T.rt[:, 128:256], False, True, 128))
+                pe(mm, ["rt", "rn", (gn, 16 * x, 16 * x + 2048)] + tgr, [bk_(bd)])
+            (nz, nzr), (zp, zpr), (cc, ccr), (chi, chr_) = part("nz"), part("zp", 1), part("cc", c0), part("chi", c0)
+            nonzero(nz, bank(bd, 0, n), [bk_(bd)], [nzr], n)
+            scan(zp, nz, T.k15[:, 0:n], 1.0, ALU.min, ALU.max, [nzr, "k15"], [zpr], n / 2)
+            mm = [(bank(ba, 0, n), T.i16[:], part("wh", 512 * u)[0], True, False, n)]
+            for x in range(x0, x1, 128):
+                mm.append((bank(ba, x - x0, x - x0 + 128), T.nz[:, x:x + 128], T.tr[:], False, False, 128))
+                mm.append((bank(ba, x - x0, x - x0 + 128), T.zp[:, x:x + 128], blk("isc", 2)[0], False, x + 128 == x1, 128))
+            pe(mm, ["i16", ("wh", u, u + 1), "tr", "isc", nzr, ("zp", x0, x1)], [bk_(ba)])
+            either(cc, bank(ba, 0, n), (-4095.0, 0.0, ALU.add, ALU.max), (AF.Relu, -4095.0, 1.0), [bk_(ba)], [ccr], n)
+            lst = bank(bb, 0, n // 16)
+            pe([(lst, T.dg[:, 15 - i:143 - i], T.cc[:, c0 + x0 + i:c0 + x1:16], i == 0, i == 15, 32) for i in range(16)], ["dg", ccr], [bk_(bb)])
+            wl, wlr = T.wl[:, l0:l1], ("wl", l0, l1)
+            lin(wl, lst, 1.0, -1.0, [bk_(bb)], [wlr])
+            positive(T.cl[:, l0:l1], lst, [bk_(bb)], [("cl", l0, l1)], 64)
+            cnt["tag"] = "shift%d" % t
+            (gi, gir), (gk, gkr), (fit, fir), (kp, kpr), (kb, kbr), tg = part("gi"), part("gk"), part("fit"), part("kp"), part("kb", c0), part("tg", c0)[0]
+            A, B = bank(ba, 0, n), bank(bb, 0, n)
+            lin(gi, ind(T.ivs[:], wl), 1.0, 0.0, ["ivs", wlr], [gir], GA(n))
+            lin(gk, ind(T.kds[:], wl), 1.0, -2048.0, ["kds", wlr], [gkr], GA(n))
+            pe([(A, T.tb[:], tg, True, False, n)], ["tb"] + tgr, [bk_(ba)])
+            pe([(A, T.wb[:], gi, False, False, n), (A, T.wc[:], gi, False, False, n), (A, T.ts[:], tg, False, True, n)],
+               ["wb", "wc", "ts", gir] + tgr, [bk_(ba)])
+            V(lambda q, fit=fit, A=A: q.tensor_scalar(fit, A, 0.0, None, ALU.is_equal), [bk_(ba)], [fir], n)
+            pe([(B, T.h16[:], gk, True, True, n)], ["h16", gkr], [bk_(bb)])
+            pe([(A, T.ge[:], fit, True, True, n)], ["ge", fir], [bk_(ba)])
+            either(chi, A, (-1.0, 1.0, ALU.max, ALU.min), (AF.Sign, 0.0, 1.0), [bk_(ba)], [chr_], n)
+            tt(kp, B, chi, ALU.mult, [bk_(bb), chr_], [kpr], n)
+            pe([(B, T.hn[:], kp, True, True, 4 * n)], ["hn", kpr], [bk_(bb)])
+            lin(kb, B, -1.0 / 16, 2048.0, [bk_(bb)], [kbr], n)
 
     def tests(t):
         l0, l1, u, c0 = 32 * t, 32 * t + 32, t % 2, 512 * t
         cnt["tag"] = "conv%d" % t
-        if t:
-            for e in range(4):
-                a, o = 2048 * t + 512 * e, 2048 * u + 512 * e
-                gcp(T.awf[:, o:o + 512], T.awu[:, a:a + 512], [("awu", a, a + 512)], [("awf", o, o + 512)], 512)
+        for e in range(4):
+            a, o = 2048 * t + 512 * e, 2048 * u + 512 * e
+            gcp(T.awf[:, o:o + 512], T.awu[:, a:a + 512], [("awu", a, a + 512)], [("awf", o, o + 512)], 512)
         cnt["tag"] = "test%d" % t
         if t == 0:
             F, fr = T.cl[:, 0:32], ("cl", 0, 32)
@@ -572,37 +638,37 @@ def rank_program(g, core, T, topo):
             live, lr = T.lin[:, l0:l1], ("lin", l0, l1)
             tt(F, live, T.cl[:, l0:l1], ALU.mult, [lr, ("cl", l0, l1)], [fr])
         scan(T.ss[:, 1:33], T.ones[:, 0:32], F, 0.0, ALU.mult, ALU.add, ["ones", fr], [("ss", 1, 33)])
-        tt(T.gd[:], F, T.jn[:], ALU.mult, [fr, "jn"], ["gd"])
         o7 = bank(7, 0, 32)
-        pe([(o7, T.i16[:], T.jh[:], True, False, 32), (o7, T.tp[:], F, False, False, 32), (o7, T.bm[:], T.ss[:, 0:32], False, False, 32),
-            (o7, T.i16[:], T.gd[:], False, True, 32)], ["i16", "jh", "tp", "bm", "ss", "gd", fr], [bk_(7)])
-        cp(T.ofu[:], o7, [bk_(7)], ["ofu"])
-        cp(ind(T.ln[:], T.ofu[:]), T.jrow[:], ["ofu", "jrow"], ["ln"], ("s", 512))
+        pe([(o7, blk("isc", 2)[0], T.ones[:, 0:32], True, False, 32), (o7, T.tp[:], F, False, False, 32), (o7, T.tr[:], F, False, False, 32),
+            (o7, T.bm[:], T.ss[:, 0:32], False, True, 32)], ["isc", "ones", "tp", "bm", "ss", "tr", fr], [bk_(7)])
+        tt(T.ofu[:], o7, T.jc[:], ALU.min, [bk_(7), "jc"], ["ofu"])
+        V(lambda q: q.tensor_copy(ind(T.ln[:], T.ofu[:]), T.jrow[:]), ["ofu", "jrow"], ["ln"], ("s", 512))
         pe([(bank(7, 0, 12), T.dl[:, 15 - i:143 - i], T.ln[:, i:CAP:16], i == 0, i == 15, 12) for i in range(16)], ["dl", "ln"], [bk_(7)])
         ll = T.lnu[:, 0:12]
-        cp(ll, bank(7, 0, 12), [bk_(7)], ["lnu"])
-        cp(T.kbu[:], ind(T.kb[:, c0:c0 + 512], ll), [("kb", t, t + 1), "lnu"], ["kbu"], GA(CAP))
+        lin(ll, bank(7, 0, 12), 1.0, 0.0, [bk_(7)], ["lnu"])
+        lin(T.kbu[:], ind(T.kb[:, c0:c0 + 512], ll), 1.0, 0.0, [("kb", c0, c0 + 512), "lnu"], ["kbu"], GA(CAP))
         for e in range(4):
             o = 2048 * u + 512 * e
             lin(T.ac[:, CAP * e:CAP * e + CAP], ind(T.awf[:, o:o + 512], ll), 1.0, -WOFF, [("awf", o, o + 512), "lnu"], [("ac", e, e + 1)], GA(CAP))
-        for q in range(4):
-            lin(T.gb[:, 768 * q:768 * q + 768], ind(T.lfs[:], T.kbu[:, 48 * q:48 * q + 48]), 1.0, 0.0, ["lfs", "kbu"], [("gb", q, q + 1)], GA(768))
-        for hf in range(2):
-            o = 384 * hf
-            pe([(bank(6 + hf, 96 * e, 96 * e + 96), T.hn[:], T.ac[:, CAP * e + 96 * hf:CAP * e + 96 * hf + 96], True, True, 384) for e in range(4)],
-               ["hn", "ac"], [bk_(6 + hf)])
+        steps = [(0, STEP), (STEP, CAP)]
+        for hf, (x0, x1) in enumerate(steps):
+            n, o = x1 - x0, 4 * x0
+            for a in (x0, x0 + n // 2):
+                lin(T.gb[:, 16 * a:16 * a + 8 * n], ind(T.lfs[:], T.kbu[:, a:a + n // 2]), 1.0, 0.0, ["lfs", "kbu"], [("gb", a, a + n // 2)], GA(8 * n))
+            pe([(bank(6 + hf, n * e, n * e + n), T.hn[:], T.ac[:, CAP * e + x0:CAP * e + x1], True, True, 4 * n) for e in range(4)], ["hn", "ac"], [bk_(6 + hf)])
             for s in range(2):
-                lin(T.a2[:, 768 * s + o:768 * s + o + 384], bank(6 + hf, 0, 384), 2.0 * s - 1.0, 0.0, [bk_(6 + hf)], [("a2", 2 * s + hf, 2 * s + hf + 1)], 384)
-        for hf in range(2):
-            o = 384 * hf
-            pe([(bank(4 + hf, 96 * e, 96 * e + 96), blk("hs", i)[0], T.gb[:, 1536 * hf + 4 * e + i:1536 * hf + 1536:16], i == 0, i == 3, 96)
-                for e in range(4) for i in range(4)], ["hs", ("gb", 2 * hf, 2 * hf + 2)], [bk_(4 + hf)])
+                lin(T.a2[:, 768 * s + o:768 * s + o + 4 * n], bank(6 + hf, 0, 4 * n), 2.0 * s - 1.0, 0.0, [bk_(6 + hf)],
+                    [("a2", 2 * s + hf, 2 * s + hf + 1)], 4 * n)
+        for hf, (x0, x1) in enumerate(steps):
+            n, o = x1 - x0, 4 * x0
+            pe([(bank(4 + hf, n * e, n * e + n), blk("hs", i)[0], T.gb[:, 16 * x0 + 4 * e + i:16 * x1:16], i == 0, i == 3, n)
+                for e in range(4) for i in range(4)], ["hs", ("gb", x0, x1)], [bk_(4 + hf)])
             for s, nm in enumerate(("uu", "vv")):
-                tt(T[nm][:, o:o + 384], bank(4 + hf, 0, 384), T.a2[:, 768 * s + o:768 * s + o + 384], ALU.not_equal,
-                   [bk_(4 + hf), ("a2", 2 * s + hf, 2 * s + hf + 1)], [(nm, hf, hf + 1)], 384)
+                tt(T[nm][:, o:o + 4 * n], bank(4 + hf, 0, 4 * n), T.a2[:, 768 * s + o:768 * s + o + 4 * n], ALU.not_equal,
+                   [bk_(4 + hf), ("a2", 2 * s + hf, 2 * s + hf + 1)], [(nm, hf, hf + 1)], 4 * n)
             for k, nm in enumerate(("uu", "vv")):
-                pe([(bank(6 + s, 96 * hf, 96 * hf + 96), T.mi[:] if s != k else T.pl[:], T[nm][:, o + 96 * e:o + 96 * e + 96], k == 0 and e == 0,
-                     k == 1 and e == 3, 96) for s in range(2) for e in range(4)], ["pl", "mi", (nm, hf, hf + 1)], [bk_(6), bk_(7)])
+                pe([(bank(6 + s, x0, x1), T.mi[:] if s != k else T.pl[:], T[nm][:, o + n * e:o + n * e + n], k == 0 and e == 0, k == 1 and e == 3, n)
+                    for s in range(2) for e in range(4)], ["pl", "mi", (nm, hf, hf + 1)], [bk_(6), bk_(7)])
         for s in range(2):
             iszero(T.fl[:, CAP * s:CAP * s + CAP], bank(6 + s, 0, CAP), [bk_(6 + s)], [("fl", s, s + 1)], CAP)
         pe([(bank(4, 0, CAP), T.gp[:], T.fl[:, 0:CAP], True, False, CAP), (bank(4, 0, CAP), T.gm[:], T.fl[:, CAP:384], False, True, CAP)],
@@ -610,7 +676,7 @@ def rank_program(g, core, T, topo):
         positive(T.rv[:, 0:CAP], bank(4, 0, CAP), [bk_(4)], [("rv", 0, CAP)], CAP)
         for h in range(2):
             relu(T.ev[:, 256 * h:256 * h + 256], ind(T.rv[:], T.ofu[:, 16 * h:16 * h + 16]), ["rv", "ofu"], [("ev", h, h + 1)], GA(256))
-        if t < NT - 1:
+        if t < LAST:
             rho = 16 * (SH[t + 1] - SH[t])
             mm = [(o7, T.iw[:, (-rho) % 128:(-rho) % 128 + 128], live, True, False, 32)]
             for i in range(16):
@@ -618,36 +684,35 @@ def rank_program(g, core, T, topo):
                 mm.append((o7, T.dm[:, s0:s0 + 128], T.ev[:, i:512:16], False, i == 15, 32))
             pe(mm, ["iw", "dm", lr, "ev"], [bk_(7)])
             lin(T.lout[:, l0:l1], o7, 1.0, 0.0, [bk_(7)], [("lout", l0, l1)])
-            k = send(1, T.lin[:, l1:l1 + 32], T.lout[:, l0:l1], [("lout", l0, l1)], [("lin", l1, l1 + 32)], 1 << 13, False)
+            send([(1, T.lin[:, l1:l1 + 32], T.lout[:, l0:l1], ("lin", l1, l1 + 32))], [("lout", l0, l1)], 1 << 13)
             if t + 2 < NT:
-                words(t + 2, [k])
+                words(t + 2)
         cnt["tag"] = "res%d" % t
-        rb, s5 = (5 if t < NT - 1 else 2), 5 * SH[t]
+        rb, s5, r0 = (5 if t < LAST else 2), 5 * SH[t], 256 * t
         mm = [(bank(rb, 0, 256), row("krow"), T.ones[0:1, 0:256], True, False, 256)]
         for h in range(2):
             o = bank(rb, 0, 256, 1, 64 * h, 64 * h + 64)
             mm.append((o, T.rb[:, s5:s5 + 64], T.cc[:, c0 + 256 * h:c0 + 256 * h + 256], False, False, 256))
             mm.append((o, T.rc[:, s5:s5 + 64], T.chi[:, c0 + 256 * h:c0 + 256 * h + 256], False, False, 256))
-        pe(mm, ["krow", "ones", "rb", "rc", ("cc", t, t + 1), ("chi", t, t + 1)], [bk_(rb)])
+        pe(mm, ["krow", "ones", "rb", "rc", ("cc", c0, c0 + 512), ("chi", c0, c0 + 512)], [bk_(rb)])
         pe([(bank(rb, 0, 256, 1, 64 * h, 64 * h + 64), T.ra[:, s5:s5 + 64], T.ev[:, 256 * h:256 * h + 256], False, True, 256) for h in range(2)],
            ["ra", "ev"], [bk_(rb)])
-        r0 = 256 * t
-        ts((T.ro if t else T.ri)[:, r0:r0 + 256], bank(rb, 0, 256), 0.0, None, ALU.max, None, [bk_(rb)], [("ro" if t else "ri", t, t + 1)], 256)
+        relu((T.ro if t else T.ri)[:, r0:r0 + 256], bank(rb, 0, 256), [bk_(rb)], [("ro" if t else "ri", t, t + 1)], 256)
         if t:
-            send(-t, T.ri[:, r0:r0 + 256], T.ro[:, r0:r0 + 256], [("ro", t, t + 1)], [("ri", t, t + 1)], 1 << 16, False)
+            send([(-t, T.ri[:, r0:r0 + 256], T.ro[:, r0:r0 + 256], ("ri", t, t + 1))], [("ro", t, t + 1)], 1 << 16)
 
     claims(0)
     for t in range(NT):
-        if t + 1 < NT:
+        if t < LAST:
             claims(t + 1)
         tests(t)
     cnt["tag"] = "end"
     py = bank(0, 0, 256)
     pe([(py, row("oc"), T.ones[0:1, 0:256], True, False, 256)]
-       + [(py, T.i16[:], T.ri[:, 256 * t:256 * t + 256], False, t == NT - 2, 256) for t in range(NT - 1)], ["oc", "ones", "i16", ("ri", 0, NT - 1)], [bk_(0)])
-    tt(T.ys[:], py, T.ri[:, 768:1024], ALU.add, [bk_(0), ("ri", NT - 1, NT)], ["ys"], 256)
+       + [(py, T.i16[:], T.ri[:, 256 * t:256 * t + 256], False, t == LAST - 1, 256) for t in range(LAST)], ["oc", "ones", "i16", ("ri", 0, LAST)], [bk_(0)])
+    tt(T.ys[:], py, T.ri[:, 256 * LAST:256 * NT], ALU.add, [bk_(0), ("ri", LAST, NT)], ["ys"], 256)
     for h in range(2):
-        dma(T.y[:, 256 * h:256 * h + 256], T.ys[64 * h:64 * h + 40, :], ["ys"], [("y", h, h + 1)], 40960)
+        dma(T.y[:, 256 * h:256 * h + 256], T.ys[64 * h:64 * h + 40, :], ["ys"], [("y", h, h + 1)], 40960, q="sa"[h])
 
     if "best" not in PLAN:
         PLAN["best"] = plan(ops)

import math
import numpy as np
from concourse.bass import DstId, RemoteDMATransfer
from concourse.mybir import AluOpType, ActivationFunctionType

ALU = AluOpType
AF = ActivationFunctionType
NV, NL, L, CAP, NT = 2048, 4096, 512, 192, 4
SH = [t * (t + 1) // 2 % 8 for t in range(NT)]
WIN = 1664
BF, F32, I32, U16 = "bfloat16", "float32", "int32", "uint16"
HALF = "float16"
BIG = float(2 ** 25)
WOFF = 32768.0
NW = 2
PARTS = [2, 1, 1, 2]
PIECE = [1024, 512, 512, 512]
GAP = 1024
STEP = 96

SCRATCH = {}
for _t, _l in [
    (BF, "lfs 4096 ivs 2048 wc 128 wf 64 wb 128 wr 128 iw 256 ni 128 isc 384 hs 512 rt 256 rn 16 ts 128 tb 128 tr 128 tp 128 bm 128 dl 144 "
         "dm 256 ge 128 gp 128 gm 128 pl 128 mi 128 h0 128 ra 96 rc 96 sr 512 br 512 gh 256 crow 128 neg 128 oc 128 krow 128 qrow 256 "
         "ones 512 rs 512 k15 512 jt 512 jrow 512 xt 2048 ct 2048 tg 2048 tl 1152 ga 8192 gc0 8192 gc1 8192 nz 512 zp 528 cl 128 "
         "gi 512 fit 512 chi 2048 lin 128 lout 128 ff 32 ss 48 ln 1664 gb 3072 uu 768 vv 768 fl 384 rv 1664 ev 512"),
    (F32, "hn 128 idf 128 jc 32 qc 8 sb 1024 sc 1024 eq 1024 awf 4096 kp 512 kb 2048 ac 768 a2 1536 ys 256"),
    (I32, "kds 2048 bks 2048 lvi 32 lbi 32"),
    (U16, "lvu 32 lbu 128 kau 512 awu 8192 wu 2048 wl 128 ofu 32 lnu 16 kbu 192"),
    (HALF, "h16 128 i16 128 dg 144 rb 96 wh 1024 cc 2048 gk 512 ro 1024 ri 1024"),
]:
    _w = _l.split()
    for _i in range(0, len(_w), 2):
        SCRATCH[_w[_i]] = ("sbuf", [128, int(_w[_i + 1])], _t)
for _n in ("p0", "p1", "p2", "p3"):
    SCRATCH[_n] = ("psum", [128, 1024], F32)
SCRATCH["lbd"] = ("dram", [256, 32], U16)
SCRATCH["awd"] = ("dram", [256 * NW, 2048 // NW], U16)
SCRATCH["tgd"] = ("dram", [256, 384], BF)

SEMAPHORES = ["ev_v", "ev_a", "ev_p", "ev_g", "sent"] + ["d%d" % i for i in range(44)] + ["r%d" % i for i in range(30)]

CYC, PEC, FIX, HOP, LAT, SEND = 0.9, 0.44, 60.0, 2300.0, 90.0, 350.0
RATE = {"c": 1.0, "g": 1.56, "s": 3.8}
LOCAL_RATE, LINK_RATE = 220.0, 60.0
CASES = [{}, {"c": 0.93, "gpsimd": 0.93, "g": 0.7, "s": 0.6, "p": 0.95, "r": 3.0, "after l": 1.4, "after c": 1.5},
         {"c": 1.35, "gpsimd": 1.35, "g": 1.5, "s": 1.6, "p": 1.35, "l": 1.3}, {"c": 0.95, "g": 0.75, "p": 1.2, "d": 0.7, "l": 1.5, "after d": 1.3},
         {"c": 1.1, "gpsimd": 1.1, "g": 1.2, "p": 1.1, "d": 1.3, "l": 0.6, "r": 2.0, "after c": 2.0}]
WEIGHT = [1.0, 1.0, 0.7, 1.0, 0.9]
TRIES, STEPS, HEAT, SIDE, SEED = 40, 26000, 1000.0, 0.3, 2
PLAN = {}


def GA(n):
    return ("g", n)


def lay(ops, before, after, key):
    n = len(ops)
    left = [len(b) for b in before]
    start, end, eng = [0.0] * n, [0.0] * n, [None] * n
    busy = {e: ([], []) for e in "vapgs"}
    pool = sorted(((key[i], i) for i in range(n) if left[i] == 0), reverse=True)
    while pool:
        i = pool.pop()[1]
        rdy = max([end[d] + lat for d, lat in before[i]] + [0.0])
        best = None
        for e, c in ops[i]["cost"].items():
            t, k = rdy, 0
            if e != "x":
                ss, es = busy[e]
                while k < len(ss) and (es[k] <= t or ss[k] < t + c):
                    t = max(t, es[k])
                    k += 1
            if best is None or t + c < best[0]:
                best = (t + c, e, t, k)
        end[i], eng[i], start[i], k = best
        if eng[i] != "x":
            busy[eng[i]][0].insert(k, start[i])
            busy[eng[i]][1].insert(k, end[i])
        for x, lat in after[i]:
            left[x] -= 1
            if left[x] == 0:
                pool.append((key[x], x))
        pool.sort(reverse=True)
    return start, end, eng


def replay(ins, cost, order, eng, lo=0, old=None):
    n = len(ins)
    end, why = (old[0][:], old[1][:]) if old else ([0.0] * n, [-1] * n)
    free, last = {"x": 0.0}, {}
    for i in reversed(order[:lo]):
        if eng[i] not in free:
            free[eng[i]], last[eng[i]] = end[i], i
            if len(free) == 6:
                break
    for i in order[lo:]:
        t, w, e = 0.0, -1, eng[i]
        for d, lat in ins[i]:
            x = end[d] + lat
            if x > t:
                t, w = x, d
        if e != "x":
            x = free.get(e, 0.0)
            if x > t:
                t, w = x, -2 - last[e]
            free[e], last[e] = t + cost[i][e], i
        end[i], why[i] = t + cost[i][e], w
    return end, why


def waits(why, i):
    held = []
    while i != -1:
        w = why[i]
        if w < -1:
            w = -2 - w
            held.append((w, i))
        i = w
    return held


def priced(ops, case):
    return ([[(d, lat * case.get("after " + ops[d]["kind"], 1.0)) for d, lat in o["in"]] for o in ops],
            [{e: c * case.get("gpsimd" if e == "g" and o["cls"] == "c" else o["cls"], 1.0) for e, c in o["cost"].items()} for o in ops])


def plan(ops):
    n = len(ops)
    ins = [o["in"] for o in ops]
    outs = [[] for _ in range(n)]
    for i, o in enumerate(ops):
        for d, lat in o["in"]:
            outs[d].append((i, lat))
    costs = [priced(ops, case) for case in CASES]
    marks = [i for i, o in enumerate(ops) if o["wr"] and o["wr"][0][0] in ("lout", "kb")]

    def score(order, eng, lo=0, old=None):
        r = [replay(c[0], c[1], order, eng, lo, old and old[k]) for k, c in enumerate(costs)]
        return sum((max(x[0]) + SIDE * sum(x[0][i] for i in marks) / len(marks)) * w for x, w in zip(r, WEIGHT)), r
    key = [0.0] * n
    for i in range(n - 1, -1, -1):
        key[i] = -min(ops[i]["cost"].values()) + min([key[x] - lat for x, lat in outs[i]] + [0.0])
    rng = np.random.default_rng(SEED)
    best = None
    for trial in range(TRIES):
        start, end, eng = lay(ops, ins, outs, key)
        order = sorted(range(n), key=lambda x: (start[x], x))
        s, held = score(order, eng)
        if best is None or s < best[0]:
            best = (s, order, eng, held)
        end = lay(ops, outs, ins, (rng.normal(size=n) * 200.0 - np.array(end)).tolist())[1]
        key = [-x for x in end]
    cur, order, eng, res = best
    pos = {x: k for k, x in enumerate(order)}
    for step in range(STEPS):
        o2, e2, u = order, eng, rng.random(6)
        end, why = res[int(u[0] * len(res))]
        held = waits(why, marks[int(u[1] * len(marks))] if u[2] < SIDE else end.index(max(end)))
        if not held:
            continue
        j, i = held[int(u[3] * len(held))]
        m, far = u[4], (0, 0, 1, 3)[int(u[5] * 4)]
        free = [x for x in (i, j) if len(ops[x]["cost"]) > 1]
        if m < 0.3 and free:
            x = free[int(u[5] * len(free))]
            e2 = list(eng)
            e2[x] = [e for e in ops[x]["cost"] if e != eng[x]][0]
            lo = hi = pos[x]
        else:
            x, k, d, rel = (i, pos[j], -1, ins) if m < 0.65 else (j, pos[i], 1, outs)
            while far and 0 <= k + d < n:
                k += d
                far -= eng[order[k]] == eng[x]
            lo, hi = min(k, pos[x]), max(k, pos[x])
            move, todo = {x}, [x]
            while todo:
                for y, lat in rel[todo.pop()]:
                    if lo <= pos[y] <= hi and y not in move:
                        move.add(y)
                        todo.append(y)
            if len(move) > 12:
                continue
            a, b = [y for y in order[lo:hi + 1] if y in move], [y for y in order[lo:hi + 1] if y not in move]
            o2 = order[:lo] + (a + b if d < 0 else b + a) + order[hi + 1:]
        s, h = score(o2, e2, lo, res)
        if s <= cur or rng.random() < math.exp((cur - s) / (HEAT * (1 - step / STEPS) + 1.0)):
            cur, res, order, eng = s, h, o2, e2
            for k in range(lo, hi + 1):
                pos[order[k]] = k
            if s < best[0]:
                best = (s, o2, e2, h)
    return best


def rank_program(g, core, T, topo):
    rank = T.rank_of(core)
    if rank is None:
        return None
    N = len(T.cores)
    ops = []
    hist = {}
    line = []
    cnt = {"d": 0, "r": 0, "sent": 0, "tag": "load"}
    Q = {"v": g.vector, "a": g.scalar, "p": g.tensor, "g": g, "s": g.sync, "x": None}

    def add(engs, fn, rd, wr, cost, lat=LAT, kind="c", extra=(), cls="c", soft=()):
        i = len(ops)
        deps = set(extra) | set(soft)
        for isw, lst in ((False, rd), (True, wr)):
            for x in lst:
                nm, lo, hi = x if isinstance(x, tuple) else (x, 0, 1 << 30)
                w = isw or nm[0] == "@"
                h = hist.setdefault(nm, [])
                for (j, jw, a, b) in h:
                    if j != i and a < hi and lo < b and (w or jw):
                        deps.add(j)
                if w:
                    h[:] = [e for e in h if not (lo <= e[2] and e[3] <= hi)]
                h.append((i, w, lo, hi))
        ops.append({"fn": fn, "deps": sorted(deps), "lat": lat, "kind": kind, "cls": cls, "wr": wr, "soft": tuple(soft), "tag": cnt["tag"],
                    "in": [(d, 0.0 if d in soft or cls == ops[d]["cls"] == "p" else ops[d]["lat"]) for d in sorted(deps)],
                    "cost": cost if isinstance(cost, dict) else {e: cost for e in engs}})
        return i

    def bank(b, lo=0, hi=512, st=1, p0=0, p1=128):
        return T["p%d" % (b // 2)][p0:p1, (b % 2) * 512 + lo:(b % 2) * 512 + hi:st]

    def bk_(b):
        return "@%d" % b

    def comp(engs, fn, rd, wr, cyc, half=False):
        cls, n = cyc if isinstance(cyc, tuple) else ("c", cyc)
        cost = {e: FIX + max(64, n * RATE[cls] * (0.5 if half and e == "v" else 1.0)) * CYC for e in engs}
        return add(engs, fn, rd, wr, cost, cls=cls)

    def V(fn, rd, wr, cyc):
        return comp("v", lambda e: fn(g.vector), rd, wr, cyc)

    def tt(out, a, b, op, rd, wr, cyc=64):
        return V(lambda q: q.tensor_tensor(out, a, b, op), rd, wr, cyc)

    def scan(out, d0, d1, init, o0, o1, rd, wr, cyc=64):
        return V(lambda q: q.tensor_tensor_scan(out, d0, d1, init, o0, o1), rd, wr, cyc)

    def ms(out, c, wr, n):
        return V(lambda q: q.memset(out, float(c)), [], wr, n / 2)

    def lin(out, a, sc, bi, rd, wr, cyc=64, half=False):
        def fn(e):
            plain = isinstance(bi, float) and bi == 0.0
            if e == "a":
                if plain:
                    return g.scalar.activation(out, a, AF.Copy, scale=sc)
                return g.scalar.activation(out, a, AF.Identity, bias=bi, scale=sc)
            if plain and isinstance(sc, float) and sc == 1.0:
                return g.vector.tensor_copy(out, a)
            if plain:
                return g.vector.tensor_scalar(out, a, sc, None, ALU.mult)
            return g.vector.tensor_scalar(out, a, sc, bi, ALU.mult, ALU.add)
        return comp("va", fn, rd, wr, cyc, half)

    def act(out, a, func, rd, wr, cyc, bias=0.0, scale=1.0, more=0.0, soft=()):
        return add("a", lambda e: g.scalar.activation(out, a, func, bias=bias, scale=scale), rd, wr, FIX + more + max(64, cyc) * CYC, soft=soft)

    def either(out, a, vec, sca, rd, wr, cyc, half=False):
        def fn(e):
            if e == "a":
                return g.scalar.activation(out, a, sca[0], bias=sca[1], scale=sca[2])
            if vec[1] is None:
                return g.vector.tensor_scalar(out, a, vec[0], None, vec[2])
            return g.vector.tensor_scalar(out, a, vec[0], vec[1], vec[2], vec[3])
        return comp("va", fn, rd, wr, cyc, half)

    def nonzero(out, a, rd, wr, cyc):
        return either(out, a, (0.0, None, ALU.not_equal), (AF.Abs, 0.0, 1.0), rd, wr, cyc)

    def iszero(out, a, rd, wr, cyc):
        return either(out, a, (0.0, None, ALU.is_equal), (AF.Relu, 1.0, -1.0), rd, wr, cyc)

    def positive(out, a, rd, wr, cyc):
        return either(out, a, (0.0, None, ALU.is_gt), (AF.Sign, 0.0, 1.0), rd, wr, cyc)

    def relu(out, a, rd, wr, cyc, sc=1.0, half=False):
        return either(out, a, (sc, 0.0, ALU.mult, ALU.max), (AF.Relu, 0.0, sc), rd, wr, cyc, half)

    def pe(mms, rd, wr):
        def fn(e):
            r = None
            for m in mms:
                r = g.tensor.matmul(m[0], m[1], m[2], m[3], m[4])
            return r
        return add("p", fn, rd, wr, FIX + sum(max(64, m[5]) for m in mms) * PEC, cls="p")

    def iota(out, pat, base, cm, wr, n):
        return add("g", lambda e: g.iota(out, pat, base, cm, allow_small_or_imprecise_dtypes=True), [], wr, 130 + 2 * n * CYC)

    def sel(out, a, pat, op, fill, base, cm, rd, wr, n):
        return add("g", lambda e: g.affine_select(out, a, pat, op, fill, base, cm), rd, wr, 170 + 2 * n * CYC)

    def gcp(out, a, rd, wr, n):
        return sel(out, a, [[0, n]], ALU.is_ge, 0.0, 0, 0, rd, wr, n)

    def gfill(out, c, wr, n):
        def fn(e):
            if e == "a":
                return g.scalar.activation(out, T.ones[:, 0:n], AF.Copy, scale=float(c))
            return g.affine_select(out, T.ones[:, 0:n], [[0, n]], ALU.is_gt, float(c), 0, 0)
        return add("ag", fn, ["ones"], wr, {"a": FIX + max(64, n) * CYC, "g": 170 + 2 * n * CYC})

    def put(view, pat, a, c, nm, n):
        return sel(view, view, pat, ALU.not_equal, float(c), -a, 1, [nm], [nm], n)

    def band(out, src, pat, lo, hi, rd, nm, n):
        sel(out, src, pat, ALU.is_ge, 0.0, -lo, 1, rd, [nm], n)
        return sel(out, out, [[-s, c] for s, c in pat], ALU.is_ge, 0.0, hi, -1, [nm], [nm], n)

    def dma(out, src, rd, wr, nbytes, soft=(), q="s"):
        sem = T.sem["d%d" % cnt["d"]]
        cnt["d"] += 1
        i = add(q, lambda e: Q[e].dma_start(out, src).then_inc(sem, 16), rd, wr, nbytes / LOCAL_RATE + 60.0, lat=2000.0, kind="d", cls="d", soft=soft)
        ops[i]["sem"], ops[i]["val"] = sem, 16
        return i

    def send(moves, rd, nbytes):
        def share(a, b, k):
            es = topo.engines(a, b)
            n = len(es)
            return es if len(moves) == 1 else es[:n // 2] if k == 0 else es[n // 2 + (k - 1) * n // 4:n // 2 + k * n // 4]
        trs, sems = [], []
        for k, (dr, out, src, land) in enumerate(moves):
            sems.append(T.sem["r%d" % cnt["r"]])
            cnt["r"] += 1
            dst = T.cores[(rank + dr) % N]
            rid, pid = topo.addr(dst)[:2]
            es = share(core, dst, k)
            cnt["sent"] += len(es)
            trs.append((out, src, sems[k], pid, rid, sum(1 << x for x in es)))

        def fn(e):
            if len(trs) == 1:
                o, s, sem, pid, rid, mask = trs[0]
                return g.remote_dma(o, s, sem, T.sem.sent, pid, rid, mask)
            return g.remote_dma_fused([RemoteDMATransfer(dst_ids=[DstId(rid=rid, pnc=pid)], dma_engine_mask=mask, remote_sem=sem, src=s, dst=o)
                                       for o, s, sem, pid, rid, mask in trs], local_sem=T.sem.sent)
        i = add("g", fn, rd, [], SEND, lat=0.0, kind="r", extra=line[-2:-1], cls="r")
        before = [i] + line[-1:]
        for k, (dr, out, src, land) in enumerate(moves):
            j = add("x", None, [], [land], nbytes * (1 if len(moves) == 1 else 3 if k else 2) / LINK_RATE, lat=HOP, kind="l", extra=before, cls="l")
            ops[j]["sem"], ops[j]["val"] = sems[k], len(share(T.cores[(rank - dr) % N], core, k))
        line.extend([i, add("x", None, [], [], nbytes * len(moves) / LINK_RATE, lat=0.0, kind="r", extra=before, cls="l")])

    def ind(win, off):
        return win.indirect(off)

    def blk(nm, i):
        return T[nm][:, 128 * i:128 * i + 128], (nm, 128 * i, 128 * i + 128)

    def row(nm, i=0, n=128):
        return T[nm][0:1, 128 * i:128 * i + n]

    def back(t):
        return 16 * ((-SH[t]) % 8)

    G8, G16, GW = [[-16, 8]], [[0, 2], [-16, 8]], [[-16, 8], [0, 16]]
    ident = T.iw[:, 0:128]
    LAST = NT - 1

    k = ()
    for (o, x, wr, nb) in [(T.ivs[:, 0:1024], T.iv[:, 0:1024], ("ivs", 0, 1024), 18), (T.lbi[:], T.lb[:], "lbi", 14),
                           (T.ivs[:, 1024:2048], T.iv[:, 1024:2048], ("ivs", 1024, 2048), 18), (T.lvi[:], T.lv[:], "lvi", 14),
                           (T.bks[:], T.bk[:], "bks", 20), (T.kds[:], T.kd[:], "kds", 20), (T.lfs[:], T.lf[:], "lfs", 20)]:
        k = (dma(o, x, [], [wr], 1 << nb, k),)

    cnt["tag"] = "const0"
    l8, l16 = math.log(8.0), math.log(16.0)
    iota(row("qrow", 0), [[0, 8], [1, 16]], 0, 0, [blk("qrow", 0)[1]], 128)
    k = act(row("qrow", 1), row("qrow", 0), AF.Exp, [blk("qrow", 0)[1]], [blk("qrow", 1)[1]], 128, 15 * l16 + 1.0, -l16, 1300.0)
    ms(T.ones[:], 1, ["ones"], 512)
    ms(T.sr[0:1, 0:128:2], 8, [("sr", 0, 128)], 64)
    ms(T.sr[0:1, 1:128:2], -8, [("sr", 0, 128)], 64)
    for i, s in ((3, 2), (1, 1), (2, 1)):
        iota(row("sr", i), [[0, 64 >> i], [-2 * s, 2], [0, 1 << i]], s, 0, [blk("sr", i)[1]], 128)
    sel(T.gh[0:8, 0:128], T.ones[0:8, 0:128], [[-1, 8], [0, 16]], ALU.is_equal, 0.0, 0, 1, ["ones"], [("gh", 0, 128)], 128)
    lin(T.gh[0:8, 128:256], T.gh[0:8, 0:128], -128.0, 0.0, [("gh", 0, 128)], [("gh", 128, 256)], 128, half=True)
    ex = bank(6, 0, 128)
    pe([(ex, row("sr", i), row("sr", i), n == 0, False, 128) for n, i in enumerate((0, 3, 1, 2, 2))]
       + [(ex, T.gh[0:8, 0:128], T.gh[0:8, 128:256], False, True, 128)], ["sr", "gh"], [bk_(6)])
    for m in range(2):
        act(T.wc[:, m::2], bank(6, 1 - m, 128, 2), AF.Exp, [bk_(6)], [("wc", m, m + 1)], 64, -92.5 * l8, -0.5 * l8, soft=(k,))
    act(T.wb[:], ex, AF.Exp, [bk_(6)], ["wb"], 128, -92.5 * l8 + math.log(BIG), -0.5 * l8, soft=(k,))
    tt(T.wf[:], T.wc[:, 0::2], T.wc[:, 1::2], ALU.subtract, ["wc"], ["wf"], 128)
    ms(row("neg"), -2.0 ** 24, ["neg"], 128)
    ms(T.rs[:], 0, ["rs"], 512)
    ms(T.rs[:, 0::8], -2.0 ** 26, ["rs"], 64)
    ms(T.xt[:], 0, ["xt"], 2048)
    ms(T.wr[:], 0, ["wr"], 128)
    ms(row("crow"), 0, ["crow"], 128)
    for a, st, c in ((4, 8, -256), (5, 8, -131072), (3, 4, 1)):
        ms(T.crow[0:1, a::st], c, ["crow"], 32)
    sel(T.iw[:], T.ones[:, 0:256], [[0, 2], [-1, 128]], ALU.is_equal, 0.0, 0, 1, ["ones"], ["iw"], 256)
    lin(T.idf[:], ident, 1.0, 0.0, ["iw"], ["idf"], 128)
    lin(T.ni[:], ident, -1.0, 0.0, ["iw"], ["ni"], 128, half=True)
    for m in range(2):
        src = T.wc[:, m::16]
        sel(T.wr[:, 4 + 8 * m::16], src, [[16, 8]], ALU.is_ge, 0.0, 5, -1, ["wc", "wr"], [("wr%d" % m, 0, 1)], 8)
        band(T.wr[:, 5 + 8 * m::16], src, G8, 6, 11, ["wc", "wr"], ("wr%d" % m, 1, 2), 8)
        sel(T.wr[:, 6 + 8 * m::16], src, G8, ALU.is_ge, 0.0, -12, 1, ["wc", "wr"], [("wr%d" % m, 2, 3)], 8)

    cnt["tag"] = "lists"
    lin(T.lbu[:, 0:32], T.lbi[:], 1.0, 0.0, ["lbi"], [("lbu", 0, 32)])
    lin(T.lvu[:], T.lvi[:], 1.0, 0.0, ["lvi"], ["lvu"])
    dma(T.lbd[0:128, :], T.lbu[:, 0:32], [("lbu", 0, 32)], [("lbd", 0, 1)], 1 << 13)
    dma(T.lbd[128:240, :], T.lbu[0:112, 0:32], [("lbu", 0, 32)], [("lbd", 1, 2)], 1 << 13)
    send([(t, T.lbu[:, 32 * t:32 * t + 32], T.lbd[back(t):back(t) + 128, :], ("lbu", 32 * t, 32 * t + 32)) for t in range(1, NT)], ["lbd"], 1 << 13)

    cnt["tag"] = "canon"
    for hf in range(2):
        cs, iv = range(8 * hf, 8 * hf + 8), ("ivs", 1024 * hf, 1024 * hf + 1024)
        pe([(bank(hf), row("neg"), T.ones[0:1, :], True, False, 512)], ["neg", "ones"], [bk_(hf)])
        pe([(T.p0[:, 64 * c:64 * c + 64], T.ivs[:, 128 * c:128 * c + 128], T.wc[:, m::2], False, m == 1 and c == cs[-1], 64) for m in range(2) for c in cs],
           [iv, "wc"], [bk_(hf)])
        pe([(T.p1[:, 64 * c:64 * c + 64], T.ivs[:, 128 * c:128 * c + 128], T.wf[:], True, True, 64) for c in cs], [iv, "wf"], [bk_(2 + hf)])
    for b in range(4):
        pe([(bank(4 + b), row("crow"), T.ones[0:1, :], True, False, 512), (bank(4 + b), T.wr[:], T.ivs[:, 512 * b:512 * b + 512], False, False, 512)],
           ["crow", "ones", "wr", "wr0", "wr1", ("ivs", 512 * b, 512 * b + 512)], [bk_(4 + b)])

    def split(src, sn, hf, r0, b):
        xa, k = 1024 * hf + r0, 2 * hf + r0 // 8
        x = [T.xt[:, xa + i:1024 * hf + 1024:16] for i in range(3)]
        xn = [("xt%d" % i, k, k + 1) for i in range(3)]
        r = bank(b, 0, 64)
        lin(x[0], src, 1.0, 0.0, [sn, "xt"], [xn[0]])
        pe([(r, T.idf[:], src, True, False, 256), (r, T.ni[:], x[0], False, True, 64)], ["idf", "ni", sn, xn[0]], [bk_(b)])
        lin(x[1], r, 1.0, 0.0, [bk_(b), "xt"], [xn[1]])
        tt(x[2], r, x[1], ALU.subtract, [bk_(b), xn[1], "xt"], [xn[2]])
    for hf in range(2):
        a, b = 512 * hf, 512 * hf + 512
        sb, scr, eqr = ("sb", a, b), ("sc", a, b), ("eq", a, b)
        act(bank(2 + hf), bank(2 + hf), AF.Abs, [], [bk_(2 + hf)], 512)
        scan(T.sc[:, a:b], T.rs[:], bank(hf), 0.0, ALU.add, ALU.max, ["rs", bk_(hf)], [scr], 512)

        def cmp8(e, a=a, b=b):
            r = None
            for m in range(8):
                r = g.vector.tensor_tensor(T.eq[:, a + m:b:8], T.p0[:, a + m:b:8], T.sc[:, a + 7:b:8], ALU.is_equal)
            return r
        add("v", cmp8, [bk_(hf), scr], [eqr], 8 * (FIX + 64 * CYC))
        tt(T.eq[:, a:b], bank(2 + hf), T.eq[:, a:b], ALU.mult, [bk_(2 + hf), eqr], [eqr], 512)
        scan(T.sb[:, a:b], T.rs[:], T.eq[:, a:b], 0.0, ALU.add, ALU.max, ["rs", eqr], [sb], 512)
        split(T.sc[:, a + 7:b:8], scr, hf, 0, hf)
        split(T.sb[:, a + 7:b:8], sb, hf, 8, 2 + hf)
        for u in range(2):
            bn, lo = 4 + 2 * hf + u, 1024 * hf + 512 * u
            pe([(bank(bn, 128 * k, 128 * k + 128), T.xt[:, lo + 128 * k:lo + 128 * k + 128], ident, False, k == 3, 128) for k in range(4)],
               [("xt%d" % i, 2 * hf, 2 * hf + 2) for i in range(3)] + ["xt", "iw"], [bk_(bn)])
            lin(T.ct[:, lo:lo + 512], bank(bn), 1.0, 0.0, [bk_(bn)], [("ct", lo, lo + 512)], 512)

    cnt["tag"] = "const1"
    sel(T.rt[:], T.ones[:, 0:256], [[-8, 2], [-16, 8], [0, 16]], ALU.is_ge, 0.0, 0, 1, ["ones"], ["rt"], 256)
    sel(T.rt[:], T.rt[:], [[8, 2], [16, 8], [0, 16]], ALU.is_ge, 0.0, 2, -1, ["rt"], ["rt"], 256)
    lin(T.rt[:, 0:128], T.rt[:, 0:128], BIG, 0.0, ["rt"], ["rt"], 128, half=True)
    lin(T.rn[:], T.rt[:, 0::16], -1.0, 0.0, ["rt"], ["rn"])
    band(T.bm[:], T.ones[:, 0:128], GW, 0, 15, ["ones"], "bm", 128)
    lin(T.tr[:], ident, -4096.0, 0.0, ["iw"], ["tr"], 128, half=True)
    lin(T.i16[:], ident, 1.0, 0.0, ["iw"], ["i16"], 128, half=True)
    gfill(T.dg[:], 0, ["dg"], 144)
    gcp(T.dg[:, 15:143:16], T.bm[:, 0::16], ["bm", "dg"], ["dg"], 8)
    gfill(T.k15[:], 0, ["k15"], 512)
    gfill(T.k15[:, 15::16], 1, ["k15"], 32)
    gfill(T.zp[:, 0:1], 1, [("zp", 0, 1)], 1)
    for i in range(3):
        lin(blk("isc", i)[0], ident, float(16 ** (i + 1)), 0.0, ["iw"], [blk("isc", i)[1]], 128, half=True)
    cnt["tag"] = "const2"
    for i in range(4):
        iota(row("br", i), [[0, 64 >> i], [1, 2], [0, 1 << i]], 0, 0, [blk("br", i)[1]], 128)
    hx = bank(3, 0, 128)
    pe([(hx, row("br", i), row("br", i), i == 0, i == 3, 128) for i in range(4)]
       + [(bank(3, 128, 129), row("qrow", 1), T.ones[0:1, 0:1], True, True, 64)], ["br", "qrow", "ones"], [bk_(3)])
    lin(T.qc[:, 0:1], bank(3, 128, 129), 1.0, 0.0, [bk_(3)], ["qc"])
    act(hx, hx, AF.Abs, [], [bk_(3)], 128, -2.0)
    act(hx, hx, AF.Abs, [], [bk_(3)], 128, -1.0)
    lin(T.h0[:], hx, 2.0, -1.0, [bk_(3)], ["h0"], 128)
    band(T.h0[:], T.h0[:], GW, 0, 15, ["h0"], "h0", 128)
    lin(T.h16[:], T.h0[:], 1.0, 0.0, ["h0"], ["h16"], 128, half=True)
    lin(T.hn[:], T.h0[:], -1.0, 0.0, ["h0"], ["hn"], 128)
    lin(T.ge[:], T.h0[:], T.qc[:, 0:1], 0.0, ["h0", "qc"], ["ge"], 128)
    for nm, r0, sc in (("ts", 4, 1.0), ("tb", 12, BIG)):
        gfill(T[nm][:], -sc, [nm], 128)
        band(T[nm][:], T[nm][:], GW, r0, r0 + 2, [nm], nm, 128)
        put(T[nm][:], GW, 3, -256 * sc, nm, 128)
        put(T[nm][:], GW, 7, -131072 * sc, nm, 128)
    cnt["tag"] = "const3"
    for i in range(4):
        lin(blk("hs", i)[0], T.h0[:], 16.0 ** i, 0.0, ["h0"], [blk("hs", i)[1]], 128, half=True)
    relu(T.pl[:], T.h0[:], ["h0"], ["pl"], 128, half=True)
    relu(T.mi[:], T.h0[:], ["h0"], ["mi"], 128, -1.0, half=True)
    lin(T.gp[:], T.ge[:], 1.0, 0.0, ["ge"], ["gp"], 128, half=True)
    lin(T.gm[:], T.ge[:], 0.25, 0.0, ["ge"], ["gm"], 128, half=True)
    lin(T.gp[:, 3::16], T.ge[:, 0::16], -1.0, 0.0, ["ge"], ["gp"])
    gcp(T.gp[:, 5::16], T.ge[:, 0::16], ["ge"], ["gp"], 8)
    for c in (3, 5):
        gcp(T.gm[:, c::16], T.gm[:, 0::16], ["gm"], ["gm"], 8)
    sel(T.tp[:], T.bm[:], [[1, 128]], ALU.is_gt, 0.0, 0, -1, ["bm"], ["tp"], 128)
    iota(T.jc[:], [[16, 32]], 512, 1, ["jc"], 32)
    iota(T.jt[:], [[1, 32], [0, 16]], 0, 0, ["jt"], 512)
    iota(T.jrow[:], [[0, 32], [1, 16]], 0, 0, ["jrow"], 512)
    dma(T.jrow[0::16, :], T.jt[0::16, :], ["jt"], ["jrow"], 1 << 13)
    for nm in ("dl", "dm"):
        gfill(T[nm][:], 0, [nm], SCRATCH[nm][1][1])
    gfill(T.ln[:, 0:CAP], 0, ["ln"], CAP)
    for a in range(CAP, WIN, 512):
        b = min(a + 512, WIN)
        gfill(T.rv[:, a:b], 0, [("rv", a, b)], b - a)
    gfill(T.ss[:, 0:1], 0, [("ss", 0, 1)], 1)
    put(T.dl[:, 15:143:16], G8, 0, 16, "dl", 8)
    put(T.dl[:, 15:143:16], G8, 1, 1, "dl", 8)
    put(T.dm[:, 15::16], G16, 0, -1, "dm", 16)
    cnt["tag"] = "const4"
    for nm in ("ra", "rb", "rc", "oc", "krow"):
        gfill(T[nm][:], 0, [nm], SCRATCH[nm][1][1])
    band(T.rb[:, 1:80:5], T.ones[:, 0:16], G16, 0, 15, ["ones", "rb"], "rb", 16)
    for nm, f, a, c in [("ra", 0, 0, rank + 1), ("ra", 1, 0, 2048), ("ra", 1, 5, -1), ("ra", 2, 0, 16), ("ra", 3, 0, 15), ("ra", 4, 0, 1),
                        ("ra", 4, 3, -2), ("rc", 1, 0, -2048), ("rc", 2, 0, -8.5)] + \
            [("ra", 3, b, -b) for b in (1, 2, 4, 8)] + [("rc", 2, b, -0.5 * b) for b in (1, 2, 4, 8)]:
        put(T[nm][:, f:80:5], G16, a, c, nm, 16)
    for nm, f, c in (("krow", 4, 1), ("oc", 0, -1), ("oc", 4, -NT)):
        for h in range(2):
            gfill(T[nm][:, 64 * h + f:64 * h + 40:5], c, [nm], 8)

    cnt["tag"] = "targets"
    lin(T.tg[:, 0:512], ind(T.ct[:], T.lvu[:]), 1.0, 0.0, ["ct", "lvu"], [("tg", 0, 512)], GA(512))
    for k in range(3):
        dma(T.tgd[0:128, 128 * k:128 * k + 128], T.tg[k::4, 0:512], [("tg", 0, 512)], [("tgd", k, k + 1)], 1 << 15)
        dma(T.tgd[128:240, 128 * k:128 * k + 128], T.tg[k:112:4, 0:512], [("tg", 0, 512)], [("tgd", 3 + k, 4 + k)], 1 << 15)
    dma(T.tg[3::4, 512:2048], T.ct[3::4, 0:1536], ["ct"], ["tgone"], 3 << 15)
    send([(t, T.tl[:, 384 * t - 384:384 * t], T.tgd[back(t):back(t) + 128, :], ("tl", t, t + 1)) for t in range(1, NT)], ["tgd"], 3 << 15)
    for t in range(1, NT):
        for k in range(3):
            a = 384 * (t - 1) + 128 * k
            dma(T.tg[k::4, 512 * t:512 * t + 512], T.tl[:, a:a + 128], [("tl", t, t + 1)], [("tg%d" % t, k, k + 1)], 1 << 15)
    cnt["tag"] = "words"
    lin(T.kau[:], ind(T.kds[:], T.lvu[:]), 1.0, 0.0, ["kds", "lvu"], ["kau"], GA(512))
    for a in range(0, 8192, GAP):
        lin(T.ga[:, a:a + GAP], ind(T.lfs[:], T.kau[:, a // 16:(a + GAP) // 16]), 1.0, 0.0, ["lfs", "kau"], [("ga", a, a + GAP)], GA(GAP))
    for hf in range(2):
        for ep in range(2):
            mm = []
            for e in (2 * ep, 2 * ep + 1):
                for i in range(4):
                    w = ident if i == 0 else blk("isc", i - 1)[0]
                    mm.append((bank(4 + e, 256 * hf, 256 * hf + 256), w, T.ga[:, 4096 * hf + 4 * e + i:4096 * hf + 4096:16],
                               i == 0, i == 3, 256))
            pe(mm, ["iw", "isc", ("ga", 4096 * hf, 4096 * hf + 4096)], [bk_(4 + 2 * ep), bk_(5 + 2 * ep)])
    wd = 2048 // NW
    for e in range(4):
        a = 512 * e
        lin(T.awu[:, a:a + 512], bank(4 + e), 1.0, WOFF, [bk_(4 + e)], [("awu", a, a + 512)], 512)
    for e in range(NW):
        a, r0 = wd * e, 256 * e
        dma(T.awd[r0:r0 + 128, :], T.awu[:, a:a + wd], [("awu", a, a + wd)], [("awd", 2 * e, 2 * e + 1)], 256 * wd)
        dma(T.awd[r0 + 128:r0 + 240, :], T.awu[0:112, a:a + wd], [("awu", a, a + wd)], [("awd", 2 * e + 1, 2 * e + 2)], 224 * wd)

    def words(t):
        for e in range(NW):
            a, r0 = 2048 * t + wd * e, 256 * e + back(t)
            send([(t, T.awu[:, a:a + wd], T.awd[r0:r0 + 128, :], ("awu", a, a + wd))], [("awd", 2 * e, 2 * e + 2)], 256 * wd)
    words(1)

    def claims(t):
        c0, u, n = 512 * t, t % 2, L // PARTS[t]
        cnt["tag"] = "claim%d" % t
        tgr = [("tg", c0, c0 + 512), "tg%d" % t] + (["tgone"] if t else [])
        gc, gn = T["gc%d" % u], "gc%d" % u
        lin(T.wu[:, c0:c0 + 512], ind(T.bks[:], T.lbu[:, 32 * t:32 * t + 32]), 1.0, 0.0, ["bks", ("lbu", 32 * t, 32 * t + 32)], [("wu", t, t + 1)], GA(512))
        gcp(T.wh[:, 512 * u:512 * u + 512], T.wu[:, c0:c0 + 512], [("wu", t, t + 1)], [("wh", u, u + 1)], 512)
        w = PIECE[t]
        for a in range(0, 8192, w):
            lin(gc[:, a:a + w], ind(T.ct[:], T.wu[:, c0 + a // 16:c0 + (a + w) // 16]), 1.0, 0.0, ["ct", ("wu", t, t + 1)], [(gn, a, a + w)], GA(w))
        for p in range(PARTS[t]):
            x0, x1 = n * p, n * p + n
            bd, ba, bb = (u, 3, 2) if n == L else (p, 3 - p, p)
            l0, l1 = 32 * t + x0 // 16, 32 * t + x1 // 16

            def part(nm, o=0):
                return T[nm][:, o + x0:o + x1], (nm, o + x0, o + x1)
            cnt["tag"] = "claim%d" % t
            for x in range(x0, x1, 128):
                o, tgx = x - x0, T.tg[:, c0 + x:c0 + x + 128]
                mm = [(bank(bd, o, o + 128), tgx, T.rt[:, 0:128], True, False, 128)]
                for h in range(2):
                    mm += [(bank(bd, o + k, o + 128, 16), gc[:, 16 * x + k:16 * x + 2048:16], T.rn[:, 8 * h:8 * h + 8], False, False, 8) for k in range(16)]
                mm.append((bank(bd, o, o + 128), tgx, T.rt[:, 128:256], False, True, 128))
                pe(mm, ["rt", "rn", (gn, 16 * x, 16 * x + 2048)] + tgr, [bk_(bd)])
            (nz, nzr), (zp, zpr), (cc, ccr), (chi, chr_) = part("nz"), part("zp", 1), part("cc", c0), part("chi", c0)
            nonzero(nz, bank(bd, 0, n), [bk_(bd)], [nzr], n)
            scan(zp, nz, T.k15[:, 0:n], 1.0, ALU.min, ALU.max, [nzr, "k15"], [zpr], n / 2)
            mm = [(bank(ba, 0, n), T.i16[:], part("wh", 512 * u)[0], True, False, n)]
            for x in range(x0, x1, 128):
                mm.append((bank(ba, x - x0, x - x0 + 128), T.nz[:, x:x + 128], T.tr[:], False, False, 128))
                mm.append((bank(ba, x - x0, x - x0 + 128), T.zp[:, x:x + 128], blk("isc", 2)[0], False, x + 128 == x1, 128))
            pe(mm, ["i16", ("wh", u, u + 1), "tr", "isc", nzr, ("zp", x0, x1)], [bk_(ba)])
            either(cc, bank(ba, 0, n), (-4095.0, 0.0, ALU.add, ALU.max), (AF.Relu, -4095.0, 1.0), [bk_(ba)], [ccr], n)
            lst = bank(bb, 0, n // 16)
            pe([(lst, T.dg[:, 15 - i:143 - i], T.cc[:, c0 + x0 + i:c0 + x1:16], i == 0, i == 15, 32) for i in range(16)], ["dg", ccr], [bk_(bb)])
            wl, wlr = T.wl[:, l0:l1], ("wl", l0, l1)
            lin(wl, lst, 1.0, -1.0, [bk_(bb)], [wlr])
            positive(T.cl[:, l0:l1], lst, [bk_(bb)], [("cl", l0, l1)], 64)
            cnt["tag"] = "shift%d" % t
            (gi, gir), (gk, gkr), (fit, fir), (kp, kpr), (kb, kbr), tg = part("gi"), part("gk"), part("fit"), part("kp"), part("kb", c0), part("tg", c0)[0]
            A, B = bank(ba, 0, n), bank(bb, 0, n)
            lin(gi, ind(T.ivs[:], wl), 1.0, 0.0, ["ivs", wlr], [gir], GA(n))
            lin(gk, ind(T.kds[:], wl), 1.0, -2048.0, ["kds", wlr], [gkr], GA(n))
            pe([(A, T.tb[:], tg, True, False, n)], ["tb"] + tgr, [bk_(ba)])
            pe([(A, T.wb[:], gi, False, False, n), (A, T.wc[:], gi, False, False, n), (A, T.ts[:], tg, False, True, n)],
               ["wb", "wc", "ts", gir] + tgr, [bk_(ba)])
            V(lambda q, fit=fit, A=A: q.tensor_scalar(fit, A, 0.0, None, ALU.is_equal), [bk_(ba)], [fir], n)
            pe([(B, T.h16[:], gk, True, True, n)], ["h16", gkr], [bk_(bb)])
            pe([(A, T.ge[:], fit, True, True, n)], ["ge", fir], [bk_(ba)])
            either(chi, A, (-1.0, 1.0, ALU.max, ALU.min), (AF.Sign, 0.0, 1.0), [bk_(ba)], [chr_], n)
            tt(kp, B, chi, ALU.mult, [bk_(bb), chr_], [kpr], n)
            pe([(B, T.hn[:], kp, True, True, 4 * n)], ["hn", kpr], [bk_(bb)])
            lin(kb, B, -1.0 / 16, 2048.0, [bk_(bb)], [kbr], n)

    def tests(t):
        l0, l1, u, c0 = 32 * t, 32 * t + 32, t % 2, 512 * t
        cnt["tag"] = "conv%d" % t
        for e in range(4):
            a, o = 2048 * t + 512 * e, 2048 * u + 512 * e
            gcp(T.awf[:, o:o + 512], T.awu[:, a:a + 512], [("awu", a, a + 512)], [("awf", o, o + 512)], 512)
        cnt["tag"] = "test%d" % t
        if t == 0:
            F, fr = T.cl[:, 0:32], ("cl", 0, 32)
            live, lr = T.ones[:, 0:32], "ones"
        else:
            F, fr = T.ff[:], "ff"
            live, lr = T.lin[:, l0:l1], ("lin", l0, l1)
            tt(F, live, T.cl[:, l0:l1], ALU.mult, [lr, ("cl", l0, l1)], [fr])
        scan(T.ss[:, 1:33], T.ones[:, 0:32], F, 0.0, ALU.mult, ALU.add, ["ones", fr], [("ss", 1, 33)])
        o7 = bank(7, 0, 32)
        pe([(o7, blk("isc", 2)[0], T.ones[:, 0:32], True, False, 32), (o7, T.tp[:], F, False, False, 32), (o7, T.tr[:], F, False, False, 32),
            (o7, T.bm[:], T.ss[:, 0:32], False, True, 32)], ["isc", "ones", "tp", "bm", "ss", "tr", fr], [bk_(7)])
        tt(T.ofu[:], o7, T.jc[:], ALU.min, [bk_(7), "jc"], ["ofu"])
        V(lambda q: q.tensor_copy(ind(T.ln[:], T.ofu[:]), T.jrow[:]), ["ofu", "jrow"], ["ln"], ("s", 512))
        pe([(bank(7, 0, 12), T.dl[:, 15 - i:143 - i], T.ln[:, i:CAP:16], i == 0, i == 15, 12) for i in range(16)], ["dl", "ln"], [bk_(7)])
        ll = T.lnu[:, 0:12]
        lin(ll, bank(7, 0, 12), 1.0, 0.0, [bk_(7)], ["lnu"])
        lin(T.kbu[:], ind(T.kb[:, c0:c0 + 512], ll), 1.0, 0.0, [("kb", c0, c0 + 512), "lnu"], ["kbu"], GA(CAP))
        for e in range(4):
            o = 2048 * u + 512 * e
            lin(T.ac[:, CAP * e:CAP * e + CAP], ind(T.awf[:, o:o + 512], ll), 1.0, -WOFF, [("awf", o, o + 512), "lnu"], [("ac", e, e + 1)], GA(CAP))
        steps = [(0, STEP), (STEP, CAP)]
        for hf, (x0, x1) in enumerate(steps):
            n, o = x1 - x0, 4 * x0
            for a in (x0, x0 + n // 2):
                lin(T.gb[:, 16 * a:16 * a + 8 * n], ind(T.lfs[:], T.kbu[:, a:a + n // 2]), 1.0, 0.0, ["lfs", "kbu"], [("gb", a, a + n // 2)], GA(8 * n))
            pe([(bank(6 + hf, n * e, n * e + n), T.hn[:], T.ac[:, CAP * e + x0:CAP * e + x1], True, True, 4 * n) for e in range(4)], ["hn", "ac"], [bk_(6 + hf)])
            for s in range(2):
                lin(T.a2[:, 768 * s + o:768 * s + o + 4 * n], bank(6 + hf, 0, 4 * n), 2.0 * s - 1.0, 0.0, [bk_(6 + hf)],
                    [("a2", 2 * s + hf, 2 * s + hf + 1)], 4 * n)
        for hf, (x0, x1) in enumerate(steps):
            n, o = x1 - x0, 4 * x0
            pe([(bank(4 + hf, n * e, n * e + n), blk("hs", i)[0], T.gb[:, 16 * x0 + 4 * e + i:16 * x1:16], i == 0, i == 3, n)
                for e in range(4) for i in range(4)], ["hs", ("gb", x0, x1)], [bk_(4 + hf)])
            for s, nm in enumerate(("uu", "vv")):
                tt(T[nm][:, o:o + 4 * n], bank(4 + hf, 0, 4 * n), T.a2[:, 768 * s + o:768 * s + o + 4 * n], ALU.not_equal,
                   [bk_(4 + hf), ("a2", 2 * s + hf, 2 * s + hf + 1)], [(nm, hf, hf + 1)], 4 * n)
            for k, nm in enumerate(("uu", "vv")):
                pe([(bank(6 + s, x0, x1), T.mi[:] if s != k else T.pl[:], T[nm][:, o + n * e:o + n * e + n], k == 0 and e == 0, k == 1 and e == 3, n)
                    for s in range(2) for e in range(4)], ["pl", "mi", (nm, hf, hf + 1)], [bk_(6), bk_(7)])
        for s in range(2):
            iszero(T.fl[:, CAP * s:CAP * s + CAP], bank(6 + s, 0, CAP), [bk_(6 + s)], [("fl", s, s + 1)], CAP)
        pe([(bank(4, 0, CAP), T.gp[:], T.fl[:, 0:CAP], True, False, CAP), (bank(4, 0, CAP), T.gm[:], T.fl[:, CAP:384], False, True, CAP)],
           ["gp", "gm", "fl"], [bk_(4)])
        positive(T.rv[:, 0:CAP], bank(4, 0, CAP), [bk_(4)], [("rv", 0, CAP)], CAP)
        for h in range(2):
            relu(T.ev[:, 256 * h:256 * h + 256], ind(T.rv[:], T.ofu[:, 16 * h:16 * h + 16]), ["rv", "ofu"], [("ev", h, h + 1)], GA(256))
        if t < LAST:
            rho = 16 * (SH[t + 1] - SH[t])
            mm = [(o7, T.iw[:, (-rho) % 128:(-rho) % 128 + 128], live, True, False, 32)]
            for i in range(16):
                s0 = (15 - i - rho) % 128
                mm.append((o7, T.dm[:, s0:s0 + 128], T.ev[:, i:512:16], False, i == 15, 32))
            pe(mm, ["iw", "dm", lr, "ev"], [bk_(7)])
            lin(T.lout[:, l0:l1], o7, 1.0, 0.0, [bk_(7)], [("lout", l0, l1)])
            send([(1, T.lin[:, l1:l1 + 32], T.lout[:, l0:l1], ("lin", l1, l1 + 32))], [("lout", l0, l1)], 1 << 13)
            if t + 2 < NT:
                words(t + 2)
        cnt["tag"] = "res%d" % t
        rb, s5, r0 = (5 if t < LAST else 2), 5 * SH[t], 256 * t
        mm = [(bank(rb, 0, 256), row("krow"), T.ones[0:1, 0:256], True, False, 256)]
        for h in range(2):
            o = bank(rb, 0, 256, 1, 64 * h, 64 * h + 64)
            mm.append((o, T.rb[:, s5:s5 + 64], T.cc[:, c0 + 256 * h:c0 + 256 * h + 256], False, False, 256))
            mm.append((o, T.rc[:, s5:s5 + 64], T.chi[:, c0 + 256 * h:c0 + 256 * h + 256], False, False, 256))
        pe(mm, ["krow", "ones", "rb", "rc", ("cc", c0, c0 + 512), ("chi", c0, c0 + 512)], [bk_(rb)])
        pe([(bank(rb, 0, 256, 1, 64 * h, 64 * h + 64), T.ra[:, s5:s5 + 64], T.ev[:, 256 * h:256 * h + 256], False, True, 256) for h in range(2)],
           ["ra", "ev"], [bk_(rb)])
        relu((T.ro if t else T.ri)[:, r0:r0 + 256], bank(rb, 0, 256), [bk_(rb)], [("ro" if t else "ri", t, t + 1)], 256)
        if t:
            send([(-t, T.ri[:, r0:r0 + 256], T.ro[:, r0:r0 + 256], ("ri", t, t + 1))], [("ro", t, t + 1)], 1 << 16)

    claims(0)
    for t in range(NT):
        if t < LAST:
            claims(t + 1)
        tests(t)
    cnt["tag"] = "end"
    py = bank(0, 0, 256)
    pe([(py, row("oc"), T.ones[0:1, 0:256], True, False, 256)]
       + [(py, T.i16[:], T.ri[:, 256 * t:256 * t + 256], False, t == LAST - 1, 256) for t in range(LAST)], ["oc", "ones", "i16", ("ri", 0, LAST)], [bk_(0)])
    tt(T.ys[:], py, T.ri[:, 256 * LAST:256 * NT], ALU.add, [bk_(0), ("ri", LAST, NT)], ["ys"], 256)
    for h in range(2):
        dma(T.y[:, 256 * h:256 * h + 256], T.ys[64 * h:64 * h + 40, :], ["ys"], [("y", h, h + 1)], 40960, q="sa"[h])

    if "best" not in PLAN:
        PLAN["best"] = plan(ops)
    order = PLAN["best"][1]
    seq = {"v": 0, "a": 0, "p": 0, "g": 0}
    for i in order:
        o = ops[i]
        o["eng"] = PLAN["best"][2][i]
        if o["kind"] == "c":
            seq[o["eng"]] += 1
            o["sem"], o["val"], o["key"] = T.sem["ev_" + o["eng"]], seq[o["eng"]], o["eng"]
        else:
            o["key"] = i
    seen = {e: {} for e in Q}
    for i in order:
        o = ops[i]
        e = o["eng"]
        if e == "x":
            continue
        need = {}
        for d in o["deps"]:
            p = ops[d]
            if p["kind"] == "r" or d in o["soft"] or (e == "p" and p["eng"] == "p"):
                continue
            if p["val"] > need.get(p["key"], (0, None))[0]:
                need[p["key"]] = (p["val"], p["sem"])
        for k, (val, sem) in need.items():
            if seen[e].get(k, 0) < val:
                Q[e].wait_ge(sem, val)
                seen[e][k] = val
        r = o["fn"](e)
        if o["kind"] == "c":
            r.then_inc(o["sem"], 1)
    for i in order:
        o = ops[i]
        if o["kind"] in "dl" and not any(seen[e].get(i, 0) for e in Q):
            g.wait_ge(o["sem"], o["val"])
    for e in seq:
        g.wait_ge(T.sem["ev_" + e], seq[e])
    g.wait_ge(T.sem.sent, cnt["sent"])
    return ops
